import numpy as np, ml_dtypes
CORES = [6,15,38,47]
N = 4
BF = ml_dtypes.bfloat16
def gentries(a):
    return np.ascontiguousarray(a.reshape(8, 16, -1).transpose(0, 2, 1)).reshape(8, -1)
def gtable(e):
    e = np.asarray(e); return np.ascontiguousarray(e.reshape(8, -1, 16).transpose(0, 2, 1)).reshape(128, -1).astype(np.int32)
W, B, L, T, H, A = 4096, 12, 256, 4, 2, 704
def codes(rng, lo, hi):
    return np.floor(rng.random((N, 8, 16, W)) * (rng.integers(lo, hi + 1, (N, 8, 1, W)) + 1)).astype(np.int64)
def names(rng):
    hub = rng.integers(0, W, W // 16)
    def some(*shape):
        return np.where(rng.random(shape) < 0.5, hub[rng.integers(0, W // 16, shape)], rng.integers(0, W, shape))
    return some(N, 8, 16, W), some(N, 8, L)
def vals(rng, size):
    return np.clip(rng.standard_normal((N, 8, 16, W), dtype=np.float32) * np.exp2(size), -64, 64)
def plainvals(rng):
    return vals(rng, rng.integers(-2, 3, (N, 8, 16, 1)))
def pack(k, v, nm, s):
    two = nm[..., :W // 2] + W * nm[..., W // 2:]
    return {"kt": k.reshape(N, 128, W).astype(np.float32).astype(BF), "vt": v.reshape(N, 128, W).astype(np.float32).astype(BF),
            "bp": np.ascontiguousarray(two.reshape(N, 128, W // 2)).astype(np.int32), "st": np.stack([gtable(a) for a in s])}
def near():
    i, j = np.triu_indices(768); i = i + 256; j = j + 256; a = i * j
    where = np.full(2 ** 20 + 1, -1); where[a] = np.arange(len(a))
    b = (2 ** 36 + a // 2) // a; m = where[b]
    h = np.nonzero((m >= 0) & (np.abs(a * b - 2 ** 36) < 2 ** 13))[0]; m = m[h]
    z = np.concatenate([np.stack([i[h], j[h], i[m], j[m]], 1), np.stack([i[h], j[h], j[m], i[m]], 1)])
    y = z.astype(np.float32) * np.float32(2.0 ** -10); p = y[:, 0] * y[:, 1]; lim = np.float32(0.0625)
    return z[(((p * y[:, 2]) * y[:, 3]) < lim) != ((p * (y[:, 2] * y[:, 3])) < lim)]
def over(rng):
    i, j = np.triu_indices(768); i = i + 256; j = j + 256
    where = np.full(2 ** 20 + 1, -1); where[i * j] = np.arange(len(i))
    x = rng.integers(256, 1024, (3, 2 ** 19)); y = x.astype(np.float32) * np.float32(2.0 ** -10); R = (y[0] * y[1]) * y[2]
    h = np.nonzero((R > 0.07) & (R < 0.25))[0]; x = x[:, h]; R = R[h]
    c = (R.astype(np.float64) * 2.0 ** 27).astype(np.int64); m = where[(2 ** 43 + c // 2) // c]
    h = np.nonzero(m >= 0)[0]; m = m[h]; R = R[h]; z = np.stack([x[0, h], x[1, h], x[2, h], i[m], j[m]], 1)
    y = z.astype(np.float32) * np.float32(2.0 ** -10); u = y[:, 3]; v = y[:, 4]; lim = np.float32(0.0625); right = ((R * u) * v) < lim
    m24, m26 = [(((np.rint(R * np.float32(2.0 ** b)) * np.float32(2.0 ** -b)) * u) * v) < lim for b in (24, 26)]
    return z[((R * (u * v)) < lim) != right], z[(m24 != right) | (m26 != right)]
def setup_inputs(rng):
    nm, s = names(rng)
    return pack(codes(rng, 12, 15), plainvals(rng), nm, s)
def setup_inputs_spread(rng):
    nm, s = names(rng); weak = rng.random((N, 8, 1, W)) < 0.3
    k = np.where(weak, codes(rng, 4, 11), codes(rng, 14, 15)); s = np.where(rng.random(s.shape) < 0.5, s, (W * rng.random(s.shape) ** 4).astype(np.int64))
    return pack(k, vals(rng, rng.integers(-3, 4, (N, 8, 1, W))), nm, s)
def setup_inputs_ends(rng):
    k = 15 * (rng.random((N, 8, 16, W)) < rng.choice(np.array([0.0, 0.25, 0.25, 0.5, 1.0]), (N, 8, 1, W))).astype(np.int64)
    four = 15 * (rng.permutation(16) < 4).astype(np.int64); kind = np.argsort(rng.random((N, 8)), axis=1) % 3; kind[N - 1, 7] = 0
    k[..., 0] = np.where(kind[..., None] == 1, 15, four); k[..., W - 1] = np.where(kind[..., None] == 0, 15, four)
    e = (W - 1) * rng.integers(0, 2, (N, 8, 16, W // 2)); m = rng.random(e.shape) < 0.66
    nm = np.concatenate([np.where(m, e, rng.integers(0, W, e.shape)), np.where(m, e, rng.integers(0, W, e.shape))], axis=3)
    s = np.where(rng.random((N, 8, L)) < 0.72, (W - 1) * rng.integers(0, 2, (N, 8, L)), rng.integers(0, W, (N, 8, L))); s[..., L - 1] = W - 1
    v = plainvals(rng); v = np.where(rng.random(v.shape) < 0.3, np.where(rng.random(v.shape) < 0.5, 64.0, -64.0), v)
    return pack(k, v, nm, s)
def setup_inputs_crowd(rng):
    nm, s = names(rng); k = rng.integers(2, 7, (N, 8, 16, W)); k[1::2] = rng.integers(11, 16, (N // 2, 8, 16, W))
    o = rng.permutation(W); n = (H + 1) * L; ch = o[:H * L].reshape(H, L); u = o[H * L:n]; nul = o[n:n + 16]; big = o[n + 16:n + 80]; pk = o[n + 80:n + 80 + H]; top = o[n + 96:n + 112]
    def lead(r, g, keys, to):
        k[r, g][:, nul] = 0; nm[r, g][:, keys] = nul[rng.integers(0, 16, (16, len(keys)))]; nm[r, g, 15, keys] = to
    for r in range(0, N, 2):
        kind = rng.permutation(8); h5 = (int(np.nonzero(kind == 5)[0][0]) - 1) % 8
        nm[r, h5][rng.random((16, W)) < 0.25] = pk[0]
        for g in range(8):
            p = int(rng.choice(np.array([0, W - 1, rng.integers(0, W), rng.integers(0, W)])))
            if kind[g] in (0, 1, 7): nm[r, g, 15] = p
            if kind[g] == 2: nm[r, g, 15] = rng.choice(rng.integers(0, W, 3), W)
            if kind[g] == 1:
                x = (p + 1 + rng.permutation(W - 1)[:H + 1]) % W; nm[r, g, 15, x[:H]] = x[1:]
                a = s[r, g].copy(); a[np.isin(a, x)] = p; a[int(rng.choice(np.array([0, L - 1, rng.integers(0, L)])))] = x[0]; s[r, g] = a
            if kind[g] in (4, 6):
                x = k[r, g]; x[:, ch[0]] = rng.integers(12, 16, (16, L)); x[:, big] = rng.integers(11, 16, (16, 64))
                for h in range(1, H):
                    x[:, ch[h]] = 0; lead(r, g, ch[h - 1], ch[h])
                nm[r, g][:, ch[H - 1]] = big[rng.integers(0, 64, (16, L))]; a = rng.permutation(ch[0])
                if kind[g] == 6: a[int(rng.choice(np.array([0, L - 1, rng.integers(0, L)])))] = nul[0]
                s[r, g] = a; b, c = (r - 1) % N, (g - 1) % 8
                k[b, c][:, ch[0]] = 0; lead(b, c, u, rng.permutation(ch[0])); lead(b, c, ch[0], ch[0]); s[b, c] = rng.permutation(u)
            if kind[g] == 5:
                k[r, g][:, u] = rng.integers(4, 8, (16, L)); k[r, g][:, pk[0]] = 0
                lead(r, g, u, pk[0]); lead(r, g, pk[:1], pk[:1]); s[r, g] = rng.permutation(u); b, c = r + 1, (g + 1) % 8
                k[b, c][:, top] = 15
                for h in range(1, H):
                    k[b, c][:, pk[h]] = 0; lead(b, c, pk[h - 1:h], pk[h:h + 1])
                nm[b, c][:, pk[H - 1]] = rng.permutation(top); s[b, c] = np.where(s[b, c] == pk[0], top[0], s[b, c])
    return pack(k, plainvals(rng), nm, s)
def setup_inputs_corners(rng):
    nm, s = names(rng); k = codes(rng, 12, 15); own = np.arange(W)
    for r in range(N):
        kind = rng.permutation(8) % 4
        for g in range(8):
            if kind[g] == 0:
                nm[r, g, :15] = own; nm[r, g, 15] = np.where(rng.random(W) < 0.5, own, nm[r, g, 15])
            if kind[g] == 1:
                e = rng.integers(0, 3, (15, W)); nm[r, g, :15] = np.where(e == 0, 0, np.where(e == 1, W - 1, own)); nm[r, g, 15] = (own - 1) % W
            if kind[g] == 2:
                hot = rng.permutation(W) < W // 2; a = np.nonzero(hot)[0]; b = np.nonzero(~hot)[0]
                k[r, g] = np.where(hot, rng.integers(12, 16, (16, W)), 0); page = b[rng.integers(0, len(b), (16, W))]
                one = own[rng.random(W) < 0.7]; page[rng.integers(0, 16, len(one)), one] = a[rng.integers(0, len(a), len(one))]
                nm[r, g] = page; s[r, g] = a[rng.integers(0, len(a), L)]
            if kind[g] == 3:
                k[r, g] = rng.integers(0, 3, (16, W)); s[r, g, 0] = 0; s[r, g, L - 1] = W - 1
    return pack(k, plainvals(rng), nm, s)
def setup_inputs_order(rng):
    nm, s = names(rng); k = codes(rng, 12, 15); z = near(); zp, zm = over(rng); lane = np.arange(L); row = np.arange(16)[:, None]
    o = rng.permutation(W); a, b, d, nul, fac = o[:L], o[L:2 * L], o[2 * L:3 * L], o[3 * L:3 * L + 16], o[3 * L + 16:3 * L + 784]
    w = rng.permutation(16); e = w[:8, None]; sc = A + 1024 - np.arange(256, 1024)
    for r in range(N):
        kind = rng.permutation(8) % 2
        for g in range(8):
            x = k[r, g]; v = nm[r, g]
            x[w[:9, None], nul] = 0
            x[:, fac] = rng.integers(0, 16, (16, 768))
            x[e, fac] = (sc[None, :] + 15 * np.arange(8)[:, None]) // 15 // 8; x[w[8], fac] = sc % 15
            if kind[g]: continue
            x[:, a] = 0; x[e, a] = 15; x[w[8], a] = 1
            x[w[:9, None], o[L:3 * L]] = 0
            lay = rng.integers(0, 4 if r % 2 else 6, L); full = lane[lay < 3]; half = lane[lay == 3]; far = lane[lay > 3]
            y = fac[z[rng.integers(0, len(z), L)] - 256]
            y5 = fac[np.where((lay == 4)[:, None], zp[rng.integers(0, len(zp), L)], zm[rng.integers(0, len(zm), L)]) - 256]
            page = np.where((lay < 3) & (row >= 4 * lay + 4), v[:, a], nul[rng.integers(0, 16, (16, L))])
            for n in range(4): page[4 * lay[full] + n, full] = y[full, n]
            page[:2, half] = y[half, :2].T; page[15, half] = b[half]
            page[:3, far] = y5[far, :3].T; page[15, far] = d[far]
            v[:, a] = page; v[:2, b] = y[:, 2:].T; s[r, g] = a
            v[:, d[far]] = nul[rng.integers(0, 16, (16, len(far)))]; v[15, d[far]] = d[far]
            nm[(r + 1) % N, (g + 1) % 8][:2, d[far]] = y5[far, 3:].T
    return pack(k, plainvals(rng), nm, s)
def check_ranges(d):
    bad = []
    a = np.asarray(d["kt"]).astype(np.float64)
    if not np.all((a >= 0) & (a <= 15) & (a == np.floor(a))): bad.append("range of kt")
    a = np.asarray(d["vt"]).astype(np.float64)
    if not np.all((a >= -64) & (a <= 64)): bad.append("range of vt")
    for n, hi in (("bp", W * W - 1), ("st", W - 1)):
        if np.min(d[n]) < 0 or np.max(d[n]) > hi: bad.append("range of " + n)
    return bad
def take(tab, c):
    return np.take_along_axis(tab, c[:, :, None, :], 3)
def reference(kt, vt, bp, st):
    k = kt.astype(np.float32).astype(np.int64).reshape(N, 8, 16, W)
    sg = np.reciprocal(1.0 + np.exp(-vt.astype(np.float64))).reshape(N, 8, 16, W)
    u = bp.astype(np.int64).reshape(N, 8, 16, W // 2); pg = np.concatenate([u & (W - 1), u >> B], axis=3)
    c = np.stack([gentries(a) for a in st]).astype(np.int64)
    q = take(k, c); R = np.ones((N, 8, L), np.float32); acc = np.zeros((N, 8, 16, L)); one = np.float32(1); out = []
    for t in range(T):
        if t:
            c, q, R, acc = [np.roll(np.roll(a, 1, axis=0), t, axis=1) for a in (c, q, R, acc)]
        came = c; whole = np.ones((N, 8, L), bool)
        for h in range(H):
            nm = take(pg, c); flat = nm.reshape(N, 8, 16 * L)
            s = np.add.reduce(q[:, :, :, None, :] * take(k, flat).reshape(N, 8, 16, 16, L), axis=2)
            beta = np.minimum(np.maximum(s - A, 0), 960).astype(np.float32) * np.float32(2.0 ** -10)
            v = take(sg, flat).reshape(N, 8, 16, 16, L)
            broke = np.zeros((N, 8, L), bool); nxt = nm[:, :, 15]
            for i in range(16):
                on = ~broke; bi = beta[:, :, i]
                acc = acc + np.where(on, R.astype(np.float64) * bi.astype(np.float64), 0.0)[:, :, None, :] * v[:, :, :, i]
                R = np.where(on, R * (one - bi), R)
                hit = on & (R < np.float32(0.0625))
                nxt = np.where(hit, nm[:, :, i], nxt); broke = broke | hit
            c = nxt; q = np.where(broke[:, :, None, :], take(k, c), q); R = np.where(broke, one, R)
            cut = whole & broke; whole = whole & ~broke
        out.append((acc + R.astype(np.float64)[:, :, None, :] * take(sg, c)).reshape(N, 128, L))
        if t < T - 1:
            for j in range(L - 1, -1, -1):
                a, g = np.nonzero(cut[:, :, j])
                pg[a, g, 15, came[a, g, j]] = c[a, g, j]
    return {"ya": np.concatenate(out, axis=2).astype(np.float32)}

def check_inputs(d):
    bad = list(check_ranges(d))
    if not bad:
        for name, y in reference(**d).items():
            for q in range(N):
                v = np.abs(np.asarray(y[q], np.float64))
                if v.max() > 7 * np.sqrt(np.mean(v * v)): bad.append('%s of rank %d is uneven' % (name, q))
    return bad

@@ -1,0 +1,594 @@
+from concourse.mybir import AluOpType, ActivationFunctionType
+
+W, L, NV = 4096, 256, 4
+BIG = 8192.0
+KO = 0
+NB = 3
+OPT = {"NF": [6, 4, 4, 4, 4, 4, 4, 4], "VS": 2, "FS": "01111110", "cy": 0.83, "ga": 1.5, "sc": 3.8, "pe": 0.42, "sem": 60, "dl": 2000, "db": 300.0,
+       "rl": 2500, "rb": 60.0, "rounds": 700, "seed": 1, "amp": 100.0, "drift": 1.004, "moves": 4, "far": 3000.0,
+       "SUM": "dddddddv", "NG": 4, "pace": []}
+SCALES = [{}, {"ga": 0.72, "sc": 0.7}, {"ga": 1.35, "sc": 1.3}, {"pe": 1.4, "sem": 2.0}, {"dma": 1.6, "rem": 1.5}, {"dma": 0.7, "rem": 0.7, "sem": 0.5}]
+
+SCRATCH = {
+    "bpk": ("sbuf", [128, W // 2], "int32"), "pg": ("sbuf", [128, W + 16], "int32"),
+    "kq": ("sbuf", [128, W + 2 * L], "bfloat16"), "vs": ("sbuf", [128, W], "bfloat16"),
+    "sti": ("sbuf", [128, 16], "int32"),
+    "pr": ("sbuf", [128, W], "bfloat16"),
+    "vg0": ("sbuf", [128, W + L], "float32"), "vg1": ("sbuf", [128, W + L], "float32"), "vg2": ("sbuf", [128, W + L], "float32"),
+    "vg3": ("sbuf", [128, W + L], "float32"), "lx1": ("sbuf", [128, 18], "uint16"),
+    "cl": ("sbuf", [128, 18], "uint16"), "cl1": ("sbuf", [128, 16], "uint16"), "ql": ("sbuf", [128, 16], "uint16"),
+    "nm": ("sbuf", [128, 272], "float32"), "tt": ("sbuf", [128, 544], "float32"),
+    "ln0": ("sbuf", [128, L], "uint16"), "ln1": ("sbuf", [128, L], "uint16"),
+    "aw": ("sbuf", [128, 272], "float32"), "ff": ("sbuf", [128, 272], "float32"), "be": ("sbuf", [128, 272], "float32"),
+    "d1": ("sbuf", [128, 272], "float32"), "xx": ("sbuf", [128, 272], "float32"), "dn": ("sbuf", [128, 272], "float32"),
+    "cs": ("sbuf", [128, 272], "float32"), "wb0": ("sbuf", [128, 272], "float32"), "wb1": ("sbuf", [128, 272], "float32"),
+    "wh0": ("sbuf", [128, 272], "bfloat16"), "wl0": ("sbuf", [128, 272], "bfloat16"),
+    "wh1": ("sbuf", [128, 272], "bfloat16"), "wl1": ("sbuf", [128, 272], "bfloat16"),
+    "tiny": ("sbuf", [128, 192], "float32"), "came": ("sbuf", [128, 16], "float32"),
+    "cex": ("sbuf", [128, L], "float32"), "nm0": ("sbuf", [128, L], "float32"), "eq": ("sbuf", [128, L], "float32"),
+    "cnt": ("sbuf", [128, L], "float32"), "val": ("sbuf", [128, L], "int32"), "so": ("sbuf", [128, 32], "uint16"),
+    "xh": ("sbuf", [128, 32], "bfloat16"), "xl": ("sbuf", [128, 32], "bfloat16"),
+    "yy": ("sbuf", [128, NV * L], "float32"),
+    "pi": ("sbuf", [128, 8], "int32"), "pf": ("sbuf", [128, 16], "float32"), "ti": ("sbuf", [128, 80], "int32"),
+    "io": ("sbuf", [128, L], "float32"), "jj": ("sbuf", [128, L], "float32"), "rm": ("sbuf", [128, L], "float32"),
+    "tw": ("sbuf", [128, 240], "float32"), "pq": ("sbuf", [128, 32], "float32"),
+    "li": ("sbuf", [128, 16], "uint16"), "le": ("sbuf", [128, 16], "uint16"),
+    "lw": ("sbuf", [128, 18], "uint16"), "lf": ("sbuf", [128, 18], "uint16"), "lx": ("sbuf", [128, 18], "uint16"),
+    "wd": ("sbuf", [128, 144], "bfloat16"), "idf": ("sbuf", [128, 256], "float32"), "idb": ("sbuf", [128, 256], "bfloat16"),
+    "sel": ("sbuf", [128, 2048], "bfloat16"), "cc": ("sbuf", [128, 512], "bfloat16"),
+    "ps_s": ("psum", [128, 512], "float32"), "ps_q": ("psum", [128, 512], "float32"), "ps_r": ("psum", [128, 512], "float32"),
+    "ps_a": ("psum", [128, 512], "float32"), "ps_m": ("psum", [128, 512], "float32"),
+    "ps_w0": ("psum", [128, 512], "float32"), "ps_w1": ("psum", [128, 512], "float32"), "ps_w2": ("psum", [128, 512], "float32"),
+}
+for _t in range(NV - 1):
+    SCRATCH["sb%d" % _t] = ("sbuf", [128, 48], "float32")
+    SCRATCH["qs%d" % _t] = ("sbuf", [128, L], "bfloat16")
+    SCRATCH["as%d" % _t] = ("sbuf", [128, L], "float32")
+    SCRATCH["lc%d" % _t] = ("sbuf", [128, 32], "float32")
+    SCRATCH["lq%d" % _t] = ("sbuf", [128, L], "bfloat16")
+    SCRATCH["la%d" % _t] = ("sbuf", [128, L], "float32")
+SEMAPHORES = ["eV", "eS", "eP", "eG"] + ["d%d" % i for i in range(40)] + ["a%d" % i for i in range(9)]
+
+A = AluOpType
+F = ActivationFunctionType
+ORDER = {}
+
+
+def v(name, a, b, s=1):
+    return (name, a, b, s)
+
+
+def ind(win, off):
+    return ("*", win, off)
+
+
+def cols(x):
+    return 16 * cols(x[2]) if x[0] == "*" else len(range(x[1], x[2], x[3]))
+
+
+def bits(x):
+    if x[3] == 1:
+        return ((1 << (x[2] - x[1])) - 1) << x[1]
+    m = 0
+    for c in range(x[1], x[2], x[3]):
+        m |= 1 << c
+    return m
+
+
+def meets(ops):
+    hist, before, out = {}, {}, []
+    for i, o in enumerate(ops):
+        deps = set()
+        acc = [(x[0], bits(x), False) for x in o["r"]] + [(x[0], bits(x), True) for x in o["w"]]
+        for b, m, wr in acc:
+            h = hist.setdefault(b, [])
+            if b.startswith("ps_"):
+                if h and (ops[h[0][0]]["st"] != o["st"] or o["st"] == "P"):
+                    before[b] = [e[0] for e in h]
+                    h[:] = []
+                deps.update(before.get(b, []))
+            for j, mj, wj in h:
+                if (m & mj) and (wr or wj):
+                    deps.add(j)
+        for b, m, wr in acc:
+            h = hist[b]
+            if wr:
+                h[:] = [e for e in h if (e[1] & ~m) or e[0] == i]
+            h.append((i, m, wr))
+        out.append(deps)
+    return out
+
+
+def schedule(ops, pace):
+    deps = meets(ops)
+    n = len(ops)
+    for i, o in enumerate(ops):
+        if o["e"] is None:
+            deps[i].add(o["from"])
+    for a, b in pace:
+        deps[b].add(a)
+    succ = [[] for _ in ops]
+    for i in range(n):
+        for j in deps[i]:
+            succ[j].append(i)
+    gap = lambda j, i: 0 if ops[i]["e"] is None or ops[i]["st"] == ops[j]["st"] == "P" else OPT["sem"]
+    c, lat = [o["c"] for o in ops], [o["lat"] for o in ops]
+
+    def place(order, back):
+        at, busy = [0.0] * n, {e: [] for e in "VSPGY"}
+        for i in order:
+            if back:
+                t = max([at[k] + c[k] + lat[i] - c[i] + gap(i, k) for k in succ[i]] + [lat[i] - c[i]])
+            else:
+                t = max([at[j] + lat[j] + gap(j, i) for j in deps[i]] + [0.0])
+            if ops[i]["e"] is not None:
+                b = busy[ops[i]["e"]]
+                lo, hi = 0, len(b)
+                while lo < hi:
+                    mid = (lo + hi) // 2
+                    if b[mid][1] <= t:
+                        lo = mid + 1
+                    else:
+                        hi = mid
+                while lo < len(b) and b[lo][0] < t + c[i]:
+                    t = max(t, b[lo][1])
+                    lo += 1
+                b.insert(lo, (t, t + c[i]))
+            at[i] = t
+        return at
+
+    hard = [[(j, gap(j, i) > 0) for j in deps[i]] for i in range(n)]
+
+    def replay(order, scale):
+        end, free, sem = [0.0] * n, {e: 0.0 for e in "VSPGY"}, OPT["sem"] * scale.get("sem", 1.0)
+        for i in order:
+            o = ops[i]
+            t = max([end[j] + (sem if w else 0.0) for j, w in hard[i]] + [free.get(o["e"], 0.0)])
+            k = scale.get(o["k"], 1.0)
+            end[i] = t + lat[i] * k
+            if o["e"] is not None:
+                free[o["e"]] = t + c[i] * k
+        return max(end)
+
+    state, groups = [OPT["seed"]], sorted(set(o["grp"] for o in ops))
+
+    def draw():
+        state[0] = (state[0] * 1103515245 + 12345) % 2 ** 31
+        return state[0] / 2 ** 31
+
+    def shaken(key, amp, back):
+        out, moved = list(key), {}
+        for _ in range(OPT["moves"]):
+            moved[groups[int(draw() * len(groups))]] = OPT["far"] * (2 * draw() - 1)
+        for i in (range(n - 1, -1, -1) if back else range(n)):
+            out[i] = max([key[i] + amp * draw() + moved.get(ops[i]["grp"], 0.0)] + [out[j] for j in (succ[i] if back else deps[i])])
+        return out
+
+    at = place(range(n), False)
+    best = None
+    for r in range(OPT["rounds"]):
+        key = shaken([-at[i] - c[i] for i in range(n)], OPT["amp"], True)
+        u = place(sorted(range(n), key=lambda i: (key[i], -i)), True)
+        key = shaken([-u[i] - c[i] for i in range(n)], OPT["amp"], False)
+        new = place(sorted(range(n), key=lambda i: (key[i], i)), False)
+        order = sorted(range(n), key=lambda i: (-1.0 if ops[i].get("load") else new[i], i))
+        end = sum(replay(order, s) for s in SCALES) / len(SCALES)
+        if best is None or end < best[0]:
+            best = (end, order, new)
+        at = new if end < best[0] * OPT["drift"] else best[2]
+    ORDER["end"] = best[0]
+    return best[1]
+
+
+def emit(g, T, ops):
+    queue = {"V": g.vector, "S": g.scalar, "P": g.tensor, "G": g, "Y": g.sync}
+    known, done, waits, needed = {e: {} for e in queue}, [], [], set()
+    for i, deps in enumerate(meets(ops)):
+        o, ws = ops[i], []
+        if o["e"] is None:
+            done.append({o["st"]: i})
+            waits.append(ws)
+            continue
+        k = known[o["e"]]
+        for j in sorted(deps, reverse=True):
+            if k.get(ops[j]["st"], -1) >= j or o["st"] == ops[j]["st"] == "P":
+                continue
+            ws.append(j)
+            needed.add(j)
+            for s, n in done[j].items():
+                if k.get(s, -1) < n:
+                    k[s] = n
+        d = dict(k)
+        d[o["st"]] = i
+        done.append(d)
+        waits.append(ws)
+    count, token, waited = {}, {}, {}
+    for i, o in enumerate(ops):
+        if o["e"] is not None:
+            for j in waits[i]:
+                queue[o["e"]].wait_ge(T.sem[token[j][0]], token[j][1])
+                waited[token[j][0]] = max(waited.get(token[j][0], 0), token[j][1])
+        if o["sem"] is not None:
+            token[i] = (o["sem"], o["n"])
+            count[o["sem"]] = o["n"]
+            if o["e"] is not None:
+                o["f"](queue[o["e"]])
+        else:
+            ins = o["f"](queue[o["e"]])
+            if i in needed:
+                s = "e" + o["e"]
+                count[s] = count.get(s, 0) + 1
+                token[i] = (s, count[s])
+                ins.then_inc(T.sem[s], 1)
+    for s, n in count.items():
+        if waited.get(s, 0) < n:
+            g.wait_ge(T.sem[s], n)
+
+
+def rank_program(g, core, T, topo):
+    rank = T.rank_of(core)
+    if rank is None:
+        return
+    nxt = T.cores[(rank + 1) % len(T.cores)]
+    rid, pid, _se = topo.addr(nxt)
+    mask = topo.mask(core, nxt)
+    n_out = len(topo.engines(core, nxt))
+    n_in = len(topo.engines(T.cores[(rank - 1) % len(T.cores)], core))
+    ops, nd, loaded, hop = [], [0], [0.0], [9]
+    cy = OPT["cy"]
+
+    def ap(x):
+        if x[0] == "*":
+            return ap(x[1]).indirect(ap(x[2]))
+        return T[x[0]][:, x[1]:x[2]] if x[3] == 1 else T[x[0]][:, x[1]:x[2]:x[3]]
+
+    def rec(e, f, outs, ins, c, sem=None, n=0, lat=None, dma=0):
+        r, w = [], []
+        for x in ins:
+            if isinstance(x, tuple):
+                r.extend([x[1], x[2]] if x[0] == "*" else [x])
+        for x in outs:
+            if x[0] == "*":
+                w.append(x[1])
+                r.append(x[2])
+            else:
+                w.append(x)
+        ops.append({"e": e, "f": f, "r": r, "w": w, "sem": sem, "n": n, "st": sem or e, "c": c, "lat": c if lat is None else lat, "from": len(ops) - 1,
+                    "grp": "%s%d%s" % (e, hop[0], (w or r)[0][0][:4]),
+                    "k": "pe" if e == "P" else ("dma" if n == 16 else "rem") if sem else "sc" if outs[0][0] == "*" else "ga" if ins and ins[0][0] == "*" else ""})
+
+    def cost(o, a, k=1.0):
+        if o[0] == "*":
+            return 50 + cols(o) * OPT["sc"] * cy
+        if a[0] == "*":
+            return 55 + cols(a) * OPT["ga"] * cy
+        return max(64, cols(a) * k) * cy
+
+    def num(x):
+        return ap(x) if isinstance(x, tuple) else x
+
+    def cp(o, i):
+        rec("V", lambda q: q.tensor_copy(ap(o), ap(i)), [o], [i], cost(o, i))
+
+    def tt(o, a, b, op):
+        rec("V", lambda q: q.tensor_tensor(ap(o), ap(a), ap(b), op), [o], [a, b], cost(o, a, 1.0 if b[0].startswith("ps_") else 2.0))
+
+    def ts(o, a, s1, op0, s2=None, op1=None):
+        if op1 is None:
+            rec("V", lambda q: q.tensor_scalar(ap(o), ap(a), num(s1), None, op0), [o], [a, s1], cost(o, a))
+        else:
+            rec("V", lambda q: q.tensor_scalar(ap(o), ap(a), num(s1), num(s2), op0, op1), [o], [a, s1, s2], cost(o, a))
+
+    def scan(o, a, b, op0, op1):
+        rec("V", lambda q: q.tensor_tensor_scan(ap(o), ap(a), ap(b), 0.0, op0, op1), [o], [a, b], cost(o, a))
+
+    def turn(o, i):
+        rec("V", lambda q: q.transpose(ap(o), ap(i)), [o], [i], cost(o, i))
+
+    def fill_const(o, c):
+        rec("V", lambda q: q.memset(ap(o), c), [o], [], cost(o, o))
+
+    def act(o, i, fn, bias=None, scale=None):
+        if bias is None:
+            rec("S", lambda q: q.activation(ap(o), ap(i), fn), [o], [i], cost(o, i))
+        else:
+            rec("S", lambda q: q.activation(ap(o), ap(i), fn, bias=num(bias), scale=1.0 if scale is None else scale), [o], [i, bias], cost(o, i))
+
+    def mm(o, lt, r, start, stop):
+        rec("P", lambda q: q.matmul(ap(o), ap(lt), ap(r), start, stop), [o], [lt, r], max(64, cols(r)) * OPT["pe"] * (4 if lt[0] == "idf" else 1))
+
+    def dsem():
+        nd[0] += 1
+        return "d%d" % (nd[0] - 1)
+
+    def load(e, o, src, nbytes):
+        s = dsem()
+        loaded[0] += nbytes / OPT["db"]
+        rec(e, lambda q: q.dma_start(ap(o), src).then_inc(T.sem[s], 16), [o], [], 100, s, 16, OPT["dl"] + loaded[0])
+        ops[-1]["load"] = True
+
+    def store(dst, i):
+        s = dsem()
+        rec("Y", lambda q: q.dma_start(dst, ap(i)).then_inc(T.sem[s], 16), [], [i], 100, s, 16, OPT["dl"] + 500)
+
+    def move(land, i, k, nbytes):
+        s = dsem()
+        rec("G", lambda q: q.remote_dma(ap(land), ap(i), T.sem["a%d" % k], T.sem[s], pid, rid, mask), [], [i], 500, s, n_out, OPT["rl"] + nbytes / OPT["rb"])
+        rec(None, None, [land], [], 0, "a%d" % k, n_in)
+
+    load("Y", v("sti", 0, 16), T.st[:], 8192)
+    NP = 4
+    pc = W // 2 // NP
+    for k in range(NP):
+        load("Y", v("bpk", k * pc, (k + 1) * pc), T.bp[:, k * pc:(k + 1) * pc], 512 * pc)
+    load("Y", v("kq", KO, KO + W), T.kt[:], 256 * W)
+    load("Y", v("vs", 0, W), T.vt[:], 256 * W)
+
+    def iota(o, pat, base, cm, flag):
+        if flag:
+            rec("G", lambda q: q.iota(ap(o), pat, base, cm, allow_small_or_imprecise_dtypes=True), [o], [], 130 + 2 * cy * cols(o))
+        else:
+            rec("G", lambda q: q.iota(ap(o), pat, base, cm), [o], [], 130 + 2 * cy * cols(o))
+    iota(v("pi", 0, 1), [[0, 1]], 0, 1, False)
+    iota(v("io", 0, L), [[1, L]], 0, 0, True)
+    iota(v("jj", 0, L), [[0, 16], [1, 16]], 0, 0, True)
+    iota(v("sel", 0, 2048), [[0, 2048]], 1, 0, True)
+    rec("G", lambda q: q.affine_select(T.sel[:], T.sel[:], [[-1, 16], [-16, 8], [0, 16]], A.is_equal, 0.0, 0, 1), [v("sel", 0, 2048)], [v("sel", 0, 2048)], 170 + 4096 * cy)
+    fill_const(v("d1", 0, 272), 0.0)
+    fill_const(v("wb0", 256, 272), 0.0)
+    fill_const(v("aw", 0, 16), -1.0 / 16)
+    fill_const(v("pg", W, W + 16), 0)
+    fill_const(v("d1", 0, 272, 17), 1.0)
+    ts(v("pi", 1, 2), v("pi", 0, 1), 15, A.bitwise_and)
+    ts(v("pi", 2, 3), v("pi", 0, 1), 4, A.logical_shift_right)
+    ts(v("pi", 3, 4), v("pi", 0, 1), 112, A.bitwise_and)
+    cp(v("pf", 0, 4), v("pi", 0, 4))
+    cP, cR, cX, cG = [v("pf", k, k + 1) for k in range(4)]
+    c17, cD, cD8, cM15, cN15, cG15 = [v("pf", k, k + 1) for k in range(4, 10)]
+    ts(c17, cR, 17.0, A.mult)
+    ts(cD, cR, float(W), A.add)
+    ts(cD8, cR, float(W), A.add, 1 / BIG, A.mult)
+    ts(cM15, cR, 15.0, A.is_equal, -BIG, A.mult)
+    ts(cN15, cR, 15.0, A.not_equal, -BIG, A.mult)
+    ts(cG15, cG, 15.0, A.add)
+    tE, tS, tU, tV = [v("tw", 20 * k, 20 * k + 17) for k in range(4)]
+    wPL, wA, wB, wC, wO = [v("tw", 20 * k, 20 * k + 18) for k in range(4, 9)]
+    ts(tE, v("io", 0, 17), 16.0, A.mult, cR, A.add)
+    ts(tU, tE, -8.0, A.add, 1 / 17.0, A.mult)
+    cp(v("ti", 0, 17), tU)
+    cp(v("ti", 17, 18), v("pi", 1, 2))
+    cp(wPL, v("ti", 0, 18))
+    tPL = v("tw", 80, 97)
+    ts(tV, tPL, -17.0, A.mult)
+    tt(tS, tE, tV, A.add)
+    ts(v("ti", 20, 38), wPL, cX, A.add)
+    ts(v("ti", 20, 38), v("ti", 20, 38), 1, A.bitwise_and)
+    cp(wO, v("ti", 20, 38))
+    ts(v("ti", 40, 58), wPL, 16.0, A.mult, 240.0, A.add)
+    ts(v("ti", 40, 58), v("ti", 40, 58), 255, A.bitwise_and)
+    ts(wA, wPL, 16.0, A.mult)
+    ts(wB, v("ti", 40, 58), 256.0, A.add)
+    tt(wB, wB, wA, A.subtract)
+    tt(wB, wB, wO, A.mult)
+    tt(wC, wB, wA, A.add)
+    ts(v("li", 0, 16), v("io", 0, 16), v("tw", 157, 158), A.add)
+    tt(tV, tS, v("tw", 140, 157), A.add)
+    tQ, tK = v("tw", 180, 197), v("tw", 200, 217)
+    ts(tQ, tS, 16.0, A.is_equal)
+    ts(tK, tPL, 512.0, A.add)
+    tt(tK, tK, tV, A.subtract)
+    tt(tK, tK, tQ, A.mult)
+    tt(tV, tV, tK, A.add)
+    cp(v("lx", 0, 17), tV)
+    ts(tQ, tQ, 16.0, A.mult)
+    tt(tV, tV, tQ, A.add)
+    cp(v("lx1", 0, 17), tV)
+    ts(tU, tS, 16.0, A.mult)
+    tt(tU, tU, tPL, A.add)
+    cp(v("lf", 0, 17), tU)
+    cp(v("le", 0, 16), v("io", 0, 16))
+    ts(v("lw", 0, 17), v("io", 0, 17), c17, A.add)
+    ts(v("tt", 512, 528), v("tw", 0, 16), float(W), A.add)
+    ts(v("tt", 528, 544), v("tw", 0, 16), float(W + L), A.add)
+    ts(v("wd", 0, 144), v("io", 0, 144), cG15, A.is_equal, -1 / 1024.0, A.mult)
+    ts(v("idf", 0, 128), v("io", 0, 128), cP, A.is_equal)
+    ts(v("idb", 0, 128), v("io", 0, 128), cP, A.is_equal)
+    act(v("idf", 128, 256), v("idf", 0, 128), F.Copy)
+    act(v("idb", 128, 256), v("idb", 0, 128), F.Copy)
+    ts(v("cc", 0, 256), v("jj", 0, 256), cR, A.is_ge, BIG, A.mult)
+    act(v("cc", 256, 512), v("jj", 0, 256), F.Identity, cN15, 0.0)
+    act(v("rm", 0, 256), v("jj", 0, 256), F.Sign)
+    cp(v("cl1", 0, 16), v("sti", 0, 16))
+    for k in range(NP):
+        ts(v("pg", k * pc, (k + 1) * pc), v("bpk", k * pc, (k + 1) * pc), W - 1, A.bitwise_and)
+        ts(v("pg", W // 2 + k * pc, W // 2 + (k + 1) * pc), v("bpk", k * pc, (k + 1) * pc), 12, A.logical_shift_right)
+
+    KT, PG = v("kq", KO, KO + W), v("pg", 0, W + 16)
+    qA, qB, PQ, PA = v("kq", W, W + L), v("kq", W + L, W + 2 * L), v("ps_q", 0, L), v("ps_a", 0, L)
+    IDF, IDB = v("idf", 0, 128), v("idb", 0, 128)
+    tB, tT, tM, tC1, tC2, tP1, tP2, tA, tZ, tR, tY = [v("tiny", 16 * k, 16 * k + 16) for k in range(11)]
+    bank, NG, tag = [0], OPT["NG"], {}
+
+    def products(h):
+        vg, wh, wl = "vg%d" % (h % NG), "wh%d" % (h % 2), "wl%d" % (h % 2)
+        for j0 in range(8 + h % 2):
+            bk = "ps_w%d" % (bank[0] % NB)
+            bank[0] += 1
+            for u, jj in enumerate((j0, j0 + 8) if j0 < 8 else range(16)):
+                s = v("sel", 128 * jj, 128 * jj + 128)
+                b, a0, a1 = (v(bk, u, 512, 2), 0, 256) if j0 < 8 else (v(bk, u, 256, 16), 256, 272)
+                mm(b, s, v(wh, a0, a1), True, False)
+                mm(b, s, v(wl, a0, a1), False, True)
+            x, b = (v(vg, j0, W, 8), v(bk, 0, 512)) if j0 < 8 else (v(vg, W, W + L), v(bk, 0, L))
+            tt(x, x, b, A.mult)
+            tag["p%d" % j0, h] = len(ops) - 1
+        m = 16
+        if OPT["SUM"][h] == "d":
+            s, m = dsem(), 8
+            o, i = v(vg, 0, 2048), v(vg, 2048, 4096)
+            rec("G", lambda q: q.dma_start(ap(o), ap(i), accum_op=A.add).then_inc(T.sem[s], 16), [o], [o, i], 1000, s, 16, OPT["dl"] + 2 ** 21 / OPT["db"])
+        t = h // 2
+        for k in range(m):
+            mm(PA, IDF, v(vg, 256 * k, 256 * k + 256), h % 2 == 0 and k == 0, h == 1 and k == m - 1)
+            tag["s%d" % k, h] = len(ops) - 1
+        if t and (h % 2 or t == NV - 1):
+            mm(PA, v("idf", 128 - 16 * t, 256 - 16 * t), v("la%d" % (t - 1), 0, L), False, t < NV - 1)
+
+    def last_products(h):
+        vg, wh, wl = "vg%d" % (h % NG), "wh%d" % (h % 2), "wl%d" % (h % 2)
+        for c in range(2):
+            n = 144 if c else 128
+            for j0 in range(0, 16, 2):
+                bk = "ps_w%d" % (bank[0] % NB)
+                bank[0] += 1
+                t1, t2, t3 = [], [], []
+                for u in range(2):
+                    jj, o = j0 + u, 256 * u
+                    s = v("sel", 128 * jj, 128 * jj + 128)
+                    mm(v(bk, o, o + n), s, v(wh, 128 * c, 128 * c + n), True, False)
+                    mm(v(bk, o, o + n), s, v(wl, 128 * c, 128 * c + n), False, True)
+                    x0 = 2048 * c
+                    xb, xa, xc = v(vg, x0 + jj + 1024, x0 + 16 * n, 16), v(vg, x0 + jj, x0 + 1024, 16), v(vg, x0 + jj + 1024, x0 + 2048, 16)
+                    t1.append((xb, xb, v(bk, o + 64, o + n), A.mult))
+                    t2.append((v(bk, o, o + 64), xa, v(bk, o, o + 64), A.mult))
+                    t3.append((xc, xc, v(bk, o, o + 64), A.add))
+                for x in t1 + t2 + t3:
+                    tt(*x)
+            for k in range(8 * c + 4, 8 * c + 8 - 2 * c):
+                mm(PA, IDF, v(vg, 256 * k, 256 * k + 256), False, k == 13)
+        x = v("ps_r", 0, L)
+        cp(x, v(vg, 256 * 14, 256 * 15))
+        tt(x, v(vg, 256 * 15, 256 * 16), x, A.add)
+        tt(v(vg, W, W + L), v(vg, W, W + L), x, A.add)
+
+    def report(t):
+        y = v("yy", L * t, L * t + L)
+        if t < NV - 1:
+            act(v("as%d" % t, 0, L), PA, F.Copy)
+            move(v("la%d" % t, 0, L), v("as%d" % t, 0, L), 3 * t + 2, 512 * L)
+        tt(y, v("vg%d" % ((2 * t + 1) % NG), W, W + L), PA, A.add)
+        store(T.ya[:, L * t:L * t + L], y)
+
+    def hold(lt, x):
+        mm(PQ, lt, x, True, True)
+        mm(v("ps_q", L, 2 * L), lt, x, True, True)
+
+    act(qA, ind(KT, v("cl1", 0, 16)), F.Copy)
+    hold(IDB, qA)
+    src, plus = v("sti", 0, 16), 0.0
+    for h in range(2 * NV):
+        t, first, last = h // 2, h % 2 == 0, h == 2 * NV - 1
+        cutv, hop[0] = t < NV - 1, h
+        ln, wb, wh, wl, vg = "ln%d" % (h % 2), "wb%d" % (h % 2), "wh%d" % (h % 2), "wl%d" % (h % 2), "vg%d" % (h % NG)
+        q = qA if first else qB
+        one = v(src[0], src[1], src[1] + 1)
+        if h == 0:
+            cp(v("cl", 0, 16), src)
+            cp(v("cl", 16, 17), one)
+        else:
+            ts(v("cl", 0, 16), src, plus, A.add)
+            ts(v("cl", 16, 17), one, plus, A.add)
+        if first and h:
+            cp(v("d1", 0, 272, 17), v("ps_m", 16, 32))
+        if first and cutv:
+            cp(v("came", 0, 16), src)
+        cp(v("nm", 0, 272), ind(PG, v("cl", 0, 17)))
+        tag["nm", h] = len(ops) - 1
+        turn(v("tt", 0, 256), v("nm", 0, 256))
+        turn(v("tt", 256, 512), v("nm", 16, 272))
+        cp(v(ln, 0, L), ind(v("tt", 0, 512), v("li", 0, 16)))
+        if first and h:
+            hold(v("idb", 128 - 16 * t, 256 - 16 * t), v("lq%d" % (t - 1), 0, L))
+            act(qA, PQ, F.Copy)
+        if first and cutv:
+            act(v("cex", 0, L), ind(v("came", 0, 16), v("le", 0, 16)), F.Identity, 1.0)
+            act(v("nm0", 0, L), v("nm", 0, L), F.Identity, cM15)
+            ts(tC1, v("came", 0, 16), 1.0, A.add, 1 / BIG, A.mult)
+            ts(tC2, v("came", 0, 16), cD, A.subtract, 1 / (BIG * BIG), A.mult)
+        nf = OPT["NF"][h]
+        for i in range(nf):
+            tt(v("pr", 256 * i, 256 * i + 256), ind(KT, v(ln, 16 * i, 16 * i + 16)), q, A.mult)
+        for j in range(nf + 2 - nf % 2, 17, 2):
+            i = max(nf, j - 2)
+            x = v("pr", 256 * i, 256 * j)
+            act(x, ind(KT, v(ln, 16 * i, 16 * j)), F.Copy)
+            tt(x, x, v("ps_q", 0, 256 * (j - i)), A.mult)
+        for a in range(4):
+            for jj in range(16):
+                mm(v("ps_s", 64 * a, 64 * a + 64), v("wd", 15 - jj, 143 - jj), v("pr", 1024 * a + jj, 1024 * a + 1024, 16), jj == 0, jj == 15)
+        act(v("aw", 16, 272), v("ps_s", 0, 256), F.Relu, 1.625)
+        RS = v("ps_r", 0, 272)
+        if OPT["FS"][h] == "1":
+            act(v("be", 0, 272), ind(v("aw", 0, 272), v("lf", 0, 17)), F.Relu, 15 / 16.0, -1.0)
+            act(v("ff", 0, 272), v("be", 0, 272), F.Identity, 1.0, -1.0)
+        else:
+            ts(v("ff", 0, 272), ind(v("aw", 0, 272), v("lf", 0, 17)), 15 / 16.0, A.min, 1 / 16.0, A.add)
+            act(v("be", 0, 272), v("ff", 0, 272), F.Identity, 1.0, -1.0)
+        scan(RS, v("ff", 0, 272), v("d1", 0, 272), A.mult, A.add)
+        tag["scan", h] = len(ops) - 1
+        ts(v("xx", 0, 272), RS, 1 / 16.0, A.is_ge, BIG, A.mult)
+        R16, X16, C15 = v("ps_r", 16, 272, 17), v("xx", 16, 272, 17), v("cs", 15, 272, 17)
+        ts(tB, R16, 1 / 16.0, A.is_lt)
+        tt(v("dn", 0, 272), ind(v("tt", 0, 544), v("lx" if first else "lx1", 0, 17)), v("xx", 0, 272), A.subtract)
+        rn = v("d1", 0, 272, 17) if first else (tR if last else v("sb%d" % t, 32, 48))
+        tt(rn, tB, R16, A.max)
+        scan(v("cs", 0, 272), v("xx", 0, 272), v("dn", 0, 272), A.add, A.min)
+        if first:
+            ts(v("ql", 0, 16), v("cs", 16, 272, 17), BIG, A.add)
+            act(qB, ind(v("kq", 0, W + L), v("ql", 0, 16)), F.Copy)
+            hold(IDB, qB)
+            if cutv:
+                tt(tP1, tC1, X16, A.mult)
+                tt(tP2, tC2, X16, A.mult)
+            src, plus = C15, BIG
+        elif not last:
+            sb = "sb%d" % t
+            ts(v(sb, 16, 32), C15, BIG, A.add)
+            move(v("lc%d" % t, 0, 32), v(sb, 16, 48), 3 * t, 128 * 128)
+            ts(v("ql", 0, 16), v("cs", 16, 272, 17), BIG, A.add)
+            act(v("qs%d" % t, 0, L), ind(v("kq", 0, W + 2 * L), v("ql", 0, 16)), F.Copy)
+            move(v("lq%d" % t, 0, L), v("qs%d" % t, 0, L), 3 * t + 1, 256 * L)
+            tt(v(sb, 0, 16), tB, tP1, A.mult)
+            cp(v("xh", 0, 32), v(sb, 0, 32))
+            tt(v("xl", 0, 32), v(sb, 0, 32), v("xh", 0, 32), A.subtract)
+            mm(v("ps_m", 0, 512), IDB, v("cc", 0, 512), True, False)
+            for jj in range(16):
+                o, s = v("ps_m", jj, 512, 16), v("sel", 128 * jj, 128 * jj + 128)
+                mm(o, s, v("xh", 0, 32), False, False)
+                mm(o, s, v("xl", 0, 32), False, jj == 15)
+            tt(tY, tB, tP2, A.mult)
+            ts(tA, tY, cD8, A.add)
+            tt(v("eq", 0, L), v("cex", 0, L), v("ps_m", 0, L), A.is_equal)
+            tt(v("val", 0, L), v("nm0", 0, L), v("ps_m", L, 2 * L), A.max)
+            scan(v("cnt", 0, L), v("rm", 0, L), v("eq", 0, L), A.mult, A.add)
+            mm(v("ps_m", 0, 32), v("idf", 112 - 16 * t, 240 - 16 * t), v("lc%d" % t, 0, 32), True, True)
+            tt(tZ, v("cnt", 15, L, 16), tA, A.add)
+            ts(v("so", 0, 32, 2), tZ, cD8, A.min, BIG, A.mult)
+            for pl in range(15, -1, -1):
+                cp(ind(PG, v("so", 2 * pl, 2 * pl + 1)), v("val", 16 * pl, 16 * pl + 16))
+            src, plus = v("ps_m", 0, 16), 0.0
+        tt(v("ps_r", 0, 271), v("be", 1, 272), v("ps_r", 0, 271), A.mult)
+        tt(v(wb, 0, 271), v("xx", 0, 271), v("ps_r", 0, 271), A.min)
+        n = 16
+        if not first:
+            n = 17
+            cp(v(wb, 16, 272, 17), rn)
+            ts(v("cl1", 0, 16), C15, BIG, A.add)
+        act(v(wh, 0, 16 * n), ind(v(wb, 0, 272), v("lw", 0, n)), F.Copy)
+        tt(v(wl, 0, 16 * n), ind(v(wb, 0, 272), v("lw", 0, n)), v(wh, 0, 16 * n), A.subtract)
+        for a in range(0, 16, OPT["VS"]):
+            b = a + OPT["VS"]
+            act(v(vg, 256 * a, 256 * b), ind(v("vs", 0, W), v(ln, 16 * a, 16 * b)), F.Sigmoid)
+        if not first:
+            act(v(vg, W, W + L), ind(v("vs", 0, W), v("cl1", 0, 16)), F.Sigmoid)
+        if last:
+            last_products(h)
+        else:
+            products(h)
+        if not first:
+            report(t)
+    key = (n_out, n_in)
+    if key not in ORDER:
+        pace = [(tag[a, h], tag[b, h + d]) for a, b, d, hs in OPT["pace"] for h in hs if (a, h) in tag and (b, h + d) in tag]
+        ORDER[key] = schedule(ops, pace)
+    emit(g, T, [ops[i] for i in ORDER[key]])

@@ -1,89 +1,106 @@
+import numpy as np
 from concourse.mybir import AluOpType, ActivationFunctionType
 
 W, L, NV = 4096, 256, 4
-BIG = 8192.0
-KO = 0
-NB = 3
-OPT = {"NF": [6, 4, 4, 4, 4, 4, 4, 4], "VS": 2, "FS": "01111110", "cy": 0.83, "ga": 1.5, "sc": 3.8, "pe": 0.42, "sem": 60, "dl": 2000, "db": 300.0,
-       "rl": 2500, "rb": 60.0, "rounds": 700, "seed": 1, "amp": 100.0, "drift": 1.004, "moves": 4, "far": 3000.0,
-       "SUM": "dddddddv", "NG": 4, "pace": []}
-SCALES = [{}, {"ga": 0.72, "sc": 0.7}, {"ga": 1.35, "sc": 1.3}, {"pe": 1.4, "sem": 2.0}, {"dma": 1.6, "rem": 1.5}, {"dma": 0.7, "rem": 0.7, "sem": 0.5}]
+BIG, TOP = 8192.0, 4112.0
+PL, LN, SL = 8, 128, 136
+KO = 2 * LN
+NB, NG, NW = 3, 4, 3
+OPT = {"CH": [("V", 24), ("S", 52), ("S", 52)], "N17": "V", "VS": 1024, "cy": 0.83, "ga": 1.56, "sc": 3.8, "pe": 0.42, "sem": 150, "dl": 2200,
+       "db": 250.0, "vo": 10, "so": 65, "rl": 4000, "rb": 60.0, "gi": 1000, "rounds": 1500, "seed": 1, "amp": 100.0, "drift": 1.004,
+       "moves": 4, "far": 3000.0, "SUM": "dddddddddddddddv"}
+SCALES = [{}, {"ga": 0.72, "sc": 0.7}, {"ga": 1.3, "sc": 1.3}, {"pe": 1.4, "sem": 1.6}, {"dma": 1.5, "rem": 1.4}, {"dma": 0.7, "rem": 0.7, "sem": 0.5}]
 
 SCRATCH = {
     "bpk": ("sbuf", [128, W // 2], "int32"), "pg": ("sbuf", [128, W + 16], "int32"),
-    "kq": ("sbuf", [128, W + 2 * L], "bfloat16"), "vs": ("sbuf", [128, W], "bfloat16"),
-    "sti": ("sbuf", [128, 16], "int32"),
-    "pr": ("sbuf", [128, W], "bfloat16"),
-    "vg0": ("sbuf", [128, W + L], "float32"), "vg1": ("sbuf", [128, W + L], "float32"), "vg2": ("sbuf", [128, W + L], "float32"),
-    "vg3": ("sbuf", [128, W + L], "float32"), "lx1": ("sbuf", [128, 18], "uint16"),
-    "cl": ("sbuf", [128, 18], "uint16"), "cl1": ("sbuf", [128, 16], "uint16"), "ql": ("sbuf", [128, 16], "uint16"),
-    "nm": ("sbuf", [128, 272], "float32"), "tt": ("sbuf", [128, 544], "float32"),
-    "ln0": ("sbuf", [128, L], "uint16"), "ln1": ("sbuf", [128, L], "uint16"),
-    "aw": ("sbuf", [128, 272], "float32"), "ff": ("sbuf", [128, 272], "float32"), "be": ("sbuf", [128, 272], "float32"),
-    "d1": ("sbuf", [128, 272], "float32"), "xx": ("sbuf", [128, 272], "float32"), "dn": ("sbuf", [128, 272], "float32"),
-    "cs": ("sbuf", [128, 272], "float32"), "wb0": ("sbuf", [128, 272], "float32"), "wb1": ("sbuf", [128, 272], "float32"),
-    "wh0": ("sbuf", [128, 272], "bfloat16"), "wl0": ("sbuf", [128, 272], "bfloat16"),
-    "wh1": ("sbuf", [128, 272], "bfloat16"), "wl1": ("sbuf", [128, 272], "bfloat16"),
-    "tiny": ("sbuf", [128, 192], "float32"), "came": ("sbuf", [128, 16], "float32"),
-    "cex": ("sbuf", [128, L], "float32"), "nm0": ("sbuf", [128, L], "float32"), "eq": ("sbuf", [128, L], "float32"),
-    "cnt": ("sbuf", [128, L], "float32"), "val": ("sbuf", [128, L], "int32"), "so": ("sbuf", [128, 32], "uint16"),
-    "xh": ("sbuf", [128, 32], "bfloat16"), "xl": ("sbuf", [128, 32], "bfloat16"),
-    "yy": ("sbuf", [128, NV * L], "float32"),
-    "pi": ("sbuf", [128, 8], "int32"), "pf": ("sbuf", [128, 16], "float32"), "ti": ("sbuf", [128, 80], "int32"),
-    "io": ("sbuf", [128, L], "float32"), "jj": ("sbuf", [128, L], "float32"), "rm": ("sbuf", [128, L], "float32"),
-    "tw": ("sbuf", [128, 240], "float32"), "pq": ("sbuf", [128, 32], "float32"),
-    "li": ("sbuf", [128, 16], "uint16"), "le": ("sbuf", [128, 16], "uint16"),
-    "lw": ("sbuf", [128, 18], "uint16"), "lf": ("sbuf", [128, 18], "uint16"), "lx": ("sbuf", [128, 18], "uint16"),
-    "wd": ("sbuf", [128, 144], "bfloat16"), "idf": ("sbuf", [128, 256], "float32"), "idb": ("sbuf", [128, 256], "bfloat16"),
-    "sel": ("sbuf", [128, 2048], "bfloat16"), "cc": ("sbuf", [128, 512], "bfloat16"),
-    "ps_s": ("psum", [128, 512], "float32"), "ps_q": ("psum", [128, 512], "float32"), "ps_r": ("psum", [128, 512], "float32"),
-    "ps_a": ("psum", [128, 512], "float32"), "ps_m": ("psum", [128, 512], "float32"),
-    "ps_w0": ("psum", [128, 512], "float32"), "ps_w1": ("psum", [128, 512], "float32"), "ps_w2": ("psum", [128, 512], "float32"),
+    "kq": ("sbuf", [128, W + 4 * LN], "bfloat16"), "vs": ("sbuf", [128, W], "bfloat16"),
+    "sti": ("sbuf", [128, 16], "int32"), "yr": ("sbuf", [128, L], "float32"), "yy": ("sbuf", [128, NV * L], "float32"),
+    "pi": ("sbuf", [128, 8], "int32"), "pf": ("sbuf", [128, 20], "float32"), "ti": ("sbuf", [128, 80], "int32"),
+    "io": ("sbuf", [128, 256], "float32"), "jj": ("sbuf", [128, LN], "float32"), "rm": ("sbuf", [128, LN], "float32"),
+    "tw": ("sbuf", [128, 200], "float32"),
+    "li": ("sbuf", [128, 8], "uint16"), "le": ("sbuf", [128, 8], "uint16"), "lz": ("sbuf", [128, 8], "uint16"),
+    "lx0": ("sbuf", [128, 10], "uint16"), "lx1": ("sbuf", [128, 10], "uint16"),
+    "idf": ("sbuf", [128, 256], "float32"), "idb": ("sbuf", [128, 256], "bfloat16"),
+    "back": ("sbuf", [128, 256], "float32"), "fore": ("sbuf", [128, 128], "float32"), "roll": ("sbuf", [128, 16, 16], "float32"),
+    "on": ("sbuf", [128, 128 * (NV - 1)], "float32"), "sel": ("sbuf", [128, 1024], "bfloat16"), "cc": ("sbuf", [128, 3 * LN], "bfloat16"),
+    "kc": ("sbuf", [128, SL], "bfloat16"), "zz": ("sbuf", [128, L], "bfloat16"),
+    "ps_a": ("psum", [128, 512], "float32"),
 }
+for _k in range(NB):
+    SCRATCH["ps_w%d" % _k] = ("psum", [128, PL, 64], "float32")
+for _k in range(NG):
+    SCRATCH["vg%d" % _k] = ("sbuf", [128, 16 * LN], "float32")
+    SCRATCH["pd%d" % _k] = ("sbuf", [128, 2 * PL, 8, 16], "float32")
 for _t in range(NV - 1):
-    SCRATCH["sb%d" % _t] = ("sbuf", [128, 48], "float32")
-    SCRATCH["qs%d" % _t] = ("sbuf", [128, L], "bfloat16")
     SCRATCH["as%d" % _t] = ("sbuf", [128, L], "float32")
-    SCRATCH["lc%d" % _t] = ("sbuf", [128, 32], "float32")
-    SCRATCH["lq%d" % _t] = ("sbuf", [128, L], "bfloat16")
     SCRATCH["la%d" % _t] = ("sbuf", [128, L], "float32")
-SEMAPHORES = ["eV", "eS", "eP", "eG"] + ["d%d" % i for i in range(40)] + ["a%d" % i for i in range(9)]
+for _x in range(2):
+    SCRATCH["ps_m%d" % _x] = ("psum", [128, 512], "float32")
+    SCRATCH["ps_s%d" % _x] = ("psum", [128, 512], "float32")
+    for _n, _c, _d in [("cl", PL, "uint16"), ("c1", PL, "uint16"), ("ql", PL, "uint16"), ("ln", LN, "uint16"), ("so", 2 * PL, "uint16"),
+                       ("nm", LN + 16, "float32"), ("tt", 2 * LN + 32, "float32"), ("kr", 16 * LN, "bfloat16"), ("zq", 32 * LN, "bfloat16"),
+                       ("ff", SL, "float32"), ("be", SL, "float32"), ("d1", SL, "float32"), ("xx", SL, "float32"), ("dn", SL, "float32"),
+                       ("ns", 144, "float32"), ("cs", SL, "float32"), ("ty", 4 * PL, "float32"), ("cex", LN, "float32"), ("nm0", LN, "float32"),
+                       ("eq", LN, "float32"), ("cnt", LN, "float32"), ("val", LN, "int32"), ("vr", LN, "float32"),
+                       ("xa", 3 * PL, "bfloat16"), ("xb", 3 * PL, "bfloat16")]:
+        SCRATCH["%s_%d" % (_n, _x)] = ("sbuf", [128, _c], _d)
+    SCRATCH["lv_%d" % _x] = ("sbuf", [128, NW * LN], "uint16")
+    SCRATCH["wa_%d" % _x] = ("sbuf", [128, NW * PL, 17], "bfloat16")
+    SCRATCH["wb_%d" % _x] = ("sbuf", [128, NW * PL, 17], "bfloat16")
+    SCRATCH["sb_%d" % _x] = ("sbuf", [128, NV * 3 * PL], "float32")
+    SCRATCH["qs_%d" % _x] = ("sbuf", [128, (NV - 1) * LN], "bfloat16")
+    SCRATCH["lc_%d" % _x] = ("sbuf", [128, (NV - 1) * 2 * PL], "float32")
+    SCRATCH["lq_%d" % _x] = ("sbuf", [128, (NV - 1) * LN], "bfloat16")
+SEMAPHORES = ["eV", "eS", "eP", "eG"] + ["d%d" % i for i in range(60)] + ["a%d" % i for i in range(15)]
 
 A = AluOpType
 F = ActivationFunctionType
 ORDER = {}
+MASKS = {}
 
 
 def v(name, a, b, s=1):
-    return (name, a, b, s)
+    return (name, (a, b, s))
+
+
+def vn(name, *ix):
+    return (name,) + tuple(i if isinstance(i, int) else (tuple(i) + (1,))[:3] for i in ix)
+
+
+def rows(x, a, b):
+    return ("^", x, a, b)
 
 
 def ind(win, off):
     return ("*", win, off)
 
 
-def cols(x):
-    return 16 * cols(x[2]) if x[0] == "*" else len(range(x[1], x[2], x[3]))
+def name(x):
+    return x[1][0] if x[0] == "^" else x[0]
 
 
 def bits(x):
-    if x[3] == 1:
-        return ((1 << (x[2] - x[1])) - 1) << x[1]
-    m = 0
-    for c in range(x[1], x[2], x[3]):
-        m |= 1 << c
-    return m
+    if x not in MASKS:
+        y, a, b = x[1:] if x[0] == "^" else (x, 0, 128)
+        m = np.zeros([2] + SCRATCH[y[0]][1][1:], bool)
+        m[(slice(a // 64, (b + 63) // 64),) + tuple(i if isinstance(i, int) else slice(*i) for i in y[1:])] = True
+        MASKS[x] = int.from_bytes(np.packbits(m.ravel(), bitorder="little").tobytes(), "little")
+    return MASKS[x]
+
+
+def cols(x):
+    return 16 * cols(x[2]) if x[0] == "*" else bin(bits(x[1] if x[0] == "^" else x)).count("1") // 2
 
 
 def meets(ops):
     hist, before, out = {}, {}, []
     for i, o in enumerate(ops):
         deps = set()
-        acc = [(x[0], bits(x), False) for x in o["r"]] + [(x[0], bits(x), True) for x in o["w"]]
+        acc = [(name(x), bits(x), False) for x in o["r"]] + [(name(x), bits(x), True) for x in o["w"]]
         for b, m, wr in acc:
             h = hist.setdefault(b, [])
             if b.startswith("ps_"):
-                if h and (ops[h[0][0]]["st"] != o["st"] or o["st"] == "P"):
+                if h and h[0][0] != i and (ops[h[0][0]]["st"] != o["st"] or o["st"] == "P"):
                     before[b] = [e[0] for e in h]
                     h[:] = []
                 deps.update(before.get(b, []))
@@ -95,32 +112,29 @@ def meets(ops):
             if wr:
                 h[:] = [e for e in h if (e[1] & ~m) or e[0] == i]
             h.append((i, m, wr))
-        out.append(deps)
+        out.append({j: not o["st"] == ops[j]["st"] == "P" for j in deps if j != i})
     return out
 
 
-def schedule(ops, pace):
+def schedule(ops):
     deps = meets(ops)
     n = len(ops)
     for i, o in enumerate(ops):
         if o["e"] is None:
-            deps[i].add(o["from"])
-    for a, b in pace:
-        deps[b].add(a)
+            deps[i][o["from"]] = False
     succ = [[] for _ in ops]
     for i in range(n):
         for j in deps[i]:
             succ[j].append(i)
-    gap = lambda j, i: 0 if ops[i]["e"] is None or ops[i]["st"] == ops[j]["st"] == "P" else OPT["sem"]
     c, lat = [o["c"] for o in ops], [o["lat"] for o in ops]
+    gap = lambda j, i: OPT["sem"] if deps[i][j] and ops[i]["e"] is not None else 0
+    fore = [[(j, lat[j] + gap(j, i)) for j in deps[i]] for i in range(n)]
+    aft = [[(k, c[k] + lat[i] - c[i] + gap(i, k)) for k in succ[i]] for i in range(n)]
 
     def place(order, back):
         at, busy = [0.0] * n, {e: [] for e in "VSPGY"}
         for i in order:
-            if back:
-                t = max([at[k] + c[k] + lat[i] - c[i] + gap(i, k) for k in succ[i]] + [lat[i] - c[i]])
-            else:
-                t = max([at[j] + lat[j] + gap(j, i) for j in deps[i]] + [0.0])
+            t = max([at[k] + d for k, d in (aft[i] if back else fore[i])] + [lat[i] - c[i] if back else 0.0])
             if ops[i]["e"] is not None:
                 b = busy[ops[i]["e"]]
                 lo, hi = 0, len(b)
@@ -172,11 +186,12 @@ def schedule(ops, pace):
         key = shaken([-u[i] - c[i] for i in range(n)], OPT["amp"], False)
         new = place(sorted(range(n), key=lambda i: (key[i], i)), False)
         order = sorted(range(n), key=lambda i: (-1.0 if ops[i].get("load") else new[i], i))
-        end = sum(replay(order, s) for s in SCALES) / len(SCALES)
+        ends = [replay(order, s) for s in SCALES]
+        end = sum(ends) / len(ends)
         if best is None or end < best[0]:
-            best = (end, order, new)
+            best = (end, order, new, ends)
         at = new if end < best[0] * OPT["drift"] else best[2]
-    ORDER["end"] = best[0]
+    ORDER["end"] = (best[0], best[3])
     return best[1]
 
 
@@ -191,7 +206,7 @@ def emit(g, T, ops):
             continue
         k = known[o["e"]]
         for j in sorted(deps, reverse=True):
-            if k.get(ops[j]["st"], -1) >= j or o["st"] == ops[j]["st"] == "P":
+            if k.get(ops[j]["st"], -1) >= j or not deps[j]:
                 continue
             ws.append(j)
             needed.add(j)
@@ -234,15 +249,16 @@ def rank_program(g, core, T, topo):
     mask = topo.mask(core, nxt)
     n_out = len(topo.engines(core, nxt))
     n_in = len(topo.engines(T.cores[(rank - 1) % len(T.cores)], core))
-    ops, nd, loaded, hop = [], [0], [0.0], [9]
+    ops, nd, na, loaded, hop = [], [0], [0], [0.0], ["c"]
     cy = OPT["cy"]
 
     def ap(x):
         if x[0] == "*":
             return ap(x[1]).indirect(ap(x[2]))
-        return T[x[0]][:, x[1]:x[2]] if x[3] == 1 else T[x[0]][:, x[1]:x[2]:x[3]]
+        y, p = (x[1], slice(x[2], x[3])) if x[0] == "^" else (x, slice(None))
+        return T[y[0]][(p,) + tuple(i if isinstance(i, int) else slice(*i[:2]) if i[2] == 1 else slice(*i) for i in y[1:])]
 
-    def rec(e, f, outs, ins, c, sem=None, n=0, lat=None, dma=0):
+    def rec(e, f, outs, ins, c, sem=None, n=0, lat=None):
         r, w = [], []
         for x in ins:
             if isinstance(x, tuple):
@@ -254,15 +270,15 @@ def rank_program(g, core, T, topo):
             else:
                 w.append(x)
         ops.append({"e": e, "f": f, "r": r, "w": w, "sem": sem, "n": n, "st": sem or e, "c": c, "lat": c if lat is None else lat, "from": len(ops) - 1,
-                    "grp": "%s%d%s" % (e, hop[0], (w or r)[0][0][:4]),
+                    "grp": "%s%s%s" % (e, hop[0], name((w or r)[0])[:4]),
                     "k": "pe" if e == "P" else ("dma" if n == 16 else "rem") if sem else "sc" if outs[0][0] == "*" else "ga" if ins and ins[0][0] == "*" else ""})
 
-    def cost(o, a, k=1.0):
+    def cost(o, a, k=1.0, fixed=50):
         if o[0] == "*":
-            return 50 + cols(o) * OPT["sc"] * cy
+            return fixed + cols(o) * OPT["sc"] * cy
         if a[0] == "*":
-            return 55 + cols(a) * OPT["ga"] * cy
-        return max(64, cols(a) * k) * cy
+            return fixed + cols(a) * OPT["ga"] * cy
+        return OPT["vo"] + max(64, cols(a) * k) * cy
 
     def num(x):
         return ap(x) if isinstance(x, tuple) else x
@@ -271,7 +287,7 @@ def rank_program(g, core, T, topo):
         rec("V", lambda q: q.tensor_copy(ap(o), ap(i)), [o], [i], cost(o, i))
 
     def tt(o, a, b, op):
-        rec("V", lambda q: q.tensor_tensor(ap(o), ap(a), ap(b), op), [o], [a, b], cost(o, a, 1.0 if b[0].startswith("ps_") else 2.0))
+        rec("V", lambda q: q.tensor_tensor(ap(o), ap(a), ap(b), op), [o], [a, b], cost(o, a, 1.0 if "ps_" in (name(a)[:3], name(b)[:3]) else 2.0))
 
     def ts(o, a, s1, op0, s2=None, op1=None):
         if op1 is None:
@@ -285,17 +301,23 @@ def rank_program(g, core, T, topo):
     def turn(o, i):
         rec("V", lambda q: q.transpose(ap(o), ap(i)), [o], [i], cost(o, i))
 
-    def fill_const(o, c):
-        rec("V", lambda q: q.memset(ap(o), c), [o], [], cost(o, o))
+    def fill(o, c):
+        rec("V", lambda q: q.memset(ap(o), c), [o], [], cost(o, o, 0.5 if SCRATCH[name(o)][2] == "bfloat16" else 1.0))
 
     def act(o, i, fn, bias=None, scale=None):
+        c = cost(o, i, 1.0, OPT["so"])
         if bias is None:
-            rec("S", lambda q: q.activation(ap(o), ap(i), fn), [o], [i], cost(o, i))
+            rec("S", lambda q: q.activation(ap(o), ap(i), fn), [o], [i], c)
         else:
-            rec("S", lambda q: q.activation(ap(o), ap(i), fn, bias=num(bias), scale=1.0 if scale is None else scale), [o], [i, bias], cost(o, i))
+            rec("S", lambda q: q.activation(ap(o), ap(i), fn, bias=num(bias), scale=1.0 if scale is None else scale), [o], [i, bias], c)
 
-    def mm(o, lt, r, start, stop):
-        rec("P", lambda q: q.matmul(ap(o), ap(lt), ap(r), start, stop), [o], [lt, r], max(64, cols(r)) * OPT["pe"] * (4 if lt[0] == "idf" else 1))
+    def mms(calls):
+        def f(q):
+            for o, lt, r, start, stop in calls:
+                ins = q.matmul(ap(o), ap(lt), ap(r), start, stop)
+            return ins
+        rec("P", f, list(dict.fromkeys(x[0][1] if x[0][0] == "^" else x[0] for x in calls)), list(dict.fromkeys([x[1] for x in calls] + [x[2] for x in calls])),
+            sum(max(min(64, cols(x[1])), cols(x[2])) * OPT["pe"] * (4 if SCRATCH[x[1][0]][2] == "float32" else 1) for x in calls))
 
     def dsem():
         nd[0] += 1
@@ -311,10 +333,11 @@ def rank_program(g, core, T, topo):
         s = dsem()
         rec("Y", lambda q: q.dma_start(dst, ap(i)).then_inc(T.sem[s], 16), [], [i], 100, s, 16, OPT["dl"] + 500)
 
-    def move(land, i, k, nbytes):
-        s = dsem()
-        rec("G", lambda q: q.remote_dma(ap(land), ap(i), T.sem["a%d" % k], T.sem[s], pid, rid, mask), [], [i], 500, s, n_out, OPT["rl"] + nbytes / OPT["rb"])
-        rec(None, None, [land], [], 0, "a%d" % k, n_in)
+    def move(land, i, nbytes):
+        s, a = dsem(), "a%d" % na[0]
+        na[0] += 1
+        rec("G", lambda q: q.remote_dma(ap(land), ap(i), T.sem[a], T.sem[s], pid, rid, mask), [], [i], OPT["gi"], s, n_out, OPT["rl"] + nbytes / OPT["rb"])
+        rec(None, None, [land], [], 0, a, n_in)
 
     load("Y", v("sti", 0, 16), T.st[:], 8192)
     NP = 4
@@ -330,265 +353,265 @@ def rank_program(g, core, T, topo):
         else:
             rec("G", lambda q: q.iota(ap(o), pat, base, cm), [o], [], 130 + 2 * cy * cols(o))
     iota(v("pi", 0, 1), [[0, 1]], 0, 1, False)
-    iota(v("io", 0, L), [[1, L]], 0, 0, True)
-    iota(v("jj", 0, L), [[0, 16], [1, 16]], 0, 0, True)
-    iota(v("sel", 0, 2048), [[0, 2048]], 1, 0, True)
-    rec("G", lambda q: q.affine_select(T.sel[:], T.sel[:], [[-1, 16], [-16, 8], [0, 16]], A.is_equal, 0.0, 0, 1), [v("sel", 0, 2048)], [v("sel", 0, 2048)], 170 + 4096 * cy)
-    fill_const(v("d1", 0, 272), 0.0)
-    fill_const(v("wb0", 256, 272), 0.0)
-    fill_const(v("aw", 0, 16), -1.0 / 16)
-    fill_const(v("pg", W, W + 16), 0)
-    fill_const(v("d1", 0, 272, 17), 1.0)
-    ts(v("pi", 1, 2), v("pi", 0, 1), 15, A.bitwise_and)
-    ts(v("pi", 2, 3), v("pi", 0, 1), 4, A.logical_shift_right)
-    ts(v("pi", 3, 4), v("pi", 0, 1), 112, A.bitwise_and)
-    cp(v("pf", 0, 4), v("pi", 0, 4))
-    cP, cR, cX, cG = [v("pf", k, k + 1) for k in range(4)]
-    c17, cD, cD8, cM15, cN15, cG15 = [v("pf", k, k + 1) for k in range(4, 10)]
-    ts(c17, cR, 17.0, A.mult)
+    iota(v("io", 0, 256), [[0, 2], [1, 128]], 0, 0, True)
+    iota(v("tw", 9, 17), [[0, 2], [2, 4]], 0, 0, True)
+    iota(v("tw", 29, 37), [[8, 2], [0, 4]], 0, 0, True)
+    iota(v("jj", 0, LN), [[0, PL], [1, 16]], 0, 0, True)
+    iota(vn("roll", (0, 16), (0, 16)), [[8, 16], [0, 2], [1, 8]], 0, 0, True)
+    iota(v("sel", 0, 1024), [[0, 1024]], 0, 0, True)
+    for a in (0, 64):
+        rec("G", lambda q, a=a: q.affine_select(T.sel[:], T.sel[:], [[-8, 8], [-1, 8], [0, 16]], A.not_equal, 1.0, -a, 1),
+            [v("sel", 0, 1024)], [v("sel", 0, 1024)], 170 + 2048 * cy)
+    fill(v("zq_0", 0, 32 * LN), 0.0)
+    act(v("zq_1", 0, 32 * LN), v("zq_0", 0, 32 * LN), F.Copy)
+    fill(v("pg", W, W + 16), 0)
+    fill(v("kc", 0, SL), 1.6875)
+    fill(v("kc", 0, SL, 17), 0.0)
+    fill(v("zz", 0, L), 0.0)
+    fill(v("cc", 2 * LN, 3 * LN), 0.0)
+    for k, (s, op) in enumerate([(15, A.bitwise_and), (4, A.logical_shift_right), (7, A.bitwise_and), (3, A.logical_shift_right), (3, A.bitwise_and)]):
+        ts(v("pi", k + 1, k + 2), v("pi", 0, 1), s, op)
+    cp(v("pf", 0, 6), v("pi", 0, 6))
+    cP, cR, cX, cR7, cP8, cR3 = [v("pf", k, k + 1) for k in range(6)]
+    cD, cM15, cN15, cR8, cF, cB, cZ = [v("pf", k, k + 1) for k in range(6, 13)]
     ts(cD, cR, float(W), A.add)
-    ts(cD8, cR, float(W), A.add, 1 / BIG, A.mult)
     ts(cM15, cR, 15.0, A.is_equal, -BIG, A.mult)
     ts(cN15, cR, 15.0, A.not_equal, -BIG, A.mult)
-    ts(cG15, cG, 15.0, A.add)
-    tE, tS, tU, tV = [v("tw", 20 * k, 20 * k + 17) for k in range(4)]
-    wPL, wA, wB, wC, wO = [v("tw", 20 * k, 20 * k + 18) for k in range(4, 9)]
-    ts(tE, v("io", 0, 17), 16.0, A.mult, cR, A.add)
-    ts(tU, tE, -8.0, A.add, 1 / 17.0, A.mult)
-    cp(v("ti", 0, 17), tU)
-    cp(v("ti", 17, 18), v("pi", 1, 2))
-    cp(wPL, v("ti", 0, 18))
-    tPL = v("tw", 80, 97)
-    ts(tV, tPL, -17.0, A.mult)
-    tt(tS, tE, tV, A.add)
-    ts(v("ti", 20, 38), wPL, cX, A.add)
-    ts(v("ti", 20, 38), v("ti", 20, 38), 1, A.bitwise_and)
-    cp(wO, v("ti", 20, 38))
-    ts(v("ti", 40, 58), wPL, 16.0, A.mult, 240.0, A.add)
-    ts(v("ti", 40, 58), v("ti", 40, 58), 255, A.bitwise_and)
+    ts(cR8, cR, 8.0, A.is_ge)
+    ts(cF, cR, 8.0, A.mult, cX, A.add)
+    ts(cB, cR7, 16.0, A.mult, cP8, A.add)
+    ts(cZ, cR3, 8.0, A.mult, cX, A.add)
+    ts(cZ, cR, 32.0, A.mult, cZ, A.add)
+    ts(v("lz", 0, 8), v("io", 0, 8), 512.0, A.mult, cZ, A.add)
+    wPL, wN, wE, wA, wB, wO, wQ = [v("tw", 20 * k, 20 * k + 17) for k in range(7)]
+    tPL, tN, tE, tA9, tB9, tO9, tQ = [v("tw", 20 * k, 20 * k + 9) for k in range(7)]
+    ts(tE, v("io", 0, 9), 16.0, A.mult, cR, A.add)
+    ts(v("ti", 0, 9), tE, -8.0, A.add, 1 / 17.0, A.mult)
+    cp(tPL, v("ti", 0, 9))
+    ts(tN, tPL, -17.0, A.mult)
+    tt(tN, tN, tE, A.add)
+    ts(v("tw", 9, 17), v("tw", 9, 17), cR8, A.add)
+    ts(v("tw", 29, 37), v("tw", 29, 37), cR7, A.add)
+    ts(v("ti", 20, 37), wPL, cX, A.add)
+    ts(v("ti", 20, 37), v("ti", 20, 37), 1, A.bitwise_and)
+    cp(wO, v("ti", 20, 37))
+    ts(v("ti", 40, 57), wPL, 16.0, A.mult, LN - 16.0, A.add)
+    ts(v("ti", 40, 57), v("ti", 40, 57), LN - 1, A.bitwise_and)
     ts(wA, wPL, 16.0, A.mult)
-    ts(wB, v("ti", 40, 58), 256.0, A.add)
+    ts(wB, v("ti", 40, 57), float(LN), A.add)
     tt(wB, wB, wA, A.subtract)
     tt(wB, wB, wO, A.mult)
-    tt(wC, wB, wA, A.add)
-    ts(v("li", 0, 16), v("io", 0, 16), v("tw", 157, 158), A.add)
-    tt(tV, tS, v("tw", 140, 157), A.add)
-    tQ, tK = v("tw", 180, 197), v("tw", 200, 217)
-    ts(tQ, tS, 16.0, A.is_equal)
-    ts(tK, tPL, 512.0, A.add)
-    tt(tK, tK, tV, A.subtract)
-    tt(tK, tK, tQ, A.mult)
-    tt(tV, tV, tK, A.add)
-    cp(v("lx", 0, 17), tV)
+    tt(wA, wA, wN, A.add)
+    tt(wA, wA, wB, A.add)
+    cp(v("li", 0, 8), v("tw", 69, 77))
+    ts(tQ, tN, 16.0, A.is_equal)
+    ts(tB9, tPL, 2.0 * LN, A.add)
+    tt(tB9, tB9, tA9, A.subtract)
+    tt(tB9, tB9, tQ, A.mult)
+    tt(tA9, tA9, tB9, A.add)
+    cp(v("lx0", 0, 9), tA9)
     ts(tQ, tQ, 16.0, A.mult)
-    tt(tV, tV, tQ, A.add)
-    cp(v("lx1", 0, 17), tV)
-    ts(tU, tS, 16.0, A.mult)
-    tt(tU, tU, tPL, A.add)
-    cp(v("lf", 0, 17), tU)
-    cp(v("le", 0, 16), v("io", 0, 16))
-    ts(v("lw", 0, 17), v("io", 0, 17), c17, A.add)
-    ts(v("tt", 512, 528), v("tw", 0, 16), float(W), A.add)
-    ts(v("tt", 528, 544), v("tw", 0, 16), float(W + L), A.add)
-    ts(v("wd", 0, 144), v("io", 0, 144), cG15, A.is_equal, -1 / 1024.0, A.mult)
-    ts(v("idf", 0, 128), v("io", 0, 128), cP, A.is_equal)
-    ts(v("idb", 0, 128), v("io", 0, 128), cP, A.is_equal)
-    act(v("idf", 128, 256), v("idf", 0, 128), F.Copy)
-    act(v("idb", 128, 256), v("idb", 0, 128), F.Copy)
-    ts(v("cc", 0, 256), v("jj", 0, 256), cR, A.is_ge, BIG, A.mult)
-    act(v("cc", 256, 512), v("jj", 0, 256), F.Identity, cN15, 0.0)
-    act(v("rm", 0, 256), v("jj", 0, 256), F.Sign)
-    cp(v("cl1", 0, 16), v("sti", 0, 16))
+    tt(tA9, tA9, tQ, A.add)
+    cp(v("lx1", 0, 9), tA9)
+    cp(v("le", 0, 8), v("io", 0, 8))
+    ts(v("idf", 0, 256), v("io", 0, 256), cP, A.is_equal)
+    act(v("idb", 0, 256), v("idf", 0, 256), F.Copy)
+    ts(v("back", 0, 256), v("io", 0, 256), cB, A.is_equal)
+    ts(v("fore", 0, 128), v("io", 0, 128), cF, A.is_equal)
+    ts(vn("roll", (0, 16), (0, 16)), vn("roll", (0, 16), (0, 16)), cP, A.is_equal)
+    for t in range(1, NV):
+        act(v("on", 128 * t - 128, 128 * t), vn("roll", (0, 16), (8 - t, 16 - t)), F.Copy)
+    ts(v("cc", 0, LN), v("jj", 0, LN), cR, A.is_ge, -BIG, A.mult)
+    act(v("cc", LN, 2 * LN), v("jj", 0, LN), F.Identity, cN15, 0.0)
+    act(v("rm", 0, LN), v("jj", 0, LN), F.Sign)
+    QW = [[(LN, LN + W), (0, KO + W)], [(KO, W + LN), (KO, W + 2 * LN)]]
+    QA, QB = [v("kq", LN, KO), v("kq", KO + W, KO + W + LN)], [v("kq", 0, LN), v("kq", KO + W + LN, KO + W + 2 * LN)]
+    for x in range(2):
+        fill(v("d1_%d" % x, 0, SL), 0.0)
+        fill(v("d1_%d" % x, 0, SL, 17), 1.0)
+        fill(v("ps_s%d" % x, 3 * SL - 1, 3 * SL), 0.0)
+        for k, own in enumerate((QA[x], QB[x])):
+            ts(v("tt_%d" % x, 2 * LN + 16 * k, 2 * LN + 16 * k + 9), tE, float(own[1][0] - KO), A.add)
     for k in range(NP):
         ts(v("pg", k * pc, (k + 1) * pc), v("bpk", k * pc, (k + 1) * pc), W - 1, A.bitwise_and)
         ts(v("pg", W // 2 + k * pc, W // 2 + (k + 1) * pc), v("bpk", k * pc, (k + 1) * pc), 12, A.logical_shift_right)
 
-    KT, PG = v("kq", KO, KO + W), v("pg", 0, W + 16)
-    qA, qB, PQ, PA = v("kq", W, W + L), v("kq", W + L, W + 2 * L), v("ps_q", 0, L), v("ps_a", 0, L)
-    IDF, IDB = v("idf", 0, 128), v("idb", 0, 128)
-    tB, tT, tM, tC1, tC2, tP1, tP2, tA, tZ, tR, tY = [v("tiny", 16 * k, 16 * k + 16) for k in range(11)]
-    bank, NG, tag = [0], OPT["NG"], {}
+    KT, PG, VS = v("kq", KO, KO + W), v("pg", 0, W + 16), v("vs", 0, W)
+    IDF, IDB, BACK, FORE, PA = v("idf", 0, 128), v("idb", 0, 128), v("back", 0, 128), v("fore", 0, 128), v("ps_a", 0, L)
+    bank = [0]
 
-    def products(h):
-        vg, wh, wl = "vg%d" % (h % NG), "wh%d" % (h % 2), "wl%d" % (h % 2)
-        for j0 in range(8 + h % 2):
+    def split(src, a, b, scalar):
+        for p, z in ((0, a), (64, b)):
+            if scalar:
+                act(rows(z, p, p + 64), rows(src, p, p + 64), F.Copy)
+            else:
+                cp(rows(z, p, p + 64), rows(src, p, p + 64))
+            tt(rows(z, 64 - p, 128 - p), rows(src, p, p + 64), rows(z, p, p + 64), A.subtract)
+
+    def chain(h, x):
+        t, first, last = h // 2, h % 2 == 0, h == 2 * NV - 1
+        cutv, p0 = t < NV - 1, PL * (1 - x)
+        hop[0] = "%d%d" % (h, x)
+        b = lambda name, a, e, s=1: v("%s_%d" % (name, x), a, e, s)
+        ps = lambda a, e, s=1: v("ps_s%d" % x, a, e, s)
+        pm = lambda a, e, s=1: v("ps_m%d" % x, a, e, s)
+        came, camp, tB, tP = [b("ty", PL * k, PL * k + PL) for k in range(4)]
+        cl, tw, zq, e0 = b("cl", 0, PL), b("tt", 0, 2 * LN + 32), ind(b("zq", 0, 32 * LN), v("lz", 0, PL)), 3 * SL
+        if h == 0:
+            cp(cl, v("sti", p0, p0 + PL))
+            ts(came, v("sti", p0, p0 + PL), -1.0, A.mult, TOP, A.add)
+            mms([(ps(e0, e0 + PL), FORE, came, True, True)])
+            cp(camp, ps(e0, e0 + PL))
+        elif first:
+            s0 = 2 * PL * (t - 1)
+            mms([(ps(e0, e0 + PL), v("back", 128 - 16 * t, 256 - 16 * t), b("lc", s0, s0 + PL), True, True),
+                 (ps(e0 + PL, e0 + 3 * PL), v("on", 128 * t - 128, 128 * t), b("lc", s0, s0 + 2 * PL), True, True)])
+            ts(cl, ps(e0, e0 + PL), 0.0, A.add)
+            cp(b("d1", 0, SL, 17), ps(e0 + 2 * PL, e0 + 3 * PL))
+            if cutv:
+                ts(b("ty", 0, 2 * PL), ps(e0, e0 + 2 * PL), -1.0, A.mult, TOP, A.add)
+        cp(b("ln", 0, LN), ind(PG, cl))
+        if h == 0:
+            act(QA[x], ind(KT, cl), F.Copy)
+        elif first:
+            mms([(pm(2 * LN, 3 * LN), v("idb", 128 - 16 * t, 256 - 16 * t), b("lq", LN * (t - 1), LN * t), True, True)])
+            act(QA[x], pm(2 * LN, 3 * LN), F.Copy)
+        if first:
+            cp(zq, QA[x])
+        mms([(ps(0, SL), IDB, v("kc", 0, SL), True, False)])
+        l0 = 0
+        for e, n in OPT["CH"]:
+            o, i = b("kr", 16 * l0, 16 * (l0 + n)), ind(KT, b("ln", l0, l0 + n))
+            if e == "S":
+                act(o, i, F.Identity, 0.0, -1 / 1024.0)
+            else:
+                ts(o, i, -1 / 1024.0, A.mult)
+            mms([(rows(ps(17 * (l // 16) + 1, 17 * (l // 16) + 17), 32 * (l % 16 // 4), 32 * (l % 16 // 4) + 32), b("zq", 32 * l, 32 * l + 32),
+                  b("kr", 16 * l, 16 * l + 16), False, l >= LN - 16 and l % 4 == 3) for l in range(l0, l0 + n)])
+            l0 += n
+        cp(b("nm", 0, LN), b("ln", 0, LN))
+        cp(b("nm", LN, LN + 16), b("ln", 0, 16))
+        turn(b("tt", 0, LN), b("nm", 0, LN))
+        turn(b("tt", LN, 2 * LN), b("nm", 16, LN + 16))
+        k = h % NW
+        if OPT["N17"] == "V":
+            cp(b("ns", 0, 144), ind(tw, v("lx%d" % (h % 2), 0, 9)))
+        else:
+            act(b("ns", 0, 144), ind(tw, v("lx%d" % (h % 2), 0, 9)), F.Copy)
+        mms([(pm(0, SL), FORE, b("ns", 0, SL), True, True)])
+        cp(b("lv", LN * k, LN * k + LN), ind(tw, v("li", 0, 8)))
+        if first and cutv:
+            act(b("cex", 0, LN), ind(came, v("le", 0, 8)), F.Copy)
+            act(b("nm0", 0, LN), b("nm", 0, LN), F.Identity, cM15)
+        RS, WW = ps(SL, 2 * SL), ps(2 * SL, 3 * SL)
+        ts(b("ff", 0, SL), ps(0, SL), 1.0, A.min, 1 / 16.0, A.max)
+        scan(RS, b("ff", 0, SL), b("d1", 0, SL), A.mult, A.max)
+        act(b("be", 0, SL), b("ff", 0, SL), F.Identity, 1.0, -1.0)
+        ts(b("xx", 0, SL), RS, 1 / 16.0, A.is_ge, BIG, A.mult)
+        R16, X16, C15 = ps(SL + 16, 2 * SL, 17), b("xx", 16, SL, 17), b("cs", 15, SL, 17)
+        tt(b("dn", 0, SL), pm(0, SL), b("xx", 0, SL), A.subtract)
+        scan(b("cs", 0, SL), b("xx", 0, SL), b("dn", 0, SL), A.add, A.min)
+        s0, m0 = 3 * PL * t, 3 * LN
+        w0, wn = QW[x][h % 2]
+        mms([(pm(m0, m0 + PL), BACK, C15, True, True)] + ([] if last else [(pm(m0 + PL, m0 + 2 * PL), BACK, b("cs", 16, SL, 17), True, True)]))
+        if not first and cutv:
+            ts(b("sb", s0 + PL, s0 + 2 * PL), C15, BIG, A.add)
+        ts(tB, R16, 1 / 16.0, A.is_lt)
+        tt(b("d1", 0, SL, 17) if first else b("sb", s0 + 2 * PL, s0 + 3 * PL), tB, R16, A.max)
+        if not first and cutv:
+            move(b("lc", 2 * PL * t, 2 * PL * (t + 1)), b("sb", s0 + PL, s0 + 3 * PL), 128 * 64)
+        ts(cl if first else b("c1", 0, PL), pm(m0, m0 + PL), BIG, A.add)
+        if not last:
+            ts(b("ql", 0, PL), pm(m0 + PL, m0 + 2 * PL), BIG + KO - w0, A.add)
+            act(QB[x] if first else b("qs", LN * t, LN * t + LN), ind(v("kq", w0, w0 + wn), b("ql", 0, PL)), F.Copy)
+        if first:
+            cp(zq, QB[x])
+            if cutv:
+                tt(tP, X16, camp, A.min)
+        elif cutv:
+            move(b("lq", LN * t, LN * t + LN), b("qs", LN * t, LN * t + LN), 256 * LN)
+        tt(ps(2 * SL, 3 * SL - 1), b("be", 1, SL), ps(SL, 2 * SL - 1), A.mult)
+        tt(WW, b("xx", 0, SL), WW, A.min)
+        split(WW, vn("wa_%d" % x, (PL * k, PL * k + PL), (0, 17)), vn("wb_%d" % x, (PL * k, PL * k + PL), (0, 17)), True)
+        if first:
+            return
+        a = 0 if cutv else 2 * PL
+        if cutv:
+            tt(b("sb", s0, s0 + PL), tP, X16, A.subtract)
+        split(b("sb", s0 + a, s0 + 3 * PL), b("xa", a, 3 * PL), b("xb", a, 3 * PL), False)
+        calls = [(pm(m0, m0 + PL), BACK, b("sb", s0, s0 + PL), True, True), (pm(0, 3 * LN), IDB, v("cc", 0, 3 * LN), True, False)] if cutv else []
+        for jj in range(16):
+            calls.append((pm(16 * a + jj, 3 * LN, 16), v("sel", 128 * (jj % 8), 128 * (jj % 8) + 128), b("xb" if jj // 8 else "xa", a, 3 * PL), not cutv, jj == 15 or not cutv))
+        mms(calls)
+        if cutv:
+            tt(b("eq", 0, LN), b("cex", 0, LN), pm(0, LN), A.is_equal)
+            ts(b("eq", 15, LN, 16), pm(m0, m0 + PL), -1 / BIG, A.mult, TOP / BIG, A.add)
+            tt(b("val", 0, LN), b("nm0", 0, LN), pm(LN, 2 * LN), A.max)
+            scan(b("cnt", 0, LN), v("rm", 0, LN), b("eq", 0, LN), A.mult, A.max)
+            ts(b("so", 0, 2 * PL, 2), b("cnt", 15, LN, 16), BIG, A.mult, cD, A.min)
+        act(b("vr", 0, LN), ind(VS, b("c1", 0, PL)), F.Sigmoid)
+        tt(v("yr", 16 * p0, 16 * p0 + LN), b("vr", 0, LN), pm(2 * LN, 3 * LN), A.mult)
+
+    def shortcuts(x):
+        for pl in range(PL - 1, -1, -1):
+            cp(ind(PG, v("so_%d" % x, 2 * pl, 2 * pl + 1)), v("val_%d" % x, 16 * pl, 16 * pl + 16))
+
+    def values(h, x):
+        u0, k, t = 2 * h + x, h % NW, h // 2
+        hop[0] = "%d%d" % (h, x)
+        vg, pd, how = "vg%d" % (u0 % NG), "pd%d" % (u0 % NG), OPT["SUM"][u0]
+        acc = v("ps_a", LN * (1 - x), LN * (2 - x))
+        for a in range(0, 16 * LN, OPT["VS"]):
+            act(v(vg, a, a + OPT["VS"]), ind(VS, v("lv_%d" % x, LN * k + a // 16, LN * k + (a + OPT["VS"]) // 16)), F.Sigmoid)
+        if h % 2 == 0 and x == 0:
+            mms([(PA, IDB, v("zz", 0, L), True, False)])
+        if h % 2 and x and t and how != "d":
+            mms([(PA, v("idf", 128 - 16 * t, 256 - 16 * t), v("la%d" % (t - 1), 0, L), False, False)])
+        kept = {}
+        for nh, j0 in ([(0, 0), (1, 0), (0, 1), (1, 1)] if how == "v" else [(0, 0), (0, 1), (1, 0), (1, 1)]):
             bk = "ps_w%d" % (bank[0] % NB)
             bank[0] += 1
-            for u, jj in enumerate((j0, j0 + 8) if j0 < 8 else range(16)):
-                s = v("sel", 128 * jj, 128 * jj + 128)
-                b, a0, a1 = (v(bk, u, 512, 2), 0, 256) if j0 < 8 else (v(bk, u, 256, 16), 256, 272)
-                mm(b, s, v(wh, a0, a1), True, False)
-                mm(b, s, v(wl, a0, a1), False, True)
-            x, b = (v(vg, j0, W, 8), v(bk, 0, 512)) if j0 < 8 else (v(vg, W, W + L), v(bk, 0, L))
-            tt(x, x, b, A.mult)
-            tag["p%d" % j0, h] = len(ops) - 1
-        m = 16
-        if OPT["SUM"][h] == "d":
-            s, m = dsem(), 8
-            o, i = v(vg, 0, 2048), v(vg, 2048, 4096)
-            rec("G", lambda q: q.dma_start(ap(o), ap(i), accum_op=A.add).then_inc(T.sem[s], 16), [o], [o, i], 1000, s, 16, OPT["dl"] + 2 ** 21 / OPT["db"])
-        t = h // 2
-        for k in range(m):
-            mm(PA, IDF, v(vg, 256 * k, 256 * k + 256), h % 2 == 0 and k == 0, h == 1 and k == m - 1)
-            tag["s%d" % k, h] = len(ops) - 1
-        if t and (h % 2 or t == NV - 1):
-            mm(PA, v("idf", 128 - 16 * t, 256 - 16 * t), v("la%d" % (t - 1), 0, L), False, t < NV - 1)
-
-    def last_products(h):
-        vg, wh, wl = "vg%d" % (h % NG), "wh%d" % (h % 2), "wl%d" % (h % 2)
-        for c in range(2):
-            n = 144 if c else 128
-            for j0 in range(0, 16, 2):
-                bk = "ps_w%d" % (bank[0] % NB)
-                bank[0] += 1
-                t1, t2, t3 = [], [], []
-                for u in range(2):
-                    jj, o = j0 + u, 256 * u
-                    s = v("sel", 128 * jj, 128 * jj + 128)
-                    mm(v(bk, o, o + n), s, v(wh, 128 * c, 128 * c + n), True, False)
-                    mm(v(bk, o, o + n), s, v(wl, 128 * c, 128 * c + n), False, True)
-                    x0 = 2048 * c
-                    xb, xa, xc = v(vg, x0 + jj + 1024, x0 + 16 * n, 16), v(vg, x0 + jj, x0 + 1024, 16), v(vg, x0 + jj + 1024, x0 + 2048, 16)
-                    t1.append((xb, xb, v(bk, o + 64, o + n), A.mult))
-                    t2.append((v(bk, o, o + 64), xa, v(bk, o, o + 64), A.mult))
-                    t3.append((xc, xc, v(bk, o, o + 64), A.add))
-                for x in t1 + t2 + t3:
-                    tt(*x)
-            for k in range(8 * c + 4, 8 * c + 8 - 2 * c):
-                mm(PA, IDF, v(vg, 256 * k, 256 * k + 256), False, k == 13)
-        x = v("ps_r", 0, L)
-        cp(x, v(vg, 256 * 14, 256 * 15))
-        tt(x, v(vg, 256 * 15, 256 * 16), x, A.add)
-        tt(v(vg, W, W + L), v(vg, W, W + L), x, A.add)
+            mms([(vn(bk, (0, PL), (u, 64, 8)), v("sel", 128 * ((j0 + 2 * u) % 8), 128 * ((j0 + 2 * u) % 8) + 128),
+                  vn("w%s_%d" % ("ab"[u // 4], x), (PL * k, PL * k + PL), (8 * nh, 8 * nh + 8)), True, True) for u in range(8)])
+            wide, out = vn(bk, (0, PL), (0, 64)), vn(pd, (PL * nh, PL * nh + PL), (0, 8), (j0, 16, 2))
+            if how == "v" and nh == 0:
+                tt(wide, v(vg, j0, 1024, 2), wide, A.mult)
+                kept[j0] = wide
+                continue
+            tt(out, v(vg, 1024 * nh + j0, 1024 * nh + 1024, 2), wide, A.mult)
+            if how == "v":
+                tt(out, out, kept[j0], A.add)
+            if how != "d":
+                end = h % 2 and x and nh and j0
+                mms([(v("ps_a", LN * (1 - x) + j0, LN * (2 - x), 2), IDF, vn(pd, (PL * nh, PL * nh + PL), n, (j0, 16, 2)), False, bool(end and n == 7)) for n in range(8)])
+        if how == "d":
+            s = dsem()
+            o, i = vn(pd, (0, PL), (0, 8), (0, 16)), vn(pd, (PL, 2 * PL), (0, 8), (0, 16))
+            rec("G", lambda q: q.dma_start(ap(o), ap(i), accum_op=A.add).then_inc(T.sem[s], 16), [o], [o, i], OPT["gi"], s, 16, OPT["dl"] + 2 ** 20 / OPT["db"])
+            for n in range(0, 8, 2):
+                mms([(acc, IDF, vn(pd, (0, PL), m, (0, 16)), False, h == 1 and x == 1 and m == 7) for m in (n, n + 1)])
+            if h % 2 and x and t:
+                mms([(PA, v("idf", 128 - 16 * t, 256 - 16 * t), v("la%d" % (t - 1), 0, L), False, True)])
 
     def report(t):
         y = v("yy", L * t, L * t + L)
         if t < NV - 1:
             act(v("as%d" % t, 0, L), PA, F.Copy)
-            move(v("la%d" % t, 0, L), v("as%d" % t, 0, L), 3 * t + 2, 512 * L)
-        tt(y, v("vg%d" % ((2 * t + 1) % NG), W, W + L), PA, A.add)
+            move(v("la%d" % t, 0, L), v("as%d" % t, 0, L), 512 * L)
+        tt(y, v("yr", 0, L), PA, A.add)
         store(T.ya[:, L * t:L * t + L], y)
 
-    def hold(lt, x):
-        mm(PQ, lt, x, True, True)
-        mm(v("ps_q", L, 2 * L), lt, x, True, True)
-
-    act(qA, ind(KT, v("cl1", 0, 16)), F.Copy)
-    hold(IDB, qA)
-    src, plus = v("sti", 0, 16), 0.0
     for h in range(2 * NV):
-        t, first, last = h // 2, h % 2 == 0, h == 2 * NV - 1
-        cutv, hop[0] = t < NV - 1, h
-        ln, wb, wh, wl, vg = "ln%d" % (h % 2), "wb%d" % (h % 2), "wh%d" % (h % 2), "wl%d" % (h % 2), "vg%d" % (h % NG)
-        q = qA if first else qB
-        one = v(src[0], src[1], src[1] + 1)
-        if h == 0:
-            cp(v("cl", 0, 16), src)
-            cp(v("cl", 16, 17), one)
-        else:
-            ts(v("cl", 0, 16), src, plus, A.add)
-            ts(v("cl", 16, 17), one, plus, A.add)
-        if first and h:
-            cp(v("d1", 0, 272, 17), v("ps_m", 16, 32))
-        if first and cutv:
-            cp(v("came", 0, 16), src)
-        cp(v("nm", 0, 272), ind(PG, v("cl", 0, 17)))
-        tag["nm", h] = len(ops) - 1
-        turn(v("tt", 0, 256), v("nm", 0, 256))
-        turn(v("tt", 256, 512), v("nm", 16, 272))
-        cp(v(ln, 0, L), ind(v("tt", 0, 512), v("li", 0, 16)))
-        if first and h:
-            hold(v("idb", 128 - 16 * t, 256 - 16 * t), v("lq%d" % (t - 1), 0, L))
-            act(qA, PQ, F.Copy)
-        if first and cutv:
-            act(v("cex", 0, L), ind(v("came", 0, 16), v("le", 0, 16)), F.Identity, 1.0)
-            act(v("nm0", 0, L), v("nm", 0, L), F.Identity, cM15)
-            ts(tC1, v("came", 0, 16), 1.0, A.add, 1 / BIG, A.mult)
-            ts(tC2, v("came", 0, 16), cD, A.subtract, 1 / (BIG * BIG), A.mult)
-        nf = OPT["NF"][h]
-        for i in range(nf):
-            tt(v("pr", 256 * i, 256 * i + 256), ind(KT, v(ln, 16 * i, 16 * i + 16)), q, A.mult)
-        for j in range(nf + 2 - nf % 2, 17, 2):
-            i = max(nf, j - 2)
-            x = v("pr", 256 * i, 256 * j)
-            act(x, ind(KT, v(ln, 16 * i, 16 * j)), F.Copy)
-            tt(x, x, v("ps_q", 0, 256 * (j - i)), A.mult)
-        for a in range(4):
-            for jj in range(16):
-                mm(v("ps_s", 64 * a, 64 * a + 64), v("wd", 15 - jj, 143 - jj), v("pr", 1024 * a + jj, 1024 * a + 1024, 16), jj == 0, jj == 15)
-        act(v("aw", 16, 272), v("ps_s", 0, 256), F.Relu, 1.625)
-        RS = v("ps_r", 0, 272)
-        if OPT["FS"][h] == "1":
-            act(v("be", 0, 272), ind(v("aw", 0, 272), v("lf", 0, 17)), F.Relu, 15 / 16.0, -1.0)
-            act(v("ff", 0, 272), v("be", 0, 272), F.Identity, 1.0, -1.0)
-        else:
-            ts(v("ff", 0, 272), ind(v("aw", 0, 272), v("lf", 0, 17)), 15 / 16.0, A.min, 1 / 16.0, A.add)
-            act(v("be", 0, 272), v("ff", 0, 272), F.Identity, 1.0, -1.0)
-        scan(RS, v("ff", 0, 272), v("d1", 0, 272), A.mult, A.add)
-        tag["scan", h] = len(ops) - 1
-        ts(v("xx", 0, 272), RS, 1 / 16.0, A.is_ge, BIG, A.mult)
-        R16, X16, C15 = v("ps_r", 16, 272, 17), v("xx", 16, 272, 17), v("cs", 15, 272, 17)
-        ts(tB, R16, 1 / 16.0, A.is_lt)
-        tt(v("dn", 0, 272), ind(v("tt", 0, 544), v("lx" if first else "lx1", 0, 17)), v("xx", 0, 272), A.subtract)
-        rn = v("d1", 0, 272, 17) if first else (tR if last else v("sb%d" % t, 32, 48))
-        tt(rn, tB, R16, A.max)
-        scan(v("cs", 0, 272), v("xx", 0, 272), v("dn", 0, 272), A.add, A.min)
-        if first:
-            ts(v("ql", 0, 16), v("cs", 16, 272, 17), BIG, A.add)
-            act(qB, ind(v("kq", 0, W + L), v("ql", 0, 16)), F.Copy)
-            hold(IDB, qB)
-            if cutv:
-                tt(tP1, tC1, X16, A.mult)
-                tt(tP2, tC2, X16, A.mult)
-            src, plus = C15, BIG
-        elif not last:
-            sb = "sb%d" % t
-            ts(v(sb, 16, 32), C15, BIG, A.add)
-            move(v("lc%d" % t, 0, 32), v(sb, 16, 48), 3 * t, 128 * 128)
-            ts(v("ql", 0, 16), v("cs", 16, 272, 17), BIG, A.add)
-            act(v("qs%d" % t, 0, L), ind(v("kq", 0, W + 2 * L), v("ql", 0, 16)), F.Copy)
-            move(v("lq%d" % t, 0, L), v("qs%d" % t, 0, L), 3 * t + 1, 256 * L)
-            tt(v(sb, 0, 16), tB, tP1, A.mult)
-            cp(v("xh", 0, 32), v(sb, 0, 32))
-            tt(v("xl", 0, 32), v(sb, 0, 32), v("xh", 0, 32), A.subtract)
-            mm(v("ps_m", 0, 512), IDB, v("cc", 0, 512), True, False)
-            for jj in range(16):
-                o, s = v("ps_m", jj, 512, 16), v("sel", 128 * jj, 128 * jj + 128)
-                mm(o, s, v("xh", 0, 32), False, False)
-                mm(o, s, v("xl", 0, 32), False, jj == 15)
-            tt(tY, tB, tP2, A.mult)
-            ts(tA, tY, cD8, A.add)
-            tt(v("eq", 0, L), v("cex", 0, L), v("ps_m", 0, L), A.is_equal)
-            tt(v("val", 0, L), v("nm0", 0, L), v("ps_m", L, 2 * L), A.max)
-            scan(v("cnt", 0, L), v("rm", 0, L), v("eq", 0, L), A.mult, A.add)
-            mm(v("ps_m", 0, 32), v("idf", 112 - 16 * t, 240 - 16 * t), v("lc%d" % t, 0, 32), True, True)
-            tt(tZ, v("cnt", 15, L, 16), tA, A.add)
-            ts(v("so", 0, 32, 2), tZ, cD8, A.min, BIG, A.mult)
-            for pl in range(15, -1, -1):
-                cp(ind(PG, v("so", 2 * pl, 2 * pl + 1)), v("val", 16 * pl, 16 * pl + 16))
-            src, plus = v("ps_m", 0, 16), 0.0
-        tt(v("ps_r", 0, 271), v("be", 1, 272), v("ps_r", 0, 271), A.mult)
-        tt(v(wb, 0, 271), v("xx", 0, 271), v("ps_r", 0, 271), A.min)
-        n = 16
-        if not first:
-            n = 17
-            cp(v(wb, 16, 272, 17), rn)
-            ts(v("cl1", 0, 16), C15, BIG, A.add)
-        act(v(wh, 0, 16 * n), ind(v(wb, 0, 272), v("lw", 0, n)), F.Copy)
-        tt(v(wl, 0, 16 * n), ind(v(wb, 0, 272), v("lw", 0, n)), v(wh, 0, 16 * n), A.subtract)
-        for a in range(0, 16, OPT["VS"]):
-            b = a + OPT["VS"]
-            act(v(vg, 256 * a, 256 * b), ind(v("vs", 0, W), v(ln, 16 * a, 16 * b)), F.Sigmoid)
-        if not first:
-            act(v(vg, W, W + L), ind(v("vs", 0, W), v("cl1", 0, 16)), F.Sigmoid)
-        if last:
-            last_products(h)
-        else:
-            products(h)
-        if not first:
-            report(t)
+        for x in range(2):
+            chain(h, x)
+        if h % 2 and h < 2 * NV - 1:
+            for x in range(2):
+                shortcuts(x)
+        for x in range(2):
+            values(h, x)
+        if h % 2:
+            report(h // 2)
     key = (n_out, n_in)
     if key not in ORDER:
-        pace = [(tag[a, h], tag[b, h + d]) for a, b, d, hs in OPT["pace"] for h in hs if (a, h) in tag and (b, h + d) in tag]
-        ORDER[key] = schedule(ops, pace)
+        ORDER[key] = schedule(ops)
     emit(g, T, [ops[i] for i in ORDER[key]])

@@ -4,12 +4,12 @@ from concourse.mybir import AluOpType, ActivationFunctionType
 W, L, NV = 4096, 256, 4
 BIG, TOP = 8192.0, 4112.0
 PL, LN, SL = 8, 128, 136
-KO = 2 * LN
 NB, NG, NW = 3, 4, 3
-OPT = {"CH": [("V", 24), ("S", 52), ("S", 52)], "N17": "V", "VS": 1024, "cy": 0.83, "ga": 1.56, "sc": 3.8, "pe": 0.42, "sem": 150, "dl": 2200,
-       "db": 250.0, "vo": 10, "so": 65, "rl": 4000, "rb": 60.0, "gi": 1000, "rounds": 1500, "seed": 1, "amp": 100.0, "drift": 1.004,
-       "moves": 4, "far": 3000.0, "SUM": "dddddddddddddddv"}
-SCALES = [{}, {"ga": 0.72, "sc": 0.7}, {"ga": 1.3, "sc": 1.3}, {"pe": 1.4, "sem": 1.6}, {"dma": 1.5, "rem": 1.4}, {"dma": 0.7, "rem": 0.7, "sem": 0.5}]
+OPT = {"CH": [("V", 28), ("S", 52), ("S", 48)], "N17": "V", "VS": 1024, "cy": 0.83, "ga": 1.56, "sc": 3.8, "pe": 0.42, "sem": 150, "dl": 2200,
+       "db": 250.0, "vo": 10, "so": 65, "rl": 4000, "rb": 60.0, "gi": 1000, "rounds": 40,
+       "SUM": "ddddddddddddddvv"}
+SCALES = [{}, {"ga": 0.7, "sc": 0.6}, {"ga": 1.3, "sc": 1.4}, {"dma": 0.75, "rem": 0.75, "sem": 0.75}, {"dma": 1.3, "rem": 1.4, "sem": 1.5},
+          {"ga": 1.3, "dma": 0.7, "rem": 0.7, "sem": 0.7}]
 
 SCRATCH = {
     "bpk": ("sbuf", [128, W // 2], "int32"), "pg": ("sbuf", [128, W + 16], "int32"),
@@ -22,7 +22,7 @@ SCRATCH = {
     "lx0": ("sbuf", [128, 10], "uint16"), "lx1": ("sbuf", [128, 10], "uint16"),
     "idf": ("sbuf", [128, 256], "float32"), "idb": ("sbuf", [128, 256], "bfloat16"),
     "back": ("sbuf", [128, 256], "float32"), "fore": ("sbuf", [128, 128], "float32"), "roll": ("sbuf", [128, 16, 16], "float32"),
-    "on": ("sbuf", [128, 128 * (NV - 1)], "float32"), "sel": ("sbuf", [128, 1024], "bfloat16"), "cc": ("sbuf", [128, 3 * LN], "bfloat16"),
+    "nid": ("sbuf", [128, 128], "bfloat16"), "on": ("sbuf", [128, 128 * (NV - 1)], "float32"), "sel": ("sbuf", [128, 1024], "bfloat16"), "cc": ("sbuf", [128, 3 * LN], "bfloat16"),
     "kc": ("sbuf", [128, SL], "bfloat16"), "zz": ("sbuf", [128, L], "bfloat16"),
     "ps_a": ("psum", [128, 512], "float32"),
 }
@@ -37,9 +37,9 @@ for _t in range(NV - 1):
 for _x in range(2):
     SCRATCH["ps_m%d" % _x] = ("psum", [128, 512], "float32")
     SCRATCH["ps_s%d" % _x] = ("psum", [128, 512], "float32")
-    for _n, _c, _d in [("cl", PL, "uint16"), ("c1", PL, "uint16"), ("ql", PL, "uint16"), ("ln", LN, "uint16"), ("so", 2 * PL, "uint16"),
+    for _n, _c, _d in [("c0", 2 * PL, "uint16"), ("c1", 2 * PL, "uint16"), ("ln", LN, "uint16"), ("so", 2 * PL, "uint16"),
                        ("nm", LN + 16, "float32"), ("tt", 2 * LN + 32, "float32"), ("kr", 16 * LN, "bfloat16"), ("zq", 32 * LN, "bfloat16"),
-                       ("ff", SL, "float32"), ("be", SL, "float32"), ("d1", SL, "float32"), ("xx", SL, "float32"), ("dn", SL, "float32"),
+                       ("ff", SL, "float32"), ("be", SL, "float32"), ("d1", SL, "float32"), ("xx", SL, "bfloat16"),
                        ("ns", 144, "float32"), ("cs", SL, "float32"), ("ty", 4 * PL, "float32"), ("cex", LN, "float32"), ("nm0", LN, "float32"),
                        ("eq", LN, "float32"), ("cnt", LN, "float32"), ("val", LN, "int32"), ("vr", LN, "float32"),
                        ("xa", 3 * PL, "bfloat16"), ("xb", 3 * PL, "bfloat16")]:
@@ -100,16 +100,16 @@ def meets(ops):
         for b, m, wr in acc:
             h = hist.setdefault(b, [])
             if b.startswith("ps_"):
-                if h and h[0][0] != i and (ops[h[0][0]]["st"] != o["st"] or o["st"] == "P"):
+                if h and h[0][0] != i and (ops[h[0][0]]["st"] != o["st"] or (o["st"] == "P" and not o.get("adds"))):
                     before[b] = [e[0] for e in h]
                     h[:] = []
                 deps.update(before.get(b, []))
             for j, mj, wj in h:
-                if (m & mj) and (wr or wj):
+                if (m & mj) and (wr or wj) and not (wr and o.get("adds") and ops[j].get("adds")):
                     deps.add(j)
         for b, m, wr in acc:
             h = hist[b]
-            if wr:
+            if wr and not o.get("adds"):
                 h[:] = [e for e in h if (e[1] & ~m) or e[0] == i]
             h.append((i, m, wr))
         out.append({j: not o["st"] == ops[j]["st"] == "P" for j in deps if j != i})
@@ -128,27 +128,35 @@ def schedule(ops):
             succ[j].append(i)
     c, lat = [o["c"] for o in ops], [o["lat"] for o in ops]
     gap = lambda j, i: OPT["sem"] if deps[i][j] and ops[i]["e"] is not None else 0
-    fore = [[(j, lat[j] + gap(j, i)) for j in deps[i]] for i in range(n)]
-    aft = [[(k, c[k] + lat[i] - c[i] + gap(i, k)) for k in succ[i]] for i in range(n)]
+    fore = [[(k, lat[i] + gap(i, k)) for k in succ[i]] for i in range(n)]
+    aft = [[(j, c[i] + lat[j] - c[j] + gap(j, i)) for j in deps[i]] for i in range(n)]
 
     def place(order, back):
-        at, busy = [0.0] * n, {e: [] for e in "VSPGY"}
-        for i in order:
-            t = max([at[k] + d for k, d in (aft[i] if back else fore[i])] + [lat[i] - c[i] if back else 0.0])
-            if ops[i]["e"] is not None:
-                b = busy[ops[i]["e"]]
-                lo, hi = 0, len(b)
-                while lo < hi:
-                    mid = (lo + hi) // 2
-                    if b[mid][1] <= t:
-                        lo = mid + 1
-                    else:
-                        hi = mid
-                while lo < len(b) and b[lo][0] < t + c[i]:
-                    t = max(t, b[lo][1])
-                    lo += 1
-                b.insert(lo, (t, t + c[i]))
+        left = [len(succ[i] if back else deps[i]) for i in range(n)]
+        due = [lat[i] - c[i] if back else 0.0 for i in range(n)]
+        at, free, ready = [0.0] * n, {e: 0.0 for e in "VSPGY"}, {e: [] for e in "VSPGY"}
+
+        def start(i, t):
             at[i] = t
+            for k, d in (aft[i] if back else fore[i]):
+                due[k] = max(due[k], t + d)
+                left[k] -= 1
+                if left[k] == 0:
+                    arrive(k)
+
+        def arrive(k):
+            if ops[k]["e"] is None:
+                start(k, due[k])
+            else:
+                ready[ops[k]["e"]].append(k)
+        for i in [i for i in range(n) if left[i] == 0]:
+            arrive(i)
+        while any(ready.values()):
+            t, e = min((max(free[e], min(due[k] for k in r)), e) for e, r in ready.items() if r)
+            i = min((k for k in ready[e] if due[k] <= t), key=lambda k: order[k])
+            ready[e].remove(i)
+            free[e] = t + c[i]
+            start(i, t)
         return at
 
     hard = [[(j, gap(j, i) > 0) for j in deps[i]] for i in range(n)]
@@ -164,34 +172,18 @@ def schedule(ops):
                 free[o["e"]] = t + c[i] * k
         return max(end)
 
-    state, groups = [OPT["seed"]], sorted(set(o["grp"] for o in ops))
-
-    def draw():
-        state[0] = (state[0] * 1103515245 + 12345) % 2 ** 31
-        return state[0] / 2 ** 31
-
-    def shaken(key, amp, back):
-        out, moved = list(key), {}
-        for _ in range(OPT["moves"]):
-            moved[groups[int(draw() * len(groups))]] = OPT["far"] * (2 * draw() - 1)
-        for i in (range(n - 1, -1, -1) if back else range(n)):
-            out[i] = max([key[i] + amp * draw() + moved.get(ops[i]["grp"], 0.0)] + [out[j] for j in (succ[i] if back else deps[i])])
-        return out
-
-    at = place(range(n), False)
-    best = None
+    tail = [0.0] * n
+    for i in range(n - 1, -1, -1):
+        tail[i] = max([tail[k] + d for k, d in fore[i]] + [lat[i]])
+    at, best = place([-x for x in tail], False), None
     for r in range(OPT["rounds"]):
-        key = shaken([-at[i] - c[i] for i in range(n)], OPT["amp"], True)
-        u = place(sorted(range(n), key=lambda i: (key[i], -i)), True)
-        key = shaken([-u[i] - c[i] for i in range(n)], OPT["amp"], False)
-        new = place(sorted(range(n), key=lambda i: (key[i], i)), False)
-        order = sorted(range(n), key=lambda i: (-1.0 if ops[i].get("load") else new[i], i))
+        u = place([-at[i] - c[i] for i in range(n)], True)
+        at = place([-u[i] - c[i] for i in range(n)], False)
+        order = sorted(range(n), key=lambda i: (-1.0 if ops[i].get("load") else at[i], i))
         ends = [replay(order, s) for s in SCALES]
-        end = sum(ends) / len(ends)
-        if best is None or end < best[0]:
-            best = (end, order, new, ends)
-        at = new if end < best[0] * OPT["drift"] else best[2]
-    ORDER["end"] = (best[0], best[3])
+        if best is None or sum(ends) < best[0]:
+            best = (sum(ends), order, ends)
+    ORDER["end"] = (best[0] / len(SCALES), best[2])
     return best[1]
 
 
@@ -311,13 +303,14 @@ def rank_program(g, core, T, topo):
         else:
             rec("S", lambda q: q.activation(ap(o), ap(i), fn, bias=num(bias), scale=1.0 if scale is None else scale), [o], [i, bias], c)
 
-    def mms(calls):
+    def mms(calls, adds=False):
         def f(q):
             for o, lt, r, start, stop in calls:
                 ins = q.matmul(ap(o), ap(lt), ap(r), start, stop)
             return ins
         rec("P", f, list(dict.fromkeys(x[0][1] if x[0][0] == "^" else x[0] for x in calls)), list(dict.fromkeys([x[1] for x in calls] + [x[2] for x in calls])),
             sum(max(min(64, cols(x[1])), cols(x[2])) * OPT["pe"] * (4 if SCRATCH[x[1][0]][2] == "float32" else 1) for x in calls))
+        ops[-1]["adds"] = adds
 
     def dsem():
         nd[0] += 1
@@ -344,7 +337,7 @@ def rank_program(g, core, T, topo):
     pc = W // 2 // NP
     for k in range(NP):
         load("Y", v("bpk", k * pc, (k + 1) * pc), T.bp[:, k * pc:(k + 1) * pc], 512 * pc)
-    load("Y", v("kq", KO, KO + W), T.kt[:], 256 * W)
+    load("Y", v("kq", 0, W), T.kt[:], 256 * W)
     load("Y", v("vs", 0, W), T.vt[:], 256 * W)
 
     def iota(o, pat, base, cm, flag):
@@ -424,19 +417,19 @@ def rank_program(g, core, T, topo):
     ts(v("cc", 0, LN), v("jj", 0, LN), cR, A.is_ge, -BIG, A.mult)
     act(v("cc", LN, 2 * LN), v("jj", 0, LN), F.Identity, cN15, 0.0)
     act(v("rm", 0, LN), v("jj", 0, LN), F.Sign)
-    QW = [[(LN, LN + W), (0, KO + W)], [(KO, W + LN), (KO, W + 2 * LN)]]
-    QA, QB = [v("kq", LN, KO), v("kq", KO + W, KO + W + LN)], [v("kq", 0, LN), v("kq", KO + W + LN, KO + W + 2 * LN)]
+    act(v("nid", 0, 128), v("idf", 0, 128), F.Identity, 0.0, -1.0)
+    QA, QB = [[v("kq", W + LN * (2 * x + k), W + LN * (2 * x + k + 1)) for x in range(2)] for k in range(2)]
     for x in range(2):
         fill(v("d1_%d" % x, 0, SL), 0.0)
         fill(v("d1_%d" % x, 0, SL, 17), 1.0)
         fill(v("ps_s%d" % x, 3 * SL - 1, 3 * SL), 0.0)
         for k, own in enumerate((QA[x], QB[x])):
-            ts(v("tt_%d" % x, 2 * LN + 16 * k, 2 * LN + 16 * k + 9), tE, float(own[1][0] - KO), A.add)
+            ts(v("tt_%d" % x, 2 * LN + 16 * k, 2 * LN + 16 * k + 9), tE, float(own[1][0]), A.add)
     for k in range(NP):
         ts(v("pg", k * pc, (k + 1) * pc), v("bpk", k * pc, (k + 1) * pc), W - 1, A.bitwise_and)
         ts(v("pg", W // 2 + k * pc, W // 2 + (k + 1) * pc), v("bpk", k * pc, (k + 1) * pc), 12, A.logical_shift_right)
 
-    KT, PG, VS = v("kq", KO, KO + W), v("pg", 0, W + 16), v("vs", 0, W)
+    KT, PG, VS = v("kq", 0, W), v("pg", 0, W + 16), v("vs", 0, W)
     IDF, IDB, BACK, FORE, PA = v("idf", 0, 128), v("idb", 0, 128), v("back", 0, 128), v("fore", 0, 128), v("ps_a", 0, L)
     bank = [0]
 
@@ -446,6 +439,7 @@ def rank_program(g, core, T, topo):
                 act(rows(z, p, p + 64), rows(src, p, p + 64), F.Copy)
             else:
                 cp(rows(z, p, p + 64), rows(src, p, p + 64))
+        for p, z in ((0, a), (64, b)):
             tt(rows(z, 64 - p, 128 - p), rows(src, p, p + 64), rows(z, p, p + 64), A.subtract)
 
     def chain(h, x):
@@ -456,7 +450,7 @@ def rank_program(g, core, T, topo):
         ps = lambda a, e, s=1: v("ps_s%d" % x, a, e, s)
         pm = lambda a, e, s=1: v("ps_m%d" % x, a, e, s)
         came, camp, tB, tP = [b("ty", PL * k, PL * k + PL) for k in range(4)]
-        cl, tw, zq, e0 = b("cl", 0, PL), b("tt", 0, 2 * LN + 32), ind(b("zq", 0, 32 * LN), v("lz", 0, PL)), 3 * SL
+        cl, tw, zq, e0 = b("c0", 0, PL), b("tt", 0, 2 * LN + 32), ind(b("zq", 0, 32 * LN), v("lz", 0, PL)), 3 * SL
         if h == 0:
             cp(cl, v("sti", p0, p0 + PL))
             ts(came, v("sti", p0, p0 + PL), -1.0, A.mult, TOP, A.add)
@@ -498,7 +492,7 @@ def rank_program(g, core, T, topo):
             cp(b("ns", 0, 144), ind(tw, v("lx%d" % (h % 2), 0, 9)))
         else:
             act(b("ns", 0, 144), ind(tw, v("lx%d" % (h % 2), 0, 9)), F.Copy)
-        mms([(pm(0, SL), FORE, b("ns", 0, SL), True, True)])
+        mms([(pm(0, SL), FORE, b("ns", 0, SL), True, False)])
         cp(b("lv", LN * k, LN * k + LN), ind(tw, v("li", 0, 8)))
         if first and cutv:
             act(b("cex", 0, LN), ind(came, v("le", 0, 8)), F.Copy)
@@ -509,10 +503,9 @@ def rank_program(g, core, T, topo):
         act(b("be", 0, SL), b("ff", 0, SL), F.Identity, 1.0, -1.0)
         ts(b("xx", 0, SL), RS, 1 / 16.0, A.is_ge, BIG, A.mult)
         R16, X16, C15 = ps(SL + 16, 2 * SL, 17), b("xx", 16, SL, 17), b("cs", 15, SL, 17)
-        tt(b("dn", 0, SL), pm(0, SL), b("xx", 0, SL), A.subtract)
-        scan(b("cs", 0, SL), b("xx", 0, SL), b("dn", 0, SL), A.add, A.min)
-        s0, m0 = 3 * PL * t, 3 * LN
-        w0, wn = QW[x][h % 2]
+        mms([(pm(0, SL), v("nid", 0, 128), b("xx", 0, SL), False, True)])
+        scan(b("cs", 0, SL), b("xx", 0, SL), pm(0, SL), A.add, A.min)
+        s0, m0, cq, n = 3 * PL * t, 3 * LN, "c%d" % (h % 2), PL if last else 2 * PL
         mms([(pm(m0, m0 + PL), BACK, C15, True, True)] + ([] if last else [(pm(m0 + PL, m0 + 2 * PL), BACK, b("cs", 16, SL, 17), True, True)]))
         if not first and cutv:
             ts(b("sb", s0 + PL, s0 + 2 * PL), C15, BIG, A.add)
@@ -520,10 +513,9 @@ def rank_program(g, core, T, topo):
         tt(b("d1", 0, SL, 17) if first else b("sb", s0 + 2 * PL, s0 + 3 * PL), tB, R16, A.max)
         if not first and cutv:
             move(b("lc", 2 * PL * t, 2 * PL * (t + 1)), b("sb", s0 + PL, s0 + 3 * PL), 128 * 64)
-        ts(cl if first else b("c1", 0, PL), pm(m0, m0 + PL), BIG, A.add)
+        ts(b(cq, 0, n), pm(m0, m0 + n), BIG, A.add)
         if not last:
-            ts(b("ql", 0, PL), pm(m0 + PL, m0 + 2 * PL), BIG + KO - w0, A.add)
-            act(QB[x] if first else b("qs", LN * t, LN * t + LN), ind(v("kq", w0, w0 + wn), b("ql", 0, PL)), F.Copy)
+            act(QB[x] if first else b("qs", LN * t, LN * t + LN), ind(v("kq", 0, (QA if first else QB)[x][1][1]), b(cq, PL, 2 * PL)), F.Copy)
         if first:
             cp(zq, QB[x])
             if cutv:
@@ -565,8 +557,9 @@ def rank_program(g, core, T, topo):
             act(v(vg, a, a + OPT["VS"]), ind(VS, v("lv_%d" % x, LN * k + a // 16, LN * k + (a + OPT["VS"]) // 16)), F.Sigmoid)
         if h % 2 == 0 and x == 0:
             mms([(PA, IDB, v("zz", 0, L), True, False)])
-        if h % 2 and x and t and how != "d":
-            mms([(PA, v("idf", 128 - 16 * t, 256 - 16 * t), v("la%d" % (t - 1), 0, L), False, False)])
+        closes = h % 2 and x and not (t and how == "d")
+        if closes and t:
+            mms([(PA, v("idf", 128 - 16 * t, 256 - 16 * t), v("la%d" % (t - 1), 0, L), False, False)], True)
         kept = {}
         for nh, j0 in ([(0, 0), (1, 0), (0, 1), (1, 1)] if how == "v" else [(0, 0), (0, 1), (1, 0), (1, 1)]):
             bk = "ps_w%d" % (bank[0] % NB)
@@ -582,14 +575,14 @@ def rank_program(g, core, T, topo):
             if how == "v":
                 tt(out, out, kept[j0], A.add)
             if how != "d":
-                end = h % 2 and x and nh and j0
-                mms([(v("ps_a", LN * (1 - x) + j0, LN * (2 - x), 2), IDF, vn(pd, (PL * nh, PL * nh + PL), n, (j0, 16, 2)), False, bool(end and n == 7)) for n in range(8)])
+                end = bool(closes and nh and j0)
+                mms([(v("ps_a", LN * (1 - x) + j0, LN * (2 - x), 2), IDF, vn(pd, (PL * nh, PL * nh + PL), n, (j0, 16, 2)), False, end and n == 7) for n in range(8)], not end)
         if how == "d":
             s = dsem()
             o, i = vn(pd, (0, PL), (0, 8), (0, 16)), vn(pd, (PL, 2 * PL), (0, 8), (0, 16))
             rec("G", lambda q: q.dma_start(ap(o), ap(i), accum_op=A.add).then_inc(T.sem[s], 16), [o], [o, i], OPT["gi"], s, 16, OPT["dl"] + 2 ** 20 / OPT["db"])
             for n in range(0, 8, 2):
-                mms([(acc, IDF, vn(pd, (0, PL), m, (0, 16)), False, h == 1 and x == 1 and m == 7) for m in (n, n + 1)])
+                mms([(acc, IDF, vn(pd, (0, PL), m, (0, 16)), False, bool(closes and m == 7)) for m in (n, n + 1)], not (closes and n == 6))
             if h % 2 and x and t:
                 mms([(PA, v("idf", 128 - 16 * t, 256 - 16 * t), v("la%d" % (t - 1), 0, L), False, True)])
 

@@ -4,54 +4,65 @@ from concourse.mybir import AluOpType, ActivationFunctionType
 W, L, NV = 4096, 256, 4
 BIG, TOP = 8192.0, 4112.0
 PL, LN, SL = 8, 128, 136
-NB, NG, NW = 3, 4, 3
-OPT = {"CH": [("V", 28), ("S", 52), ("S", 48)], "N17": "V", "VS": 1024, "cy": 0.83, "ga": 1.56, "sc": 3.8, "pe": 0.42, "sem": 150, "dl": 2200,
-       "db": 250.0, "vo": 10, "so": 65, "rl": 4000, "rb": 60.0, "gi": 1000, "rounds": 40,
-       "SUM": "ddddddddddddddvv"}
-SCALES = [{}, {"ga": 0.7, "sc": 0.6}, {"ga": 1.3, "sc": 1.4}, {"dma": 0.75, "rem": 0.75, "sem": 0.75}, {"dma": 1.3, "rem": 1.4, "sem": 1.5},
-          {"ga": 1.3, "dma": 0.7, "rem": 0.7, "sem": 0.7}]
+NB, NG, ND, NR, NW = 3, 6, 6, 4, 3
+OPT = {"CH": [("S", 44), ("S", 44), ("S", 40)], "VS": 512, "cy": 0.83, "ga": 1.56, "sc": 3.8, "pe": 0.42, "sem": 150, "dl": 2200,
+       "db": 500.0, "vo": 10, "so": 65, "rl": 4000, "rb": 60.0, "gi": 1200, "rounds": 10,
+       "SUM": "ddddddddaaggaauu", "E": "SVSSSVSSS", "BASE": {}, "shy": 0, "shake": 100, "back": 3,
+       "ab": 0, "mend": 0, "slack": 0, "inorder": 0, "CV": [44, 44, 40, 40, 36, 36, 32, 36],
+       "WR": "0000000000000000", "SG": 1024, "yi": 100, "margin": 1000, "piece": 1000, "LAG": [0] * 8, "sgs": 0, "fl": 7500, "yl": 3000,
+       "WAIT": [(0, 0, 0), (100, 500, 30), (200, 1000, 30), (100, 300, 30)] * 12}
+SCALES = [{"of": of, "": f, "pe": f, "ga": f * ga, "sc": f * sc, "dma": d, "rem": d, "sem": d}
+          for of, f, ga, sc, d in [(1.16, 1.0, 1.0, 1.0, 1.0), (1.64, 1.25, 1.25, 1.0, 1.0), (1.34, 1.25, 0.75, 1.0, 1.0), (1.6, 1.4, 1.0, 1.3, 1.0),
+                                   (1.41, 1.1, 1.15, 0.7, 1.4), (1.16, 1.1, 0.7, 0.8, 0.75)]]
+OLD = True
 
 SCRATCH = {
     "bpk": ("sbuf", [128, W // 2], "int32"), "pg": ("sbuf", [128, W + 16], "int32"),
     "kq": ("sbuf", [128, W + 4 * LN], "bfloat16"), "vs": ("sbuf", [128, W], "bfloat16"),
-    "sti": ("sbuf", [128, 16], "int32"), "yr": ("sbuf", [128, L], "float32"), "yy": ("sbuf", [128, NV * L], "float32"),
-    "pi": ("sbuf", [128, 8], "int32"), "pf": ("sbuf", [128, 20], "float32"), "ti": ("sbuf", [128, 80], "int32"),
+    "sti": ("sbuf", [128, 16], "int32"), "yy": ("sbuf", [128, NV * L], "float32"),
+    "pi": ("sbuf", [128, 12], "int32"), "pf": ("sbuf", [128, 20], "float32"),
     "io": ("sbuf", [128, 256], "float32"), "jj": ("sbuf", [128, LN], "float32"), "rm": ("sbuf", [128, LN], "float32"),
-    "tw": ("sbuf", [128, 200], "float32"),
-    "li": ("sbuf", [128, 8], "uint16"), "le": ("sbuf", [128, 8], "uint16"), "lz": ("sbuf", [128, 8], "uint16"),
-    "lx0": ("sbuf", [128, 10], "uint16"), "lx1": ("sbuf", [128, 10], "uint16"),
+    "le": ("sbuf", [128, 8], "uint16"), "lz": ("sbuf", [128, 8], "uint16"),
+    "nsel": ("sbuf", [128, 2, 160], "float16"), "f16": ("sbuf", [128, 128], "float16"), "hsel": ("sbuf", [128, 2, 144], "float16"),
+    "zf": ("sbuf", [128, 512], "float32"),
+    "sg": ("sbuf", [128, W], "float32"), "lp": ("sbuf", [128, 16], "uint16"), "yr": ("sbuf", [128, NV * L], "float32"), "ac": ("sbuf", [128, NV * L], "float32"),
     "idf": ("sbuf", [128, 256], "float32"), "idb": ("sbuf", [128, 256], "bfloat16"),
-    "back": ("sbuf", [128, 256], "float32"), "fore": ("sbuf", [128, 128], "float32"), "roll": ("sbuf", [128, 16, 16], "float32"),
-    "nid": ("sbuf", [128, 128], "bfloat16"), "on": ("sbuf", [128, 128 * (NV - 1)], "float32"), "sel": ("sbuf", [128, 1024], "bfloat16"), "cc": ("sbuf", [128, 3 * LN], "bfloat16"),
-    "kc": ("sbuf", [128, SL], "bfloat16"), "zz": ("sbuf", [128, L], "bfloat16"),
+    "back": ("sbuf", [128, 256], "float32"), "fore": ("sbuf", [128, 128], "float32"), "roll": ("sbuf", [128, 4, 64], "float32"),
+    "nid": ("sbuf", [128, 128], "float16"), "on": ("sbuf", [128, 128 * (NV - 1)], "float32"), "sel": ("sbuf", [128, 1024], "bfloat16"), "cc": ("sbuf", [128, 3 * LN], "bfloat16"),
+    "kc": ("sbuf", [128, 2 * SL], "float16"), "zz": ("sbuf", [128, L], "bfloat16"),
     "ps_a": ("psum", [128, 512], "float32"),
 }
 for _k in range(NB):
-    SCRATCH["ps_w%d" % _k] = ("psum", [128, PL, 64], "float32")
+    SCRATCH["ps_w%d" % _k] = ("psum", [128, 512], "float32")
+if NB < 3:
+    SCRATCH["ps_x"] = ("psum", [128, 30, 17], "float32")
 for _k in range(NG):
-    SCRATCH["vg%d" % _k] = ("sbuf", [128, 16 * LN], "float32")
-    SCRATCH["pd%d" % _k] = ("sbuf", [128, 2 * PL, 8, 16], "float32")
+    SCRATCH["vg%d" % _k] = ("sbuf", [128, 8 * LN], "float32")
+for _k in range(ND):
+    SCRATCH["pd%d" % _k] = ("sbuf", [128, 2 * PL, 8, 16] if OLD else [128, 16 * LN], "float32")
+for _k in range(NR):
+    SCRATCH["wr%d" % _k] = ("sbuf", [128, 8 * LN], "float32")
 for _t in range(NV - 1):
-    SCRATCH["as%d" % _t] = ("sbuf", [128, L], "float32")
     SCRATCH["la%d" % _t] = ("sbuf", [128, L], "float32")
 for _x in range(2):
     SCRATCH["ps_m%d" % _x] = ("psum", [128, 512], "float32")
-    SCRATCH["ps_s%d" % _x] = ("psum", [128, 512], "float32")
-    for _n, _c, _d in [("c0", 2 * PL, "uint16"), ("c1", 2 * PL, "uint16"), ("ln", LN, "uint16"), ("so", 2 * PL, "uint16"),
-                       ("nm", LN + 16, "float32"), ("tt", 2 * LN + 32, "float32"), ("kr", 16 * LN, "bfloat16"), ("zq", 32 * LN, "bfloat16"),
-                       ("ff", SL, "float32"), ("be", SL, "float32"), ("d1", SL, "float32"), ("xx", SL, "bfloat16"),
-                       ("ns", 144, "float32"), ("cs", SL, "float32"), ("ty", 4 * PL, "float32"), ("cex", LN, "float32"), ("nm0", LN, "float32"),
+    SCRATCH["tf_%d" % _x] = ("sbuf", [128, 4, 32], "float16")
+    SCRATCH["tl_%d" % _x] = ("sbuf", [128, 2 * PL, 17], "float16")
+    SCRATCH["ps_s%d" % _x] = ("psum", [128, 30, 17], "float32")
+    for _n, _c, _d in [("c0", 2 * PL, "uint16"), ("c1", 2 * PL, "uint16"), ("ln", LN, "uint16"), ("lv", NW * LN, "uint16"), ("so", 2 * PL, "uint16"),
+                       ("nf", LN, "float16"), ("kr", 16 * LN, "bfloat16"), ("zq", 32 * LN, "bfloat16"),
+                       ("ff", SL + 8, "float16"), ("rs", SL, "float32"), ("wp", NW * LN, "float32"), ("d1", SL, "float32"), ("un", SL, "float16"),
+                       ("cs", SL, "float32"), ("ty", 4 * PL, "float32"), ("cex", LN, "float32"), ("nm0", LN, "float32"),
                        ("eq", LN, "float32"), ("cnt", LN, "float32"), ("val", LN, "int32"), ("vr", LN, "float32"),
                        ("xa", 3 * PL, "bfloat16"), ("xb", 3 * PL, "bfloat16")]:
         SCRATCH["%s_%d" % (_n, _x)] = ("sbuf", [128, _c], _d)
-    SCRATCH["lv_%d" % _x] = ("sbuf", [128, NW * LN], "uint16")
-    SCRATCH["wa_%d" % _x] = ("sbuf", [128, NW * PL, 17], "bfloat16")
-    SCRATCH["wb_%d" % _x] = ("sbuf", [128, NW * PL, 17], "bfloat16")
+    SCRATCH["wa_%d" % _x] = ("sbuf", [128, NW * PL, 16], "bfloat16")
+    SCRATCH["wb_%d" % _x] = ("sbuf", [128, NW * PL, 16], "bfloat16")
     SCRATCH["sb_%d" % _x] = ("sbuf", [128, NV * 3 * PL], "float32")
     SCRATCH["qs_%d" % _x] = ("sbuf", [128, (NV - 1) * LN], "bfloat16")
     SCRATCH["lc_%d" % _x] = ("sbuf", [128, (NV - 1) * 2 * PL], "float32")
     SCRATCH["lq_%d" % _x] = ("sbuf", [128, (NV - 1) * LN], "bfloat16")
-SEMAPHORES = ["eV", "eS", "eP", "eG"] + ["d%d" % i for i in range(60)] + ["a%d" % i for i in range(15)]
+SEMAPHORES = ["eV", "eS", "eP", "eG"] + ["d%d" % i for i in range(90)] + ["a%d" % i for i in range(15)]
 
 A = AluOpType
 F = ActivationFunctionType
@@ -95,7 +106,7 @@ def cols(x):
 def meets(ops):
     hist, before, out = {}, {}, []
     for i, o in enumerate(ops):
-        deps = set()
+        deps, reads = set(), set()
         acc = [(name(x), bits(x), False) for x in o["r"]] + [(name(x), bits(x), True) for x in o["w"]]
         for b, m, wr in acc:
             h = hist.setdefault(b, [])
@@ -107,12 +118,14 @@ def meets(ops):
             for j, mj, wj in h:
                 if (m & mj) and (wr or wj) and not (wr and o.get("adds") and ops[j].get("adds")):
                     deps.add(j)
+                    if not wr:
+                        reads.add(j)
         for b, m, wr in acc:
             h = hist[b]
             if wr and not o.get("adds"):
                 h[:] = [e for e in h if (e[1] & ~m) or e[0] == i]
             h.append((i, m, wr))
-        out.append({j: not o["st"] == ops[j]["st"] == "P" for j in deps if j != i})
+        out.append({j: o["st"] != ops[j]["st"] or o["st"] == "?" or (o["st"] != "P" and (j in reads or not OPT["inorder"])) for j in deps if j != i})
     return out
 
 
@@ -126,20 +139,24 @@ def schedule(ops):
     for i in range(n):
         for j in deps[i]:
             succ[j].append(i)
-    c, lat = [o["c"] for o in ops], [o["lat"] for o in ops]
+    base = OPT["BASE"]
+    cost = [{e: a[1] * base.get(o["k"], 1.0) for e, a in o["alt"].items()} for o in ops]
+    late = [(o["lat"] - o["c"]) * base.get(o["k"], 1.0) for o in ops]
     gap = lambda j, i: OPT["sem"] if deps[i][j] and ops[i]["e"] is not None else 0
-    fore = [[(k, lat[i] + gap(i, k)) for k in succ[i]] for i in range(n)]
-    aft = [[(j, c[i] + lat[j] - c[j] + gap(j, i)) for j in deps[i]] for i in range(n)]
+    fore = [[(k, late[i] + gap(i, k)) for k in succ[i]] for i in range(n)]
+    aft = [[(j, late[j] + gap(j, i)) for j in deps[i]] for i in range(n)]
+    shy, look = [OPT["shy"] if len(c) > 1 else 0.0 for c in cost], [0, 0, 0]
 
     def place(order, back):
         left = [len(succ[i] if back else deps[i]) for i in range(n)]
-        due = [lat[i] - c[i] if back else 0.0 for i in range(n)]
-        at, free, ready = [0.0] * n, {e: 0.0 for e in "VSPGY"}, {e: [] for e in "VSPGY"}
+        due = list(late) if back else [0.0] * n
+        end, eng, free, ready = [0.0] * n, [None] * n, {e: 0.0 for e in "VSPGY"}, {e: [] for e in "VSPGY"}
 
         def start(i, t):
-            at[i] = t
+            end[i] = t
             for k, d in (aft[i] if back else fore[i]):
-                due[k] = max(due[k], t + d)
+                if due[k] < t + d:
+                    due[k] = t + d
                 left[k] -= 1
                 if left[k] == 0:
                     arrive(k)
@@ -147,44 +164,175 @@ def schedule(ops):
         def arrive(k):
             if ops[k]["e"] is None:
                 start(k, due[k])
-            else:
-                ready[ops[k]["e"]].append(k)
+            for e in cost[k]:
+                if e:
+                    ready[e].append(k)
         for i in [i for i in range(n) if left[i] == 0]:
             arrive(i)
         while any(ready.values()):
-            t, e = min((max(free[e], min(due[k] for k in r)), e) for e, r in ready.items() if r)
-            i = min((k for k in ready[e] if due[k] <= t), key=lambda k: order[k])
-            ready[e].remove(i)
-            free[e] = t + c[i]
-            start(i, t)
-        return at
+            t, e = min((max(free[e], min([due[k] for k in r])), e) for e, r in ready.items() if r)
+            rank = [(order[k] + (shy[k] if e == "V" else 0.0), k) for k in ready[e] if due[k] <= t + look[0]]
+            u, i = min(rank)
+            if due[i] > t:
+                i = min([(a, k) for a, k in rank if due[k] <= t and (t + cost[k][e] <= due[i] + look[2] or a < u + look[1])] or [(u, i)])[1]
+            for z in cost[i]:
+                ready[z].remove(i)
+            eng[i] = e
+            free[e] = max(t, due[i]) + cost[i][e]
+            start(i, free[e])
+        return end, eng
 
     hard = [[(j, gap(j, i) > 0) for j in deps[i]] for i in range(n)]
 
-    def replay(order, scale):
-        end, free, sem = [0.0] * n, {e: 0.0 for e in "VSPGY"}, OPT["sem"] * scale.get("sem", 1.0)
+    def replay(order, eng, scale):
+        end, free, sem = [0.0] * n, {e: 0.0 for e in (None, "V", "S", "P", "G", "Y", "D")}, OPT["sem"] * scale.get("sem", 1.0)
         for i in order:
-            o = ops[i]
-            t = max([end[j] + (sem if w else 0.0) for j, w in hard[i]] + [free.get(o["e"], 0.0)])
+            o, e = ops[i], eng[i]
+            t = free[e]
+            for j, w in hard[i]:
+                u = end[j] + sem if w else end[j]
+                if u > t:
+                    t = u
             k = scale.get(o["k"], 1.0)
-            end[i] = t + lat[i] * k
-            if o["e"] is not None:
-                free[o["e"]] = t + c[i] * k
+            c = o["alt"][e][1]
+            end[i] = t + (o["lat"] - o["c"] + c) * k
+            if "b" in o:
+                end[i] = free["D"] = max(end[i], free["D"] + o["b"] * k)
+            if e:
+                free[e] = t + c * k
         return max(end)
 
+    def fit(order, back):
+        left = [len(succ[i] if back else deps[i]) for i in range(n)]
+        due = list(late) if back else [0.0] * n
+        end, eng, busy = [0.0] * n, [None] * n, {e: [] for e in "VSPGY"}
+        ready = sorted((order[i], i) for i in range(n) if left[i] == 0)
+        while ready:
+            i = ready.pop(0)[1]
+            t = due[i]
+            if ops[i]["e"] is not None:
+                found = []
+                for e, c in cost[i].items():
+                    u, line = due[i], busy[e]
+                    a, z = 0, len(line)
+                    while a < z:
+                        if line[(a + z) // 2][1] <= u:
+                            a = (a + z) // 2 + 1
+                        else:
+                            z = (a + z) // 2
+                    while a < len(line) and line[a][0] < u + c:
+                        u = line[a][1]
+                        a += 1
+                    found.append((u + c + (shy[i] if e == "V" else 0.0), u + c, e, a))
+                t, e, a = min(found)[1:]
+                busy[e].insert(a, (t - cost[i][e], t))
+                eng[i] = e
+            end[i] = t
+            more = False
+            for k, d in (aft[i] if back else fore[i]):
+                if due[k] < t + d:
+                    due[k] = t + d
+                left[k] -= 1
+                if left[k] == 0:
+                    ready.append((order[k], k))
+                    more = True
+            if more:
+                ready.sort()
+        return end, eng
+
+    if OPT["sgs"]:
+        place = fit
     tail = [0.0] * n
     for i in range(n - 1, -1, -1):
-        tail[i] = max([tail[k] + d for k, d in fore[i]] + [lat[i]])
-    at, best = place([-x for x in tail], False), None
-    for r in range(OPT["rounds"]):
-        u = place([-at[i] - c[i] for i in range(n)], True)
-        at = place([-u[i] - c[i] for i in range(n)], False)
-        order = sorted(range(n), key=lambda i: (-1.0 if ops[i].get("load") else at[i], i))
-        ends = [replay(order, s) for s in SCALES]
+        tail[i] = max([tail[k] + d for k, d in fore[i]] + [late[i]]) + min(cost[i].values())
+    best, top, seed = None, None, 1
+    for r in range(OPT["rounds"] * len(OPT["WAIT"])):
+        if r % OPT["rounds"] == 0:
+            look[:] = OPT["WAIT"][r // OPT["rounds"]]
+            end, best = place([-x for x in tail], False)[0], None
+        u = place([-x for x in end], True)[0]
+        shake = []
+        for i in range(n):
+            seed = (seed * 1103515245 + 12345) % 2 ** 31
+            shake.append(OPT["shake"] * (1 + r % 4) * seed / 2 ** 31 + ops[i]["lag"])
+        end, eng = place([shake[i] - u[i] for i in range(n)], False)
+        order = sorted(range(n), key=lambda i: (-1.0 if ops[i].get("load") else end[i] - cost[i][eng[i]], i))
+        ends = [replay(order, eng, s) / s["of"] for s in SCALES]
         if best is None or sum(ends) < best[0]:
-            best = (sum(ends), order, ends)
-    ORDER["end"] = (best[0] / len(SCALES), best[2])
-    return best[1]
+            best = (sum(ends), order, eng, ends, end)
+        if top is None or best[0] < top[0]:
+            top = best
+        if r % OPT["back"] == OPT["back"] - 1:
+            end = best[4]
+    order, eng = list(top[1]), list(top[2])
+    wait = [[[(j, OPT["sem"] * s.get("sem", 1.0) if w else 0.0) for j, w in hard[i]] for i in range(n)] for s in SCALES]
+    unit = [[s.get(o["k"], 1.0) for o in ops] for s in SCALES]
+    slow, share = [o["lat"] - o["c"] for o in ops], [o.get("b", 0.0) for o in ops]
+    price = [o["alt"][eng[i]][1] for i, o in enumerate(ops)]
+
+    def run(s, p, old):
+        end, fin, why = [list(a) for a in old]
+        free, last, w, u = {None: 0.0, "D": 0.0}, {}, wait[s], unit[s]
+        for i in order[p - 1::-1] if p else []:
+            if eng[i] not in last:
+                last[eng[i]], free[eng[i]] = i, fin[i]
+            if share[i] and not free["D"]:
+                free["D"] = end[i]
+            if len(last) == 6 and free["D"]:
+                break
+        free[None] = 0.0
+        for i in order[p:]:
+            e = eng[i]
+            t, y = free.get(e, 0.0), -1 - last.get(e, n)
+            for j, d in w[i]:
+                if end[j] + d > t:
+                    t, y = end[j] + d, j
+            c = t + price[i] * u[i]
+            end[i] = c + slow[i] * u[i]
+            if share[i]:
+                end[i] = free["D"] = max(end[i], free["D"] + share[i] * u[i])
+            if e:
+                free[e], last[e] = c, i
+            fin[i], why[i] = c, y
+        return end, fin, why
+
+    state = [run(s, 0, [[0.0] * n] * 3) for s in range(len(SCALES))]
+    worth = lambda st: sum(max(a[0]) / s["of"] for a, s in zip(st, SCALES))
+    now = worth(state)
+    for r in range(OPT["mend"]):
+        seed = (seed * 1103515245 + 12345) % 2 ** 31
+        end, fin, why = state[(seed >> 8) % len(SCALES)]
+        i, pairs = end.index(max(end)), []
+        while i < n:
+            if why[i] < 0 and -1 - why[i] < n:
+                pairs.append((-1 - why[i], i))
+            i = why[i] if why[i] >= 0 else -1 - why[i]
+        seed = (seed * 1103515245 + 12345) % 2 ** 31
+        j, i = pairs[(seed >> 8) % len(pairs)]
+        a, z, kept, flip = order.index(j), order.index(i), list(order), None
+        seed = (seed * 1103515245 + 12345) % 2 ** 31
+        if (seed >> 8) % 3 == 0 and len(cost[i]) + len(cost[j]) > 2:
+            flip = i if len(cost[i]) > 1 else j
+            was = eng[flip]
+            eng[flip] = "V" if was == "S" else "S"
+            price[flip] = ops[flip]["alt"][eng[flip]][1]
+        else:
+            up, rest = [i], []
+            for k in order[z - 1:a:-1]:
+                (up if any(k in deps[m] for m in up) else rest).append(k)
+            if ops[j].get("load") or any(j in deps[m] for m in up):
+                continue
+            order[a:z + 1] = up[::-1] + [j] + rest[::-1]
+        new = [run(s, a, state[s]) for s in range(len(SCALES))]
+        if worth(new) <= now + OPT["slack"] * (1 - r / OPT["mend"]):
+            state, now = new, worth(new)
+        elif flip is None:
+            order[:] = kept
+        else:
+            eng[flip] = was
+            price[flip] = ops[flip]["alt"][was][1]
+    ORDER["end"] = (now / len(SCALES), [max(a[0]) / s["of"] for a, s in zip(state, SCALES)])
+    return order, eng
 
 
 def emit(g, T, ops):
@@ -242,7 +390,7 @@ def rank_program(g, core, T, topo):
     n_out = len(topo.engines(core, nxt))
     n_in = len(topo.engines(T.cores[(rank - 1) % len(T.cores)], core))
     ops, nd, na, loaded, hop = [], [0], [0], [0.0], ["c"]
-    cy = OPT["cy"]
+    cy, lag = OPT["cy"], [0.0]
 
     def ap(x):
         if x[0] == "*":
@@ -262,14 +410,17 @@ def rank_program(g, core, T, topo):
             else:
                 w.append(x)
         ops.append({"e": e, "f": f, "r": r, "w": w, "sem": sem, "n": n, "st": sem or e, "c": c, "lat": c if lat is None else lat, "from": len(ops) - 1,
+                    "alt": {e: (f, c)}, "lag": lag[0],
                     "grp": "%s%s%s" % (e, hop[0], name((w or r)[0])[:4]),
-                    "k": "pe" if e == "P" else ("dma" if n == 16 else "rem") if sem else "sc" if outs[0][0] == "*" else "ga" if ins and ins[0][0] == "*" else ""})
+                    "k": "pe" if e == "P" else ("dma" if n >= 16 else "rem") if sem else "sc" if outs[0][0] == "*" else "ga" if ins and ins[0][0] == "*" else ""})
 
     def cost(o, a, k=1.0, fixed=50):
         if o[0] == "*":
             return fixed + cols(o) * OPT["sc"] * cy
         if a[0] == "*":
             return fixed + cols(a) * OPT["ga"] * cy
+        if k == 1.0 and fixed == 50 and "32" not in SCRATCH[name(o)][2] + SCRATCH[name(a)][2]:
+            k = 0.5
         return OPT["vo"] + max(64, cols(a) * k) * cy
 
     def num(x):
@@ -303,13 +454,31 @@ def rank_program(g, core, T, topo):
         else:
             rec("S", lambda q: q.activation(ap(o), ap(i), fn, bias=num(bias), scale=1.0 if scale is None else scale), [o], [i, bias], c)
 
+    def either():
+        o = ops.pop()
+        ops[-1]["alt"].update(o["alt"])
+        ops[-1]["st"] = "?"
+
+    def move_on(o, i, how="?", scale=None):
+        if how != "S":
+            cp(o, i) if scale is None else ts(o, i, scale, A.mult)
+        if how != "V":
+            act(o, i, F.Copy) if scale is None else act(o, i, F.Identity, 0.0, scale)
+        if how == "?":
+            either()
+
     def mms(calls, adds=False):
+        c = [max(min(64, cols(x[1])), cols(x[2])) * OPT["pe"] * (4 if SCRATCH[x[1][0]][2] == "float32" else 1) for x in calls]
+        if sum(c) > OPT["piece"] and len(calls) > 1:
+            mms(calls[:len(calls) // 2], adds)
+            mms(calls[len(calls) // 2:], adds)
+            return
+
         def f(q):
             for o, lt, r, start, stop in calls:
                 ins = q.matmul(ap(o), ap(lt), ap(r), start, stop)
             return ins
-        rec("P", f, list(dict.fromkeys(x[0][1] if x[0][0] == "^" else x[0] for x in calls)), list(dict.fromkeys([x[1] for x in calls] + [x[2] for x in calls])),
-            sum(max(min(64, cols(x[1])), cols(x[2])) * OPT["pe"] * (4 if SCRATCH[x[1][0]][2] == "float32" else 1) for x in calls))
+        rec("P", f, list(dict.fromkeys(x[0][1] if x[0][0] == "^" else x[0] for x in calls)), list(dict.fromkeys([x[1] for x in calls] + [x[2] for x in calls])), sum(c))
         ops[-1]["adds"] = adds
 
     def dsem():
@@ -329,7 +498,8 @@ def rank_program(g, core, T, topo):
     def move(land, i, nbytes):
         s, a = dsem(), "a%d" % na[0]
         na[0] += 1
-        rec("G", lambda q: q.remote_dma(ap(land), ap(i), T.sem[a], T.sem[s], pid, rid, mask), [], [i], OPT["gi"], s, n_out, OPT["rl"] + nbytes / OPT["rb"])
+        rec("G", lambda q: q.remote_dma(ap(land), ap(i), T.sem[a], T.sem[s], pid, rid, mask), [], [i], OPT["gi"], s, n_out, OPT["rl"] + nbytes / OPT["rb"] + (2000 if na[0] == 1 else 0))
+        ops[-1]["arr"] = a
         rec(None, None, [land], [], 0, a, n_in)
 
     load("Y", v("sti", 0, 16), T.st[:], 8192)
@@ -345,100 +515,82 @@ def rank_program(g, core, T, topo):
             rec("G", lambda q: q.iota(ap(o), pat, base, cm, allow_small_or_imprecise_dtypes=True), [o], [], 130 + 2 * cy * cols(o))
         else:
             rec("G", lambda q: q.iota(ap(o), pat, base, cm), [o], [], 130 + 2 * cy * cols(o))
-    iota(v("pi", 0, 1), [[0, 1]], 0, 1, False)
-    iota(v("io", 0, 256), [[0, 2], [1, 128]], 0, 0, True)
-    iota(v("tw", 9, 17), [[0, 2], [2, 4]], 0, 0, True)
-    iota(v("tw", 29, 37), [[8, 2], [0, 4]], 0, 0, True)
     iota(v("jj", 0, LN), [[0, PL], [1, 16]], 0, 0, True)
-    iota(vn("roll", (0, 16), (0, 16)), [[8, 16], [0, 2], [1, 8]], 0, 0, True)
-    iota(v("sel", 0, 1024), [[0, 1024]], 0, 0, True)
-    for a in (0, 64):
-        rec("G", lambda q, a=a: q.affine_select(T.sel[:], T.sel[:], [[-8, 8], [-1, 8], [0, 16]], A.not_equal, 1.0, -a, 1),
-            [v("sel", 0, 1024)], [v("sel", 0, 1024)], 170 + 2048 * cy)
+    ops[-1]["load"] = True
+    iota(v("pi", 0, 1), [[0, 1]], 0, 1, False)
+    iota(v("io", 0, SL), [[1, SL]], 0, 0, True)
+    iota(v("cex_0", 0, 4 * PL), [[LN, 4], [0, PL]], 0, 0, True)
+
+    def pick(o, pat, base, one=1.0, src=None):
+        src = src or v("zf", 0, cols(o))
+        rec("G", lambda q: q.affine_select(ap(o), ap(src), pat, A.not_equal, one, base, -1), [o], [src], 170 + 2 * cy * cols(o))
+    iota(v("zf", 0, 512), [[0, 512]], 0, 0, True)
+    pick(v("nid", 0, 128), [[1, 128]], 0, -1.0)
+    for u in range(2):
+        pick(vn("nsel", u, (0, 160)), [[32, 5], [-1000, 2], [1, 16]], 1000 + 16 * u)
+    for o in ("f16", "fore"):
+        pick(v(o, 0, 128), [[4, 4], [16, 8], [1, 4]], 0)
+    pick(v("back", 0, 128), [[4, 8], [32, 4], [1, 4]], 0)
+    s = dsem()
+    rec("G", lambda q, s=s: q.dma_start(T.back[:, 128:256], T.back[:, 0:128]).then_inc(T.sem[s], 16), [v("back", 128, 256)], [v("back", 0, 128)], 3000, s, 16, 5000)
+    pick(v("idf", 0, 256), [[0, 2], [1, 128]], 0)
+    pick(vn("roll", (0, 4), (0, 64)), [[32, 4], [0, 2], [1, 32]], 0)
+    for a in range(4):
+        z = v("sel", 512 * (a % 2), 512 * (a % 2) + 512)
+        pick(z, [[1, 4], [4, 8], [0, 16]], 32 * a, 1.0, z if a > 1 else None)
     fill(v("zq_0", 0, 32 * LN), 0.0)
     act(v("zq_1", 0, 32 * LN), v("zq_0", 0, 32 * LN), F.Copy)
     fill(v("pg", W, W + 16), 0)
-    fill(v("kc", 0, SL), 1.6875)
-    fill(v("kc", 0, SL, 17), 0.0)
-    fill(v("zz", 0, L), 0.0)
-    fill(v("cc", 2 * LN, 3 * LN), 0.0)
-    for k, (s, op) in enumerate([(15, A.bitwise_and), (4, A.logical_shift_right), (7, A.bitwise_and), (3, A.logical_shift_right), (3, A.bitwise_and)]):
-        ts(v("pi", k + 1, k + 2), v("pi", 0, 1), s, op)
-    cp(v("pf", 0, 6), v("pi", 0, 6))
-    cP, cR, cX, cR7, cP8, cR3 = [v("pf", k, k + 1) for k in range(6)]
-    cD, cM15, cN15, cR8, cF, cB, cZ = [v("pf", k, k + 1) for k in range(6, 13)]
+    act(v("zz", 0, L), v("zf", 0, L), F.Copy)
+    act(v("cc", 2 * LN, 3 * LN), v("zf", 0, LN), F.Copy)
+    for k, (s, m) in enumerate([(0, 15), (4, 7), (0, 3)]):
+        ts(v("pi", k + 1, k + 2), v("pi", 0, 1), s, A.logical_shift_right, m, A.bitwise_and)
+    cp(v("pf", 0, 3), v("pi", 1, 4))
+    cR, cX, cR3, cD, cM15, cN15, cZ, cY = [v("pf", k, k + 1) for k in range(8)]
     ts(cD, cR, float(W), A.add)
     ts(cM15, cR, 15.0, A.is_equal, -BIG, A.mult)
     ts(cN15, cR, 15.0, A.not_equal, -BIG, A.mult)
-    ts(cR8, cR, 8.0, A.is_ge)
-    ts(cF, cR, 8.0, A.mult, cX, A.add)
-    ts(cB, cR7, 16.0, A.mult, cP8, A.add)
-    ts(cZ, cR3, 8.0, A.mult, cX, A.add)
-    ts(cZ, cR, 32.0, A.mult, cZ, A.add)
-    ts(v("lz", 0, 8), v("io", 0, 8), 512.0, A.mult, cZ, A.add)
-    wPL, wN, wE, wA, wB, wO, wQ = [v("tw", 20 * k, 20 * k + 17) for k in range(7)]
-    tPL, tN, tE, tA9, tB9, tO9, tQ = [v("tw", 20 * k, 20 * k + 9) for k in range(7)]
-    ts(tE, v("io", 0, 9), 16.0, A.mult, cR, A.add)
-    ts(v("ti", 0, 9), tE, -8.0, A.add, 1 / 17.0, A.mult)
-    cp(tPL, v("ti", 0, 9))
-    ts(tN, tPL, -17.0, A.mult)
-    tt(tN, tN, tE, A.add)
-    ts(v("tw", 9, 17), v("tw", 9, 17), cR8, A.add)
-    ts(v("tw", 29, 37), v("tw", 29, 37), cR7, A.add)
-    ts(v("ti", 20, 37), wPL, cX, A.add)
-    ts(v("ti", 20, 37), v("ti", 20, 37), 1, A.bitwise_and)
-    cp(wO, v("ti", 20, 37))
-    ts(v("ti", 40, 57), wPL, 16.0, A.mult, LN - 16.0, A.add)
-    ts(v("ti", 40, 57), v("ti", 40, 57), LN - 1, A.bitwise_and)
-    ts(wA, wPL, 16.0, A.mult)
-    ts(wB, v("ti", 40, 57), float(LN), A.add)
-    tt(wB, wB, wA, A.subtract)
-    tt(wB, wB, wO, A.mult)
-    tt(wA, wA, wN, A.add)
-    tt(wA, wA, wB, A.add)
-    cp(v("li", 0, 8), v("tw", 69, 77))
-    ts(tQ, tN, 16.0, A.is_equal)
-    ts(tB9, tPL, 2.0 * LN, A.add)
-    tt(tB9, tB9, tA9, A.subtract)
-    tt(tB9, tB9, tQ, A.mult)
-    tt(tA9, tA9, tB9, A.add)
-    cp(v("lx0", 0, 9), tA9)
-    ts(tQ, tQ, 16.0, A.mult)
-    tt(tA9, tA9, tQ, A.add)
-    cp(v("lx1", 0, 9), tA9)
+    ts(cZ, cX, 4.0, A.mult, cR3, A.add)
+    ts(cY, cR, 32.0, A.mult, cZ, A.add)
+    ts(v("lz", 0, 8), v("io", 0, 8), 512.0, A.mult, cY, A.add)
+    if not OLD:
+        iota(v("cex_1", 0, 2 * PL), [[LN, 2], [1, PL]], 0, 0, True)
+        for u in range(2):
+            pick(vn("hsel", u, (0, 144)), [[16, 9], [-1000, 2], [1, 8]], 1000 + 8 * u)
+        ts(cZ, cR, 8.0, A.mult)
+        ts(v("lp", 0, 16), v("cex_1", 0, 2 * PL), cZ, A.add)
+    ts(v("kc", 0, SL), v("io", 0, SL), 0.0, A.mult, -1.6875, A.add)
+    ts(v("kc", 0, SL, 17), v("io", 0, PL), 0.0, A.mult)
+    ts(v("kc", SL, 2 * SL), v("io", 0, SL), 0.0, A.mult, -2048 / BIG, A.add)
+    ts(v("kc", SL + 16, 2 * SL, 17), v("io", 0, PL), -16 / BIG, A.mult, -W / BIG, A.add)
+    for x in range(2):
+        ts(vn("tl_%d" % x, (0, 2 * PL), 16), v("cex_0", 2 * PL * x, 2 * PL * (x + 1)), cR, A.add, 1 / BIG, A.mult)
     cp(v("le", 0, 8), v("io", 0, 8))
-    ts(v("idf", 0, 256), v("io", 0, 256), cP, A.is_equal)
-    act(v("idb", 0, 256), v("idf", 0, 256), F.Copy)
-    ts(v("back", 0, 256), v("io", 0, 256), cB, A.is_equal)
-    ts(v("fore", 0, 128), v("io", 0, 128), cF, A.is_equal)
-    ts(vn("roll", (0, 16), (0, 16)), vn("roll", (0, 16), (0, 16)), cP, A.is_equal)
+    pick(v("idb", 0, 256), [[0, 2], [1, 128]], 0)
     for t in range(1, NV):
-        act(v("on", 128 * t - 128, 128 * t), vn("roll", (0, 16), (8 - t, 16 - t)), F.Copy)
+        act(v("on", 128 * t - 128, 128 * t), vn("roll", (0, 4), (32 - 4 * t, 64 - 4 * t)), F.Copy)
     ts(v("cc", 0, LN), v("jj", 0, LN), cR, A.is_ge, -BIG, A.mult)
     act(v("cc", LN, 2 * LN), v("jj", 0, LN), F.Identity, cN15, 0.0)
-    act(v("rm", 0, LN), v("jj", 0, LN), F.Sign)
-    act(v("nid", 0, 128), v("idf", 0, 128), F.Identity, 0.0, -1.0)
+    act(v("rm", 0, LN), v("jj", 0, LN), F.Sigmoid, -100.0, 200.0)
+    ops[-1].update(load=True, c=1420, lat=1420, alt={"S": (ops[-1]["f"], 1420)})
     QA, QB = [[v("kq", W + LN * (2 * x + k), W + LN * (2 * x + k + 1)) for x in range(2)] for k in range(2)]
     for x in range(2):
-        fill(v("d1_%d" % x, 0, SL), 0.0)
-        fill(v("d1_%d" % x, 0, SL, 17), 1.0)
-        fill(v("ps_s%d" % x, 3 * SL - 1, 3 * SL), 0.0)
-        for k, own in enumerate((QA[x], QB[x])):
-            ts(v("tt_%d" % x, 2 * LN + 16 * k, 2 * LN + 16 * k + 9), tE, float(own[1][0]), A.add)
+        act(v("d1_%d" % x, 0, SL), v("zf", 0, SL), F.Copy)
+        act(v("d1_%d" % x, 0, SL, 17), v("zf", 0, PL), F.Identity, 1.0)
+        ts(v("ff_%d" % x, SL, SL + 8), v("io", 0, 8), 0.0, A.mult)
     for k in range(NP):
         ts(v("pg", k * pc, (k + 1) * pc), v("bpk", k * pc, (k + 1) * pc), W - 1, A.bitwise_and)
         ts(v("pg", W // 2 + k * pc, W // 2 + (k + 1) * pc), v("bpk", k * pc, (k + 1) * pc), 12, A.logical_shift_right)
 
     KT, PG, VS = v("kq", 0, W), v("pg", 0, W + 16), v("vs", 0, W)
     IDF, IDB, BACK, FORE, PA = v("idf", 0, 128), v("idb", 0, 128), v("back", 0, 128), v("fore", 0, 128), v("ps_a", 0, L)
-    bank = [0]
+    bank, turns, SG, LV = [0], [0, 0], v("sg", 0, W), SL + LN
+    for a in range(0, 0 if OLD else W, OPT["SG"]):
+        act(v("sg", a, a + OPT["SG"]), v("vs", a, a + OPT["SG"]), F.Sigmoid)
 
     def split(src, a, b, scalar):
         for p, z in ((0, a), (64, b)):
-            if scalar:
-                act(rows(z, p, p + 64), rows(src, p, p + 64), F.Copy)
-            else:
-                cp(rows(z, p, p + 64), rows(src, p, p + 64))
+            move_on(rows(z, p, p + 64), rows(src, p, p + 64), scalar)
         for p, z in ((0, a), (64, b)):
             tt(rows(z, 64 - p, 128 - p), rows(src, p, p + 64), rows(z, p, p + 64), A.subtract)
 
@@ -447,151 +599,222 @@ def rank_program(g, core, T, topo):
         cutv, p0 = t < NV - 1, PL * (1 - x)
         hop[0] = "%d%d" % (h, x)
         b = lambda name, a, e, s=1: v("%s_%d" % (name, x), a, e, s)
-        ps = lambda a, e, s=1: v("ps_s%d" % x, a, e, s)
+        ps = lambda a, e, c0=0, c1=17: vn("ps_s%d" % x, (a, e), (c0, c1))
         pm = lambda a, e, s=1: v("ps_m%d" % x, a, e, s)
-        came, camp, tB, tP = [b("ty", PL * k, PL * k + PL) for k in range(4)]
-        cl, tw, zq, e0 = b("c0", 0, PL), b("tt", 0, 2 * LN + 32), ind(b("zq", 0, 32 * LN), v("lz", 0, PL)), 3 * SL
+        came, camp, tP = [b("ty", PL * k, PL * k + PL) for k in range(3)]
+        cl, zq, k = b("c0", 0, PL), ind(b("zq", 0, 32 * LN), v("lz", 0, PL)), h % NW
+        ln = lambda a, e: b("ln", a, e)
         if h == 0:
             cp(cl, v("sti", p0, p0 + PL))
-            ts(came, v("sti", p0, p0 + PL), -1.0, A.mult, TOP, A.add)
-            mms([(ps(e0, e0 + PL), FORE, came, True, True)])
-            cp(camp, ps(e0, e0 + PL))
+            ts(came, v("sti", p0, p0 + PL), -1 / BIG, A.mult, TOP / BIG, A.add)
+            mms([(ps(16, 17, 0, PL), FORE, came, True, True)])
+            cp(camp, ps(16, 17, 0, PL))
         elif first:
             s0 = 2 * PL * (t - 1)
-            mms([(ps(e0, e0 + PL), v("back", 128 - 16 * t, 256 - 16 * t), b("lc", s0, s0 + PL), True, True),
-                 (ps(e0 + PL, e0 + 3 * PL), v("on", 128 * t - 128, 128 * t), b("lc", s0, s0 + 2 * PL), True, True)])
-            ts(cl, ps(e0, e0 + PL), 0.0, A.add)
-            cp(b("d1", 0, SL, 17), ps(e0 + 2 * PL, e0 + 3 * PL))
+            mms([(ps(16, 17, 0, PL), v("back", 128 - 16 * t, 256 - 16 * t), b("lc", s0, s0 + PL), True, True),
+                 (ps(17, 19, 0, PL), v("on", 128 * t - 128, 128 * t), b("lc", s0, s0 + 2 * PL), True, True)])
+            ts(cl, ps(16, 17, 0, PL), 0.0, A.add)
+            move_on(b("d1", 0, SL, 17), ps(18, 19, 0, PL), OPT["E"][5])
             if cutv:
-                ts(b("ty", 0, 2 * PL), ps(e0, e0 + 2 * PL), -1.0, A.mult, TOP, A.add)
-        cp(b("ln", 0, LN), ind(PG, cl))
+                ts(b("ty", 0, 2 * PL), ps(16, 18, 0, PL), -1 / BIG, A.mult, TOP / BIG, A.add)
+        cp(ln(0, LN), ind(PG, cl))
         if h == 0:
-            act(QA[x], ind(KT, cl), F.Copy)
+            move_on(QA[x], ind(KT, cl), OPT["E"][2])
         elif first:
-            mms([(pm(2 * LN, 3 * LN), v("idb", 128 - 16 * t, 256 - 16 * t), b("lq", LN * (t - 1), LN * t), True, True)])
-            act(QA[x], pm(2 * LN, 3 * LN), F.Copy)
+            mms([(ps(0, PL, 0, 16), v("idb", 128 - 16 * t, 256 - 16 * t), b("lq", LN * (t - 1), LN * t), True, True)])
+            move_on(QA[x], ps(0, PL, 0, 16), OPT["E"][4])
         if first:
             cp(zq, QA[x])
-        mms([(ps(0, SL), IDB, v("kc", 0, SL), True, False)])
+        NID, NAMES, r0 = v("nid", 0, 128), pm(0, SL), PL * (h % 2)
+        tl = lambda a, e: vn("tl_%d" % x, (r0, r0 + PL), (a, e))
+        ts(b("nf", 0, LN), ln(0, LN), -2048.0, A.add, 1 / BIG, A.mult)
+        turn(vn("tf_%d" % x, (0, 4), (0, 32)), b("nf", 0, LN))
+        mms([(pm(SL + 64 * u, SL + 64 * u + 64), vn("nsel", u, (16 - 16 * o, 144 - 16 * o)), vn("tf_%d" % x, (0, 4), (16 * o, 16 * o + 16)), not o, bool(o))
+             for u in range(2) for o in range(2)])
+        for u in range(2):
+            cp(vn("tl_%d" % x, (r0 + u, r0 + PL, 2), (0, 16)), pm(SL + 64 * u, SL + 64 * u + 64))
+        if OLD:
+            for nh in range(2):
+                ts(b("lv", LN * k + 64 * nh, LN * k + 64 * nh + 64), tl(8 * nh, 8 * nh + 8), BIG, A.mult, 2048.0, A.add)
+        else:
+            mms([(pm(LV + 64 * nh + p2, LV + 64 * nh + 64, 4), vn("hsel", nh, (8 - 8 * o, 136 - 8 * o)), b("nf", 32 * p2 + 16 * o, 32 * p2 + 16 * o + 16), not o, bool(o))
+                 for nh in range(2) for p2 in range(4) for o in range(2)])
+            ts(b("lv", LN * k, LN * k + LN), pm(LV, LV + LN), BIG, A.mult, 2048.0, A.add)
+        mms([(NAMES, NID, v("kc", SL, 2 * SL), True, False), (NAMES, v("f16", 0, 128), tl(0, 17), False, False)])
+        mms([(ps(0, PL), NID, v("kc", 0, SL), True, False)])
         l0 = 0
-        for e, n in OPT["CH"]:
-            o, i = b("kr", 16 * l0, 16 * (l0 + n)), ind(KT, b("ln", l0, l0 + n))
-            if e == "S":
-                act(o, i, F.Identity, 0.0, -1 / 1024.0)
-            else:
-                ts(o, i, -1 / 1024.0, A.mult)
-            mms([(rows(ps(17 * (l // 16) + 1, 17 * (l // 16) + 17), 32 * (l % 16 // 4), 32 * (l % 16 // 4) + 32), b("zq", 32 * l, 32 * l + 32),
+        nv = OPT["CV"][h]
+        for e, n in [("V", nv), ("S", 64 - nv // 4 * 2), ("S", 64 - nv + nv // 4 * 2)] if nv else OPT["CH"]:
+            move_on(b("kr", 16 * l0, 16 * (l0 + n)), ind(KT, ln(l0, l0 + n)), e, -1 / 1024.0)
+            mms([(rows(vn("ps_s%d" % x, l // 16, (1, 17)), 32 * (l % 16 // 4), 32 * (l % 16 // 4) + 32), b("zq", 32 * l, 32 * l + 32),
                   b("kr", 16 * l, 16 * l + 16), False, l >= LN - 16 and l % 4 == 3) for l in range(l0, l0 + n)])
             l0 += n
-        cp(b("nm", 0, LN), b("ln", 0, LN))
-        cp(b("nm", LN, LN + 16), b("ln", 0, 16))
-        turn(b("tt", 0, LN), b("nm", 0, LN))
-        turn(b("tt", LN, 2 * LN), b("nm", 16, LN + 16))
-        k = h % NW
-        if OPT["N17"] == "V":
-            cp(b("ns", 0, 144), ind(tw, v("lx%d" % (h % 2), 0, 9)))
-        else:
-            act(b("ns", 0, 144), ind(tw, v("lx%d" % (h % 2), 0, 9)), F.Copy)
-        mms([(pm(0, SL), FORE, b("ns", 0, SL), True, False)])
-        cp(b("lv", LN * k, LN * k + LN), ind(tw, v("li", 0, 8)))
         if first and cutv:
-            act(b("cex", 0, LN), ind(came, v("le", 0, 8)), F.Copy)
-            act(b("nm0", 0, LN), b("nm", 0, LN), F.Identity, cM15)
-        RS, WW = ps(SL, 2 * SL), ps(2 * SL, 3 * SL)
-        ts(b("ff", 0, SL), ps(0, SL), 1.0, A.min, 1 / 16.0, A.max)
+            move_on(b("cex", 0, LN), ind(came, v("le", 0, 8)), OPT["E"][3])
+            ts(b("nm0", 0, LN), ln(0, LN), cM15, A.add)
+        pw = (lambda a, e: vn("ps_x", (PL * x, PL * x + PL), (a, e))) if NB < 3 else (lambda a, e: ps(PL, 2 * PL, a, e))
+        RS, WW, W1 = b("rs", 0, SL), pw(0, 17), pw(0, 16)
+        ts(b("ff", 0, SL), ps(0, PL), 1.0, A.min, 1 / 16.0, A.max)
         scan(RS, b("ff", 0, SL), b("d1", 0, SL), A.mult, A.max)
-        act(b("be", 0, SL), b("ff", 0, SL), F.Identity, 1.0, -1.0)
-        ts(b("xx", 0, SL), RS, 1 / 16.0, A.is_ge, BIG, A.mult)
-        R16, X16, C15 = ps(SL + 16, 2 * SL, 17), b("xx", 16, SL, 17), b("cs", 15, SL, 17)
-        mms([(pm(0, SL), v("nid", 0, 128), b("xx", 0, SL), False, True)])
-        scan(b("cs", 0, SL), b("xx", 0, SL), pm(0, SL), A.add, A.min)
-        s0, m0, cq, n = 3 * PL * t, 3 * LN, "c%d" % (h % 2), PL if last else 2 * PL
+        ts(b("un", 0, SL), RS, 1 / 16.0, A.is_lt)
+        R16, U16, C15 = b("rs", 16, SL, 17), b("un", 16, SL, 17), b("cs", 15, SL, 17)
+        mms([(NAMES, NID, b("un", 0, SL), False, True)])
+        mms([(WW, NID, b("ff", 1, SL + 1), True, False), (WW, NID, b("un", 0, SL), False, True)])
+        scan(b("cs", 0, SL), b("un", 0, SL), NAMES, A.mult, A.max)
+        s0, m0, cq, n = 3 * PL * t, LV + LN, "c%d" % (h % 2), PL if last else 2 * PL
         mms([(pm(m0, m0 + PL), BACK, C15, True, True)] + ([] if last else [(pm(m0 + PL, m0 + 2 * PL), BACK, b("cs", 16, SL, 17), True, True)]))
         if not first and cutv:
-            ts(b("sb", s0 + PL, s0 + 2 * PL), C15, BIG, A.add)
-        ts(tB, R16, 1 / 16.0, A.is_lt)
-        tt(b("d1", 0, SL, 17) if first else b("sb", s0 + 2 * PL, s0 + 3 * PL), tB, R16, A.max)
+            ts(b("sb", s0 + PL, s0 + 2 * PL), C15, BIG, A.mult)
+        tt(b("d1", 0, SL, 17) if first else b("sb", s0 + 2 * PL, s0 + 3 * PL), U16, R16, A.max)
         if not first and cutv:
             move(b("lc", 2 * PL * t, 2 * PL * (t + 1)), b("sb", s0 + PL, s0 + 3 * PL), 128 * 64)
-        ts(b(cq, 0, n), pm(m0, m0 + n), BIG, A.add)
+        ts(b(cq, 0, n), pm(m0, m0 + n), BIG, A.mult)
         if not last:
-            act(QB[x] if first else b("qs", LN * t, LN * t + LN), ind(v("kq", 0, (QA if first else QB)[x][1][1]), b(cq, PL, 2 * PL)), F.Copy)
+            move_on(QB[x] if first else b("qs", LN * t, LN * t + LN), ind(v("kq", 0, (QA if first else QB)[x][1][1]), b(cq, PL, 2 * PL)), OPT["E"][2])
         if first:
             cp(zq, QB[x])
             if cutv:
-                tt(tP, X16, camp, A.min)
+                tt(tP, camp, U16, A.subtract)
         elif cutv:
             move(b("lq", LN * t, LN * t + LN), b("qs", LN * t, LN * t + LN), 256 * LN)
-        tt(ps(2 * SL, 3 * SL - 1), b("be", 1, SL), ps(SL, 2 * SL - 1), A.mult)
-        tt(WW, b("xx", 0, SL), WW, A.min)
-        split(WW, vn("wa_%d" % x, (PL * k, PL * k + PL), (0, 17)), vn("wb_%d" % x, (PL * k, PL * k + PL), (0, 17)), True)
+        if OPT["E"][6] != "S":
+            ts(W1, W1, 1.0, A.add, 0.0, A.max)
+        if OPT["E"][6] != "V":
+            act(W1, W1, F.Relu, 1.0)
+        if OPT["E"][6] == "?":
+            either()
+        tt(WW, RS, WW, A.mult)
+        nd2 = int(OPT["WR"][2 * h + x])
+        for nh in range(nd2):
+            move_on(b("wp", LN * k + 64 * nh, LN * k + 64 * nh + 64), pw(8 * nh, 8 * nh + 8), OPT["E"][8])
+        if nd2 < 2:
+            split(pw(8 * nd2, 16), vn("wa_%d" % x, (PL * k, PL * k + PL), (8 * nd2, 16)), vn("wb_%d" % x, (PL * k, PL * k + PL), (8 * nd2, 16)), OPT["E"][0])
         if first:
             return
         a = 0 if cutv else 2 * PL
         if cutv:
-            tt(b("sb", s0, s0 + PL), tP, X16, A.subtract)
-        split(b("sb", s0 + a, s0 + 3 * PL), b("xa", a, 3 * PL), b("xb", a, 3 * PL), False)
-        calls = [(pm(m0, m0 + PL), BACK, b("sb", s0, s0 + PL), True, True), (pm(0, 3 * LN), IDB, v("cc", 0, 3 * LN), True, False)] if cutv else []
+            tt(b("sb", s0, s0 + PL), tP, U16, A.mult)
+        split(b("sb", s0 + a, s0 + 3 * PL), b("xa", a, 3 * PL), b("xb", a, 3 * PL), OPT["E"][1])
+        if cutv:
+            mms([(pm(m0 + 2 * PL, m0 + 3 * PL), BACK, b("sb", s0, s0 + PL), True, True), (pm(0, 3 * LN), IDB, v("cc", 0, 3 * LN), True, False)])
+        calls = []
         for jj in range(16):
             calls.append((pm(16 * a + jj, 3 * LN, 16), v("sel", 128 * (jj % 8), 128 * (jj % 8) + 128), b("xb" if jj // 8 else "xa", a, 3 * PL), not cutv, jj == 15 or not cutv))
         mms(calls)
         if cutv:
             tt(b("eq", 0, LN), b("cex", 0, LN), pm(0, LN), A.is_equal)
-            ts(b("eq", 15, LN, 16), pm(m0, m0 + PL), -1 / BIG, A.mult, TOP / BIG, A.add)
+            ts(b("eq", 15, LN, 16), pm(m0 + 2 * PL, m0 + 3 * PL), -1.0, A.mult, TOP / BIG, A.add)
             tt(b("val", 0, LN), b("nm0", 0, LN), pm(LN, 2 * LN), A.max)
             scan(b("cnt", 0, LN), v("rm", 0, LN), b("eq", 0, LN), A.mult, A.max)
             ts(b("so", 0, 2 * PL, 2), b("cnt", 15, LN, 16), BIG, A.mult, cD, A.min)
         act(b("vr", 0, LN), ind(VS, b("c1", 0, PL)), F.Sigmoid)
-        tt(v("yr", 16 * p0, 16 * p0 + LN), b("vr", 0, LN), pm(2 * LN, 3 * LN), A.mult)
+        tt(v("yr", L * t + 16 * p0, L * t + 16 * p0 + LN), b("vr", 0, LN), pm(2 * LN, 3 * LN), A.mult)
 
     def shortcuts(x):
         for pl in range(PL - 1, -1, -1):
             cp(ind(PG, v("so_%d" % x, 2 * pl, 2 * pl + 1)), v("val_%d" % x, 16 * pl, 16 * pl + 16))
 
+    def fold(o, i):
+        s = dsem()
+        rec("G", lambda q: q.dma_start(ap(o), ap(i), accum_op=A.add).then_inc(T.sem[s], 16), [o], [o, i, v("back", 128, 256)], OPT["gi"], s, 16, OPT["fl"])
+        if OPT["ab"]:
+            ops[-1]["b"] = OPT["ab"]
+
+    def spread(wr, wp, c0):
+        s, z = dsem(), dsem()
+
+        def first(q):
+            for a in range(4):
+                q.dma_start(T[wr][0:128:16, 256 * a:256 * a + 256], T[wp][32 * a:32 * a + 32, c0:c0 + 64]).then_inc(T.sem[s], 16)
+
+        def others(q):
+            for i in range(1, 16):
+                q.dma_start(T[wr][i:128:16, :], T[wr][0:128:16, :]).then_inc(T.sem[z], 16)
+        rec("Y", first, [v(wr, 0, 1024)], [v(wp, c0, c0 + 64)], 4 * OPT["yi"], s, 64, OPT["yl"] + 4 * OPT["yi"])
+        rec("Y", others, [v(wr, 0, 1024)], [v(wr, 0, 1024)], 15 * OPT["yi"], z, 240, OPT["yl"] + 15 * OPT["yi"] + 500)
+
     def values(h, x):
         u0, k, t = 2 * h + x, h % NW, h // 2
         hop[0] = "%d%d" % (h, x)
-        vg, pd, how = "vg%d" % (u0 % NG), "pd%d" % (u0 % NG), OPT["SUM"][u0]
+        pd, how, nd2, vg = "pd%d" % (u0 % ND), OPT["SUM"][u0], int(OPT["WR"][u0]), {}
         acc = v("ps_a", LN * (1 - x), LN * (2 - x))
-        for a in range(0, 16 * LN, OPT["VS"]):
-            act(v(vg, a, a + OPT["VS"]), ind(VS, v("lv_%d" % x, LN * k + a // 16, LN * k + (a + OPT["VS"]) // 16)), F.Sigmoid)
+        lv = lambda a, e: v("lv_%d" % x, LN * k + a // 16, LN * k + e // 16)
+        for nh in range(nd2, 2):
+            vg[nh] = "vg%d" % (turns[0] % NG)
+            turns[0] += 1
+            act(v(vg[nh], 0, 1024), ind(VS, lv(1024 * nh, 1024 * nh + 1024)), F.Sigmoid)
+        for nh in range(nd2):
+            wr = "wr%d" % (turns[1] % NR)
+            turns[1] += 1
+            spread(wr, "wp_%d" % x, LN * k + 64 * nh)
+            for a in range(0, 1024, OPT["VS"]):
+                tt(v(pd, 1024 * nh + a, 1024 * nh + a + OPT["VS"]), ind(SG, lv(1024 * nh + a, 1024 * nh + a + OPT["VS"])), v(wr, a, a + OPT["VS"]), A.mult)
         if h % 2 == 0 and x == 0:
             mms([(PA, IDB, v("zz", 0, L), True, False)])
-        closes = h % 2 and x and not (t and how == "d")
+        closes = h % 2 and x and not (t and how in "dbg")
         if closes and t:
             mms([(PA, v("idf", 128 - 16 * t, 256 - 16 * t), v("la%d" % (t - 1), 0, L), False, False)], True)
         kept = {}
-        for nh, j0 in ([(0, 0), (1, 0), (0, 1), (1, 1)] if how == "v" else [(0, 0), (0, 1), (1, 0), (1, 1)]):
-            bk = "ps_w%d" % (bank[0] % NB)
-            bank[0] += 1
-            mms([(vn(bk, (0, PL), (u, 64, 8)), v("sel", 128 * ((j0 + 2 * u) % 8), 128 * ((j0 + 2 * u) % 8) + 128),
-                  vn("w%s_%d" % ("ab"[u // 4], x), (PL * k, PL * k + PL), (8 * nh, 8 * nh + 8)), True, True) for u in range(8)])
-            wide, out = vn(bk, (0, PL), (0, 64)), vn(pd, (PL * nh, PL * nh + PL), (0, 8), (j0, 16, 2))
-            if how == "v" and nh == 0:
-                tt(wide, v(vg, j0, 1024, 2), wide, A.mult)
-                kept[j0] = wide
+        for nh, j0 in ([(0, 0), (1, 0), (0, 1), (1, 1)] if how in "vu" else [(0, 0), (0, 1), (1, 0), (1, 1)]):
+            o0 = 1024 * nh + 512 * j0
+            if OLD:
+                bk = "ps_w%d" % (bank[0] % NB)
+                bank[0] += 1
+                mms([(v(bk, u, 512, 8), v("sel", 128 * ((j0 + 2 * u) % 8), 128 * ((j0 + 2 * u) % 8) + 128),
+                      vn("w%s_%d" % ("ab"[u // 4], x), (PL * k, PL * k + PL), (8 * nh, 8 * nh + 8)), True, True) for u in range(8)])
+                wide, out = v(bk, 0, 512), vn(pd, (PL * nh, PL * nh + PL), (0, 8), (j0, 16, 2))
+                if how in "vug" and nh == 0:
+                    tt(wide, v(vg[nh], j0, 1024, 2), wide, A.mult)
+                    if how != "v":
+                        tt(out if how == "g" else wide, vn("pd%d" % ((u0 - 2) % ND), (0, PL), (0, 8), (j0, 16, 2)), wide, A.add)
+                    kept[j0] = wide
+                    continue
+                tt(out, v(vg[nh], j0, 1024, 2), wide, A.mult)
+                if how in "vu":
+                    tt(out, out, kept[j0], A.add)
+                if how in "vpu":
+                    end = bool(closes and nh and j0)
+                    mms([(v("ps_a", LN * (1 - x) + j0, LN * (2 - x), 2), IDF, vn(pd, (PL * nh, PL * nh + PL), n, (j0, 16, 2)), False, end and n == 7) for n in range(8)], not end)
                 continue
-            tt(out, v(vg, 1024 * nh + j0, 1024 * nh + 1024, 2), wide, A.mult)
-            if how == "v":
-                tt(out, out, kept[j0], A.add)
-            if how != "d":
+            if nh >= nd2:
+                bk = "ps_w%d" % (bank[0] % NB)
+                bank[0] += 1
+                mms([(v(bk, 64 * u, 64 * u + 64), v("sel", 128 * u, 128 * u + 128),
+                      vn("w%s_%d" % ("ab"[j0], x), (PL * k, PL * k + PL), (8 * nh, 8 * nh + 8)), True, True) for u in range(8)])
+                wide, out = v(bk, 0, 512), v(pd, o0, o0 + 512)
+                if how in "vug" and nh == 0:
+                    tt(wide, v(vg[nh], 512 * j0, 512 * j0 + 512), wide, A.mult)
+                    if how != "v":
+                        tt(out if how == "g" else wide, v("pd%d" % ((u0 - 2) % ND), 512 * j0, 512 * j0 + 512), wide, A.add)
+                    kept[j0] = wide
+                    continue
+                tt(out, v(vg[nh], 512 * j0, 512 * j0 + 512), wide, A.mult)
+                if how in "vu":
+                    tt(out, out, kept[j0], A.add)
+            if how in "vpu":
                 end = bool(closes and nh and j0)
-                mms([(v("ps_a", LN * (1 - x) + j0, LN * (2 - x), 2), IDF, vn(pd, (PL * nh, PL * nh + PL), n, (j0, 16, 2)), False, end and n == 7) for n in range(8)], not end)
-        if how == "d":
-            s = dsem()
-            o, i = vn(pd, (0, PL), (0, 8), (0, 16)), vn(pd, (PL, 2 * PL), (0, 8), (0, 16))
-            rec("G", lambda q: q.dma_start(ap(o), ap(i), accum_op=A.add).then_inc(T.sem[s], 16), [o], [o, i], OPT["gi"], s, 16, OPT["dl"] + 2 ** 20 / OPT["db"])
+                a0 = LN * (1 - x) + 64 * j0
+                mms([(v("ps_a", a0, a0 + 64), IDF, v(pd, o0 + n, o0 + 512, 8), False, end and n == 7) for n in range(8)], not end)
+        half = lambda z, nh: vn(z, (PL * nh, PL * nh + PL), (0, 8), (0, 16)) if OLD else v(z, 1024 * nh, 1024 * nh + 1024)
+        if how in "dag":
+            fold(half(pd, 0), half(pd, 1))
+        if how == "b":
+            mine, pd = pd, "pd%d" % ((u0 - 2) % ND)
+            for nh in range(2):
+                fold(half(pd, 0), half(mine, nh))
+        if how in "dbg":
             for n in range(0, 8, 2):
-                mms([(acc, IDF, vn(pd, (0, PL), m, (0, 16)), False, bool(closes and m == 7)) for m in (n, n + 1)], not (closes and n == 6))
+                mms([(acc, IDF, vn(pd, (0, PL), m, (0, 16)) if OLD else v(pd, m, 1024, 8), False, bool(closes and m == 7)) for m in (n, n + 1)], not (closes and n == 6))
             if h % 2 and x and t:
                 mms([(PA, v("idf", 128 - 16 * t, 256 - 16 * t), v("la%d" % (t - 1), 0, L), False, True)])
 
     def report(t):
-        y = v("yy", L * t, L * t + L)
+        y, ac = v("yy", L * t, L * t + L), v("ac", L * t, L * t + L)
+        if t < NV - 1 or not OLD:
+            move_on(ac, PA, OPT["E"][7] if t < NV - 1 else "V")
         if t < NV - 1:
-            act(v("as%d" % t, 0, L), PA, F.Copy)
-            move(v("la%d" % t, 0, L), v("as%d" % t, 0, L), 512 * L)
-        tt(y, v("yr", 0, L), PA, A.add)
+            move(v("la%d" % t, 0, L), ac, 512 * L)
+        tt(y, v("yr", L * t, L * t + L), PA, A.add) if OLD else tt(y, ind(ac, v("lp", 0, 16)), v("yr", L * t, L * t + L), A.add)
         store(T.ya[:, L * t:L * t + L], y)
 
     for h in range(2 * NV):
@@ -600,11 +823,16 @@ def rank_program(g, core, T, topo):
         if h % 2 and h < 2 * NV - 1:
             for x in range(2):
                 shortcuts(x)
+        lag[0] = OPT["LAG"][h]
         for x in range(2):
             values(h, x)
         if h % 2:
             report(h // 2)
+        lag[0] = 0.0
     key = (n_out, n_in)
     if key not in ORDER:
         ORDER[key] = schedule(ops)
-    emit(g, T, [ops[i] for i in ORDER[key]])
+    for o, e in zip(ops, ORDER[key][1]):
+        if len(o["alt"]) > 1:
+            o.update(e=e, st=e, f=o["alt"][e][0], c=o["alt"][e][1], lat=o["alt"][e][1], grp=e + o["grp"][1:])
+    emit(g, T, [ops[i] for i in ORDER[key][0]])

import numpy as np
from concourse.mybir import AluOpType, ActivationFunctionType

W, L, NV = 4096, 256, 4
BIG, TOP = 8192.0, 4112.0
PL, LN, SL = 8, 128, 136
NB, NG, ND, NR, NW = 3, 6, 6, 4, 3
OPT = {"CH": [("S", 44), ("S", 44), ("S", 40)], "VS": 512, "cy": 0.83, "ga": 1.56, "sc": 3.8, "pe": 0.42, "sem": 150, "dl": 2200,
       "db": 500.0, "vo": 10, "so": 65, "rl": 4000, "rb": 60.0, "gi": 1200, "rounds": 10,
       "SUM": "ddddddddaaggaauu", "E": "SVSSSVSSS", "BASE": {}, "shy": 0, "shake": 100, "back": 3,
       "ab": 0, "mend": 0, "slack": 0, "inorder": 0, "CV": [44, 44, 40, 40, 36, 36, 32, 36],
       "WR": "0000000000000000", "SG": 1024, "yi": 100, "margin": 1000, "piece": 1000, "LAG": [0] * 8, "sgs": 0, "fl": 7500, "yl": 3000,
       "WAIT": [(0, 0, 0), (100, 500, 30), (200, 1000, 30), (100, 300, 30)] * 12}
SCALES = [{"of": of, "": f, "pe": f, "ga": f * ga, "sc": f * sc, "dma": d, "rem": d, "sem": d}
          for of, f, ga, sc, d in [(1.16, 1.0, 1.0, 1.0, 1.0), (1.64, 1.25, 1.25, 1.0, 1.0), (1.34, 1.25, 0.75, 1.0, 1.0), (1.6, 1.4, 1.0, 1.3, 1.0),
                                   (1.41, 1.1, 1.15, 0.7, 1.4), (1.16, 1.1, 0.7, 0.8, 0.75)]]
OLD = True

SCRATCH = {
    "bpk": ("sbuf", [128, W // 2], "int32"), "pg": ("sbuf", [128, W + 16], "int32"),
    "kq": ("sbuf", [128, W + 4 * LN], "bfloat16"), "vs": ("sbuf", [128, W], "bfloat16"),
    "sti": ("sbuf", [128, 16], "int32"), "yy": ("sbuf", [128, NV * L], "float32"),
    "pi": ("sbuf", [128, 12], "int32"), "pf": ("sbuf", [128, 20], "float32"),
    "io": ("sbuf", [128, 256], "float32"), "jj": ("sbuf", [128, LN], "float32"), "rm": ("sbuf", [128, LN], "float32"),
    "le": ("sbuf", [128, 8], "uint16"), "lz": ("sbuf", [128, 8], "uint16"),
    "nsel": ("sbuf", [128, 2, 160], "float16"), "f16": ("sbuf", [128, 128], "float16"), "hsel": ("sbuf", [128, 2, 144], "float16"),
    "zf": ("sbuf", [128, 512], "float32"),
    "sg": ("sbuf", [128, W], "float32"), "lp": ("sbuf", [128, 16], "uint16"), "yr": ("sbuf", [128, NV * L], "float32"), "ac": ("sbuf", [128, NV * L], "float32"),
    "idf": ("sbuf", [128, 256], "float32"), "idb": ("sbuf", [128, 256], "bfloat16"),
    "back": ("sbuf", [128, 256], "float32"), "fore": ("sbuf", [128, 128], "float32"), "roll": ("sbuf", [128, 4, 64], "float32"),
    "nid": ("sbuf", [128, 128], "float16"), "on": ("sbuf", [128, 128 * (NV - 1)], "float32"), "sel": ("sbuf", [128, 1024], "bfloat16"), "cc": ("sbuf", [128, 3 * LN], "bfloat16"),
    "kc": ("sbuf", [128, 2 * SL], "float16"), "zz": ("sbuf", [128, L], "bfloat16"),
    "ps_a": ("psum", [128, 512], "float32"),
}
for _k in range(NB):
    SCRATCH["ps_w%d" % _k] = ("psum", [128, 512], "float32")
if NB < 3:
    SCRATCH["ps_x"] = ("psum", [128, 30, 17], "float32")
for _k in range(NG):
    SCRATCH["vg%d" % _k] = ("sbuf", [128, 8 * LN], "float32")
for _k in range(ND):
    SCRATCH["pd%d" % _k] = ("sbuf", [128, 2 * PL, 8, 16] if OLD else [128, 16 * LN], "float32")
for _k in range(NR):
    SCRATCH["wr%d" % _k] = ("sbuf", [128, 8 * LN], "float32")
for _t in range(NV - 1):
    SCRATCH["la%d" % _t] = ("sbuf", [128, L], "float32")
for _x in range(2):
    SCRATCH["ps_m%d" % _x] = ("psum", [128, 512], "float32")
    SCRATCH["tf_%d" % _x] = ("sbuf", [128, 4, 32], "float16")
    SCRATCH["tl_%d" % _x] = ("sbuf", [128, 2 * PL, 17], "float16")
    SCRATCH["ps_s%d" % _x] = ("psum", [128, 30, 17], "float32")
    for _n, _c, _d in [("c0", 2 * PL, "uint16"), ("c1", 2 * PL, "uint16"), ("ln", LN, "uint16"), ("lv", NW * LN, "uint16"), ("so", 2 * PL, "uint16"),
                       ("nf", LN, "float16"), ("kr", 16 * LN, "bfloat16"), ("zq", 32 * LN, "bfloat16"),
                       ("ff", SL + 8, "float16"), ("rs", SL, "float32"), ("wp", NW * LN, "float32"), ("d1", SL, "float32"), ("un", SL, "float16"),
                       ("cs", SL, "float32"), ("ty", 4 * PL, "float32"), ("cex", LN, "float32"), ("nm0", LN, "float32"),
                       ("eq", LN, "float32"), ("cnt", LN, "float32"), ("val", LN, "int32"), ("vr", LN, "float32"),
                       ("xa", 3 * PL, "bfloat16"), ("xb", 3 * PL, "bfloat16")]:
        SCRATCH["%s_%d" % (_n, _x)] = ("sbuf", [128, _c], _d)
    SCRATCH["wa_%d" % _x] = ("sbuf", [128, NW * PL, 16], "bfloat16")
    SCRATCH["wb_%d" % _x] = ("sbuf", [128, NW * PL, 16], "bfloat16")
    SCRATCH["sb_%d" % _x] = ("sbuf", [128, NV * 3 * PL], "float32")
    SCRATCH["qs_%d" % _x] = ("sbuf", [128, (NV - 1) * LN], "bfloat16")
    SCRATCH["lc_%d" % _x] = ("sbuf", [128, (NV - 1) * 2 * PL], "float32")
    SCRATCH["lq_%d" % _x] = ("sbuf", [128, (NV - 1) * LN], "bfloat16")
SEMAPHORES = ["eV", "eS", "eP", "eG"] + ["d%d" % i for i in range(90)] + ["a%d" % i for i in range(15)]

A = AluOpType
F = ActivationFunctionType
ORDER = {}
MASKS = {}


def v(name, a, b, s=1):
    return (name, (a, b, s))


def vn(name, *ix):
    return (name,) + tuple(i if isinstance(i, int) else (tuple(i) + (1,))[:3] for i in ix)


def rows(x, a, b):
    return ("^", x, a, b)


def ind(win, off):
    return ("*", win, off)


def name(x):
    return x[1][0] if x[0] == "^" else x[0]


def bits(x):
    if x not in MASKS:
        y, a, b = x[1:] if x[0] == "^" else (x, 0, 128)
        m = np.zeros([2] + SCRATCH[y[0]][1][1:], bool)
        m[(slice(a // 64, (b + 63) // 64),) + tuple(i if isinstance(i, int) else slice(*i) for i in y[1:])] = True
        MASKS[x] = int.from_bytes(np.packbits(m.ravel(), bitorder="little").tobytes(), "little")
    return MASKS[x]


def cols(x):
    return 16 * cols(x[2]) if x[0] == "*" else bin(bits(x[1] if x[0] == "^" else x)).count("1") // 2


def meets(ops):
    hist, before, out = {}, {}, []
    for i, o in enumerate(ops):
        deps, reads = set(), set()
        acc = [(name(x), bits(x), False) for x in o["r"]] + [(name(x), bits(x), True) for x in o["w"]]
        for b, m, wr in acc:
            h = hist.setdefault(b, [])
            if b.startswith("ps_"):
                if h and h[0][0] != i and (ops[h[0][0]]["st"] != o["st"] or (o["st"] == "P" and not o.get("adds"))):
                    before[b] = [e[0] for e in h]
                    h[:] = []
                deps.update(before.get(b, []))
            for j, mj, wj in h:
                if (m & mj) and (wr or wj) and not (wr and o.get("adds") and ops[j].get("adds")):
                    deps.add(j)
                    if not wr:
                        reads.add(j)
        for b, m, wr in acc:
            h = hist[b]
            if wr and not o.get("adds"):
                h[:] = [e for e in h if (e[1] & ~m) or e[0] == i]
            h.append((i, m, wr))
        out.append({j: o["st"] != ops[j]["st"] or o["st"] == "?" or (o["st"] != "P" and (j in reads or not OPT["inorder"])) for j in deps if j != i})
    return out


def schedule(ops):
    deps = meets(ops)
    n = len(ops)
    for i, o in enumerate(ops):
        if o["e"] is None:
            deps[i][o["from"]] = False
    succ = [[] for _ in ops]
    for i in range(n):
        for j in deps[i]:
            succ[j].append(i)
    base = OPT["BASE"]
    cost = [{e: a[1] * base.get(o["k"], 1.0) for e, a in o["alt"].items()} for o in ops]
    late = [(o["lat"] - o["c"]) * base.get(o["k"], 1.0) for o in ops]
    gap = lambda j, i: OPT["sem"] if deps[i][j] and ops[i]["e"] is not None else 0
    fore = [[(k, late[i] + gap(i, k)) for k in succ[i]] for i in range(n)]
    aft = [[(j, late[j] + gap(j, i)) for j in deps[i]] for i in range(n)]
    shy, look = [OPT["shy"] if len(c) > 1 else 0.0 for c in cost], [0, 0, 0]

    def place(order, back):
        left = [len(succ[i] if back else deps[i]) for i in range(n)]
        due = list(late) if back else [0.0] * n
        end, eng, free, ready = [0.0] * n, [None] * n, {e: 0.0 for e in "VSPGY"}, {e: [] for e in "VSPGY"}

        def start(i, t):
            end[i] = t
            for k, d in (aft[i] if back else fore[i]):
                if due[k] < t + d:
                    due[k] = t + d
                left[k] -= 1
                if left[k] == 0:
                    arrive(k)

        def arrive(k):
            if ops[k]["e"] is None:
                start(k, due[k])
            for e in cost[k]:
                if e:
                    ready[e].append(k)
        for i in [i for i in range(n) if left[i] == 0]:
            arrive(i)
        while any(ready.values()):
            t, e = min((max(free[e], min([due[k] for k in r])), e) for e, r in ready.items() if r)
            rank = [(order[k] + (shy[k] if e == "V" else 0.0), k) for k in ready[e] if due[k] <= t + look[0]]
            u, i = min(rank)
            if due[i] > t:
                i = min([(a, k) for a, k in rank if due[k] <= t and (t + cost[k][e] <= due[i] + look[2] or a < u + look[1])] or [(u, i)])[1]
            for z in cost[i]:
                ready[z].remove(i)
            eng[i] = e
            free[e] = max(t, due[i]) + cost[i][e]
            start(i, free[e])
        return end, eng

    hard = [[(j, gap(j, i) > 0) for j in deps[i]] for i in range(n)]

    def replay(order, eng, scale):
        end, free, sem = [0.0] * n, {e: 0.0 for e in (None, "V", "S", "P", "G", "Y", "D")}, OPT["sem"] * scale.get("sem", 1.0)
        for i in order:
            o, e = ops[i], eng[i]
            t = free[e]
            for j, w in hard[i]:
                u = end[j] + sem if w else end[j]
                if u > t:
                    t = u
            k = scale.get(o["k"], 1.0)
            c = o["alt"][e][1]
            end[i] = t + (o["lat"] - o["c"] + c) * k
            if "b" in o:
                end[i] = free["D"] = max(end[i], free["D"] + o["b"] * k)
            if e:
                free[e] = t + c * k
        return max(end)

    def fit(order, back):
        left = [len(succ[i] if back else deps[i]) for i in range(n)]
        due = list(late) if back else [0.0] * n
        end, eng, busy = [0.0] * n, [None] * n, {e: [] for e in "VSPGY"}
        ready = sorted((order[i], i) for i in range(n) if left[i] == 0)
        while ready:
            i = ready.pop(0)[1]
            t = due[i]
            if ops[i]["e"] is not None:
                found = []
                for e, c in cost[i].items():
                    u, line = due[i], busy[e]
                    a, z = 0, len(line)
                    while a < z:
                        if line[(a + z) // 2][1] <= u:
                            a = (a + z) // 2 + 1
                        else:
                            z = (a + z) // 2
                    while a < len(line) and line[a][0] < u + c:
                        u = line[a][1]
                        a += 1
                    found.append((u + c + (shy[i] if e == "V" else 0.0), u + c, e, a))
                t, e, a = min(found)[1:]
                busy[e].insert(a, (t - cost[i][e], t))
                eng[i] = e
            end[i] = t
            more = False
            for k, d in (aft[i] if back else fore[i]):
                if due[k] < t + d:
                    due[k] = t + d
                left[k] -= 1
                if left[k] == 0:
                    ready.append((order[k], k))
                    more = True
            if more:
                ready.sort()
        return end, eng

    if OPT["sgs"]:
        place = fit
    tail = [0.0] * n
    for i in range(n - 1, -1, -1):
        tail[i] = max([tail[k] + d for k, d in fore[i]] + [late[i]]) + min(cost[i].values())
    best, top, seed = None, None, 1
    for r in range(OPT["rounds"] * len(OPT["WAIT"])):
        if r % OPT["rounds"] == 0:
            look[:] = OPT["WAIT"][r // OPT["rounds"]]
            end, best = place([-x for x in tail], False)[0], None
        u = place([-x for x in end], True)[0]
        shake = []
        for i in range(n):
            seed = (seed * 1103515245 + 12345) % 2 ** 31
            shake.append(OPT["shake"] * (1 + r % 4) * seed / 2 ** 31 + ops[i]["lag"])
        end, eng = place([shake[i] - u[i] for i in range(n)], False)
        order = sorted(range(n), key=lambda i: (-1.0 if ops[i].get("load") else end[i] - cost[i][eng[i]], i))
        ends = [replay(order, eng, s) / s["of"] for s in SCALES]
        if best is None or sum(ends) < best[0]:
            best = (sum(ends), order, eng, ends, end)
        if top is None or best[0] < top[0]:
            top = best
        if r % OPT["back"] == OPT["back"] - 1:
            end = best[4]
    order, eng = list(top[1]), list(top[2])
    wait = [[[(j, OPT["sem"] * s.get("sem", 1.0) if w else 0.0) for j, w in hard[i]] for i in range(n)] for s in SCALES]
    unit = [[s.get(o["k"], 1.0) for o in ops] for s in SCALES]
    slow, share = [o["lat"] - o["c"] for o in ops], [o.get("b", 0.0) for o in ops]
    price = [o["alt"][eng[i]][1] for i, o in enumerate(ops)]

    def run(s, p, old):
        end, fin, why = [list(a) for a in old]
        free, last, w, u = {None: 0.0, "D": 0.0}, {}, wait[s], unit[s]
        for i in order[p - 1::-1] if p else []:
            if eng[i] not in last:
                last[eng[i]], free[eng[i]] = i, fin[i]
            if share[i] and not free["D"]:
                free["D"] = end[i]
            if len(last) == 6 and free["D"]:
                break
        free[None] = 0.0
        for i in order[p:]:
            e = eng[i]
            t, y = free.get(e, 0.0), -1 - last.get(e, n)
            for j, d in w[i]:
                if end[j] + d > t:
                    t, y = end[j] + d, j
            c = t + price[i] * u[i]
            end[i] = c + slow[i] * u[i]
            if share[i]:
                end[i] = free["D"] = max(end[i], free["D"] + share[i] * u[i])
            if e:
                free[e], last[e] = c, i
            fin[i], why[i] = c, y
        return end, fin, why

    state = [run(s, 0, [[0.0] * n] * 3) for s in range(len(SCALES))]
    worth = lambda st: sum(max(a[0]) / s["of"] for a, s in zip(st, SCALES))
    now = worth(state)
    for r in range(OPT["mend"]):
        seed = (seed * 1103515245 + 12345) % 2 ** 31
        end, fin, why = state[(seed >> 8) % len(SCALES)]
        i, pairs = end.index(max(end)), []
        while i < n:
            if why[i] < 0 and -1 - why[i] < n:
                pairs.append((-1 - why[i], i))
            i = why[i] if why[i] >= 0 else -1 - why[i]
        seed = (seed * 1103515245 + 12345) % 2 ** 31
        j, i = pairs[(seed >> 8) % len(pairs)]
        a, z, kept, flip = order.index(j), order.index(i), list(order), None
        seed = (seed * 1103515245 + 12345) % 2 ** 31
        if (seed >> 8) % 3 == 0 and len(cost[i]) + len(cost[j]) > 2:
            flip = i if len(cost[i]) > 1 else j
            was = eng[flip]
            eng[flip] = "V" if was == "S" else "S"
            price[flip] = ops[flip]["alt"][eng[flip]][1]
        else:
            up, rest = [i], []
            for k in order[z - 1:a:-1]:
                (up if any(k in deps[m] for m in up) else rest).append(k)
            if ops[j].get("load") or any(j in deps[m] for m in up):
                continue
            order[a:z + 1] = up[::-1] + [j] + rest[::-1]
        new = [run(s, a, state[s]) for s in range(len(SCALES))]
        if worth(new) <= now + OPT["slack"] * (1 - r / OPT["mend"]):
            state, now = new, worth(new)
        elif flip is None:
            order[:] = kept
        else:
            eng[flip] = was
            price[flip] = ops[flip]["alt"][was][1]
    ORDER["end"] = (now / len(SCALES), [max(a[0]) / s["of"] for a, s in zip(state, SCALES)])
    return order, eng


def emit(g, T, ops):
    queue = {"V": g.vector, "S": g.scalar, "P": g.tensor, "G": g, "Y": g.sync}
    known, done, waits, needed = {e: {} for e in queue}, [], [], set()
    for i, deps in enumerate(meets(ops)):
        o, ws = ops[i], []
        if o["e"] is None:
            done.append({o["st"]: i})
            waits.append(ws)
            continue
        k = known[o["e"]]
        for j in sorted(deps, reverse=True):
            if k.get(ops[j]["st"], -1) >= j or not deps[j]:
                continue
            ws.append(j)
            needed.add(j)
            for s, n in done[j].items():
                if k.get(s, -1) < n:
                    k[s] = n
        d = dict(k)
        d[o["st"]] = i
        done.append(d)
        waits.append(ws)
    count, token, waited = {}, {}, {}
    for i, o in enumerate(ops):
        if o["e"] is not None:
            for j in waits[i]:
                queue[o["e"]].wait_ge(T.sem[token[j][0]], token[j][1])
                waited[token[j][0]] = max(waited.get(token[j][0], 0), token[j][1])
        if o["sem"] is not None:
            token[i] = (o["sem"], o["n"])
            count[o["sem"]] = o["n"]
            if o["e"] is not None:
                o["f"](queue[o["e"]])
        else:
            ins = o["f"](queue[o["e"]])
            if i in needed:
                s = "e" + o["e"]
                count[s] = count.get(s, 0) + 1
                token[i] = (s, count[s])
                ins.then_inc(T.sem[s], 1)
    for s, n in count.items():
        if waited.get(s, 0) < n:
            g.wait_ge(T.sem[s], n)


def rank_program(g, core, T, topo):
    rank = T.rank_of(core)
    if rank is None:
        return
    nxt = T.cores[(rank + 1) % len(T.cores)]
    rid, pid, _se = topo.addr(nxt)
    mask = topo.mask(core, nxt)
    n_out = len(topo.engines(core, nxt))
    n_in = len(topo.engines(T.cores[(rank - 1) % len(T.cores)], core))
    ops, nd, na, loaded, hop = [], [0], [0], [0.0], ["c"]
    cy, lag = OPT["cy"], [0.0]

    def ap(x):
        if x[0] == "*":
            return ap(x[1]).indirect(ap(x[2]))
        y, p = (x[1], slice(x[2], x[3])) if x[0] == "^" else (x, slice(None))
        return T[y[0]][(p,) + tuple(i if isinstance(i, int) else slice(*i[:2]) if i[2] == 1 else slice(*i) for i in y[1:])]

    def rec(e, f, outs, ins, c, sem=None, n=0, lat=None):
        r, w = [], []
        for x in ins:
            if isinstance(x, tuple):
                r.extend([x[1], x[2]] if x[0] == "*" else [x])
        for x in outs:
            if x[0] == "*":
                w.append(x[1])
                r.append(x[2])
            else:
                w.append(x)
        ops.append({"e": e, "f": f, "r": r, "w": w, "sem": sem, "n": n, "st": sem or e, "c": c, "lat": c if lat is None else lat, "from": len(ops) - 1,
                    "alt": {e: (f, c)}, "lag": lag[0],
                    "grp": "%s%s%s" % (e, hop[0], name((w or r)[0])[:4]),
                    "k": "pe" if e == "P" else ("dma" if n >= 16 else "rem") if sem else "sc" if outs[0][0] == "*" else "ga" if ins and ins[0][0] == "*" else ""})

    def cost(o, a, k=1.0, fixed=50):
        if o[0] == "*":
            return fixed + cols(o) * OPT["sc"] * cy
        if a[0] == "*":
            return fixed + cols(a) * OPT["ga"] * cy
        if k == 1.0 and fixed == 50 and "32" not in SCRATCH[name(o)][2] + SCRATCH[name(a)][2]:
            k = 0.5
        return OPT["vo"] + max(64, cols(a) * k) * cy

    def num(x):
        return ap(x) if isinstance(x, tuple) else x

    def cp(o, i):
        rec("V", lambda q: q.tensor_copy(ap(o), ap(i)), [o], [i], cost(o, i))

    def tt(o, a, b, op):
        rec("V", lambda q: q.tensor_tensor(ap(o), ap(a), ap(b), op), [o], [a, b], cost(o, a, 1.0 if "ps_" in (name(a)[:3], name(b)[:3]) else 2.0))

    def ts(o, a, s1, op0, s2=None, op1=None):
        if op1 is None:
            rec("V", lambda q: q.tensor_scalar(ap(o), ap(a), num(s1), None, op0), [o], [a, s1], cost(o, a))
        else:
            rec("V", lambda q: q.tensor_scalar(ap(o), ap(a), num(s1), num(s2), op0, op1), [o], [a, s1, s2], cost(o, a))

    def scan(o, a, b, op0, op1):
        rec("V", lambda q: q.tensor_tensor_scan(ap(o), ap(a), ap(b), 0.0, op0, op1), [o], [a, b], cost(o, a))

    def turn(o, i):
        rec("V", lambda q: q.transpose(ap(o), ap(i)), [o], [i], cost(o, i))

    def fill(o, c):
        rec("V", lambda q: q.memset(ap(o), c), [o], [], cost(o, o, 0.5 if SCRATCH[name(o)][2] == "bfloat16" else 1.0))

    def act(o, i, fn, bias=None, scale=None):
        c = cost(o, i, 1.0, OPT["so"])
        if bias is None:
            rec("S", lambda q: q.activation(ap(o), ap(i), fn), [o], [i], c)
        else:
            rec("S", lambda q: q.activation(ap(o), ap(i), fn, bias=num(bias), scale=1.0 if scale is None else scale), [o], [i, bias], c)

    def either():
        o = ops.pop()
        ops[-1]["alt"].update(o["alt"])
        ops[-1]["st"] = "?"

    def move_on(o, i, how="?", scale=None):
        if how != "S":
            cp(o, i) if scale is None else ts(o, i, scale, A.mult)
        if how != "V":
            act(o, i, F.Copy) if scale is None else act(o, i, F.Identity, 0.0, scale)
        if how == "?":
            either()

    def mms(calls, adds=False):
        c = [max(min(64, cols(x[1])), cols(x[2])) * OPT["pe"] * (4 if SCRATCH[x[1][0]][2] == "float32" else 1) for x in calls]
        if sum(c) > OPT["piece"] and len(calls) > 1:
            mms(calls[:len(calls) // 2], adds)
            mms(calls[len(calls) // 2:], adds)
            return

        def f(q):
            for o, lt, r, start, stop in calls:
                ins = q.matmul(ap(o), ap(lt), ap(r), start, stop)
            return ins
        rec("P", f, list(dict.fromkeys(x[0][1] if x[0][0] == "^" else x[0] for x in calls)), list(dict.fromkeys([x[1] for x in calls] + [x[2] for x in calls])), sum(c))
        ops[-1]["adds"] = adds

    def dsem():
        nd[0] += 1
        return "d%d" % (nd[0] - 1)

    def load(e, o, src, nbytes):
        s = dsem()
        loaded[0] += nbytes / OPT["db"]
        rec(e, lambda q: q.dma_start(ap(o), src).then_inc(T.sem[s], 16), [o], [], 100, s, 16, OPT["dl"] + loaded[0])
        ops[-1]["load"] = True

    def store(dst, i):
        s = dsem()
        rec("Y", lambda q: q.dma_start(dst, ap(i)).then_inc(T.sem[s], 16), [], [i], 100, s, 16, OPT["dl"] + 500)

    def move(land, i, nbytes):
        s, a = dsem(), "a%d" % na[0]
        na[0] += 1
        rec("G", lambda q: q.remote_dma(ap(land), ap(i), T.sem[a], T.sem[s], pid, rid, mask), [], [i], OPT["gi"], s, n_out, OPT["rl"] + nbytes / OPT["rb"] + (2000 if na[0] == 1 else 0))
        ops[-1]["arr"] = a
        rec(None, None, [land], [], 0, a, n_in)

    load("Y", v("sti", 0, 16), T.st[:], 8192)
    NP = 4
    pc = W // 2 // NP
    for k in range(NP):
        load("Y", v("bpk", k * pc, (k + 1) * pc), T.bp[:, k * pc:(k + 1) * pc], 512 * pc)
    load("Y", v("kq", 0, W), T.kt[:], 256 * W)
    load("Y", v("vs", 0, W), T.vt[:], 256 * W)

    def iota(o, pat, base, cm, flag):
        if flag:
            rec("G", lambda q: q.iota(ap(o), pat, base, cm, allow_small_or_imprecise_dtypes=True), [o], [], 130 + 2 * cy * cols(o))
        else:
            rec("G", lambda q: q.iota(ap(o), pat, base, cm), [o], [], 130 + 2 * cy * cols(o))
    iota(v("jj", 0, LN), [[0, PL], [1, 16]], 0, 0, True)
    ops[-1]["load"] = True
    iota(v("pi", 0, 1), [[0, 1]], 0, 1, False)
    iota(v("io", 0, SL), [[1, SL]], 0, 0, True)
    iota(v("cex_0", 0, 4 * PL), [[LN, 4], [0, PL]], 0, 0, True)

    def pick(o, pat, base, one=1.0, src=None):
        src = src or v("zf", 0, cols(o))
        rec("G", lambda q: q.affine_select(ap(o), ap(src), pat, A.not_equal, one, base, -1), [o], [src], 170 + 2 * cy * cols(o))
    iota(v("zf", 0, 512), [[0, 512]], 0, 0, True)
    pick(v("nid", 0, 128), [[1, 128]], 0, -1.0)
    for u in range(2):
        pick(vn("nsel", u, (0, 160)), [[32, 5], [-1000, 2], [1, 16]], 1000 + 16 * u)
    for o in ("f16", "fore"):
        pick(v(o, 0, 128), [[4, 4], [16, 8], [1, 4]], 0)
    pick(v("back", 0, 128), [[4, 8], [32, 4], [1, 4]], 0)
    s = dsem()
    rec("G", lambda q, s=s: q.dma_start(T.back[:, 128:256], T.back[:, 0:128]).then_inc(T.sem[s], 16), [v("back", 128, 256)], [v("back", 0, 128)], 3000, s, 16, 5000)
    pick(v("idf", 0, 256), [[0, 2], [1, 128]], 0)
    pick(vn("roll", (0, 4), (0, 64)), [[32, 4], [0, 2], [1, 32]], 0)
    for a in range(4):
        z = v("sel", 512 * (a % 2), 512 * (a % 2) + 512)
        pick(z, [[1, 4], [4, 8], [0, 16]], 32 * a, 1.0, z if a > 1 else None)
    fill(v("zq_0", 0, 32 * LN), 0.0)
    act(v("zq_1", 0, 32 * LN), v("zq_0", 0, 32 * LN), F.Copy)
    fill(v("pg", W, W + 16), 0)
    act(v("zz", 0, L), v("zf", 0, L), F.Copy)
    act(v("cc", 2 * LN, 3 * LN), v("zf", 0, LN), F.Copy)
    for k, (s, m) in enumerate([(0, 15), (4, 7), (0, 3)]):
        ts(v("pi", k + 1, k + 2), v("pi", 0, 1), s, A.logical_shift_right, m, A.bitwise_and)
    cp(v("pf", 0, 3), v("pi", 1, 4))
    cR, cX, cR3, cD, cM15, cN15, cZ, cY = [v("pf", k, k + 1) for k in range(8)]
    ts(cD, cR, float(W), A.add)
    ts(cM15, cR, 15.0, A.is_equal, -BIG, A.mult)
    ts(cN15, cR, 15.0, A.not_equal, -BIG, A.mult)
    ts(cZ, cX, 4.0, A.mult, cR3, A.add)
    ts(cY, cR, 32.0, A.mult, cZ, A.add)
    ts(v("lz", 0, 8), v("io", 0, 8), 512.0, A.mult, cY, A.add)
    if not OLD:
        iota(v("cex_1", 0, 2 * PL), [[LN, 2], [1, PL]], 0, 0, True)
        for u in range(2):
            pick(vn("hsel", u, (0, 144)), [[16, 9], [-1000, 2], [1, 8]], 1000 + 8 * u)
        ts(cZ, cR, 8.0, A.mult)
        ts(v("lp", 0, 16), v("cex_1", 0, 2 * PL), cZ, A.add)
    ts(v("kc", 0, SL), v("io", 0, SL), 0.0, A.mult, -1.6875, A.add)
    ts(v("kc", 0, SL, 17), v("io", 0, PL), 0.0, A.mult)
    ts(v("kc", SL, 2 * SL), v("io", 0, SL), 0.0, A.mult, -2048 / BIG, A.add)
    ts(v("kc", SL + 16, 2 * SL, 17), v("io", 0, PL), -16 / BIG, A.mult, -W / BIG, A.add)
    for x in range(2):
        ts(vn("tl_%d" % x, (0, 2 * PL), 16), v("cex_0", 2 * PL * x, 2 * PL * (x + 1)), cR, A.add, 1 / BIG, A.mult)
    cp(v("le", 0, 8), v("io", 0, 8))
    pick(v("idb", 0, 256), [[0, 2], [1, 128]], 0)
    for t in range(1, NV):
        act(v("on", 128 * t - 128, 128 * t), vn("roll", (0, 4), (32 - 4 * t, 64 - 4 * t)), F.Copy)
    ts(v("cc", 0, LN), v("jj", 0, LN), cR, A.is_ge, -BIG, A.mult)
    act(v("cc", LN, 2 * LN), v("jj", 0, LN), F.Identity, cN15, 0.0)
    act(v("rm", 0, LN), v("jj", 0, LN), F.Sigmoid, -100.0, 200.0)
    ops[-1].update(load=True, c=1420, lat=1420, alt={"S": (ops[-1]["f"], 1420)})
    QA, QB = [[v("kq", W + LN * (2 * x + k), W + LN * (2 * x + k + 1)) for x in range(2)] for k in range(2)]
    for x in range(2):
        act(v("d1_%d" % x, 0, SL), v("zf", 0, SL), F.Copy)
        act(v("d1_%d" % x, 0, SL, 17), v("zf", 0, PL), F.Identity, 1.0)
        ts(v("ff_%d" % x, SL, SL + 8), v("io", 0, 8), 0.0, A.mult)
    for k in range(NP):
        ts(v("pg", k * pc, (k + 1) * pc), v("bpk", k * pc, (k + 1) * pc), W - 1, A.bitwise_and)
        ts(v("pg", W // 2 + k * pc, W // 2 + (k + 1) * pc), v("bpk", k * pc, (k + 1) * pc), 12, A.logical_shift_right)

    KT, PG, VS = v("kq", 0, W), v("pg", 0, W + 16), v("vs", 0, W)
    IDF, IDB, BACK, FORE, PA = v("idf", 0, 128), v("idb", 0, 128), v("back", 0, 128), v("fore", 0, 128), v("ps_a", 0, L)
    bank, turns, SG, LV = [0], [0, 0], v("sg", 0, W), SL + LN
    for a in range(0, 0 if OLD else W, OPT["SG"]):
        act(v("sg", a, a + OPT["SG"]), v("vs", a, a + OPT["SG"]), F.Sigmoid)

    def split(src, a, b, scalar):
        for p, z in ((0, a), (64, b)):
            move_on(rows(z, p, p + 64), rows(src, p, p + 64), scalar)
        for p, z in ((0, a), (64, b)):
            tt(rows(z, 64 - p, 128 - p), rows(src, p, p + 64), rows(z, p, p + 64), A.subtract)

    def chain(h, x):
        t, first, last = h // 2, h % 2 == 0, h == 2 * NV - 1
        cutv, p0 = t < NV - 1, PL * (1 - x)
        hop[0] = "%d%d" % (h, x)
        b = lambda name, a, e, s=1: v("%s_%d" % (name, x), a, e, s)
        ps = lambda a, e, c0=0, c1=17: vn("ps_s%d" % x, (a, e), (c0, c1))
        pm = lambda a, e, s=1: v("ps_m%d" % x, a, e, s)
        came, camp, tP = [b("ty", PL * k, PL * k + PL) for k in range(3)]
        cl, zq, k = b("c0", 0, PL), ind(b("zq", 0, 32 * LN), v("lz", 0, PL)), h % NW
        ln = lambda a, e: b("ln", a, e)
        if h == 0:
            cp(cl, v("sti", p0, p0 + PL))
            ts(came, v("sti", p0, p0 + PL), -1 / BIG, A.mult, TOP / BIG, A.add)
            mms([(ps(16, 17, 0, PL), FORE, came, True, True)])
            cp(camp, ps(16, 17, 0, PL))
        elif first:
            s0 = 2 * PL * (t - 1)
            mms([(ps(16, 17, 0, PL), v("back", 128 - 16 * t, 256 - 16 * t), b("lc", s0, s0 + PL), True, True),
                 (ps(17, 19, 0, PL), v("on", 128 * t - 128, 128 * t), b("lc", s0, s0 + 2 * PL), True, True)])
            ts(cl, ps(16, 17, 0, PL), 0.0, A.add)
            move_on(b("d1", 0, SL, 17), ps(18, 19, 0, PL), OPT["E"][5])
            if cutv:
                ts(b("ty", 0, 2 * PL), ps(16, 18, 0, PL), -1 / BIG, A.mult, TOP / BIG, A.add)
        cp(ln(0, LN), ind(PG, cl))
        if h == 0:
            move_on(QA[x], ind(KT, cl), OPT["E"][2])
        elif first:
            mms([(ps(0, PL, 0, 16), v("idb", 128 - 16 * t, 256 - 16 * t), b("lq", LN * (t - 1), LN * t), True, True)])
            move_on(QA[x], ps(0, PL, 0, 16), OPT["E"][4])
        if first:
            cp(zq, QA[x])
        NID, NAMES, r0 = v("nid", 0, 128), pm(0, SL), PL * (h % 2)
        tl = lambda a, e: vn("tl_%d" % x, (r0, r0 + PL), (a, e))
        ts(b("nf", 0, LN), ln(0, LN), -2048.0, A.add, 1 / BIG, A.mult)
        turn(vn("tf_%d" % x, (0, 4), (0, 32)), b("nf", 0, LN))
        mms([(pm(SL + 64 * u, SL + 64 * u + 64), vn("nsel", u, (16 - 16 * o, 144 - 16 * o)), vn("tf_%d" % x, (0, 4), (16 * o, 16 * o + 16)), not o, bool(o))
             for u in range(2) for o in range(2)])
        for u in range(2):
            cp(vn("tl_%d" % x, (r0 + u, r0 + PL, 2), (0, 16)), pm(SL + 64 * u, SL + 64 * u + 64))
        if OLD:
            for nh in range(2):
                ts(b("lv", LN * k + 64 * nh, LN * k + 64 * nh + 64), tl(8 * nh, 8 * nh + 8), BIG, A.mult, 2048.0, A.add)
        else:
            mms([(pm(LV + 64 * nh + p2, LV + 64 * nh + 64, 4), vn("hsel", nh, (8 - 8 * o, 136 - 8 * o)), b("nf", 32 * p2 + 16 * o, 32 * p2 + 16 * o + 16), not o, bool(o))
                 for nh in range(2) for p2 in range(4) for o in range(2)])
            ts(b("lv", LN * k, LN * k + LN), pm(LV, LV + LN), BIG, A.mult, 2048.0, A.add)
        mms([(NAMES, NID, v("kc", SL, 2 * SL), True, False), (NAMES, v("f16", 0, 128), tl(0, 17), False, False)])
        mms([(ps(0, PL), NID, v("kc", 0, SL), True, False)])
        l0 = 0
        nv = OPT["CV"][h]
        for e, n in [("V", nv), ("S", 64 - nv // 4 * 2), ("S", 64 - nv + nv // 4 * 2)] if nv else OPT["CH"]:
            move_on(b("kr", 16 * l0, 16 * (l0 + n)), ind(KT, ln(l0, l0 + n)), e, -1 / 1024.0)
            mms([(rows(vn("ps_s%d" % x, l // 16, (1, 17)), 32 * (l % 16 // 4), 32 * (l % 16 // 4) + 32), b("zq", 32 * l, 32 * l + 32),
                  b("kr", 16 * l, 16 * l + 16), False, l >= LN - 16 and l % 4 == 3) for l in range(l0, l0 + n)])
            l0 += n
        if first and cutv:
            move_on(b("cex", 0, LN), ind(came, v("le", 0, 8)), OPT["E"][3])
            ts(b("nm0", 0, LN), ln(0, LN), cM15, A.add)
        pw = (lambda a, e: vn("ps_x", (PL * x, PL * x + PL), (a, e))) if NB < 3 else (lambda a, e: ps(PL, 2 * PL, a, e))
        RS, WW, W1 = b("rs", 0, SL), pw(0, 17), pw(0, 16)
        ts(b("ff", 0, SL), ps(0, PL), 1.0, A.min, 1 / 16.0, A.max)
        scan(RS, b("ff", 0, SL), b("d1", 0, SL), A.mult, A.max)
        ts(b("un", 0, SL), RS, 1 / 16.0, A.is_lt)
        R16, U16, C15 = b("rs", 16, SL, 17), b("un", 16, SL, 17), b("cs", 15, SL, 17)
        mms([(NAMES, NID, b("un", 0, SL), False, True)])
        mms([(WW, NID, b("ff", 1, SL + 1), True, False), (WW, NID, b("un", 0, SL), False, True)])
        scan(b("cs", 0, SL), b("un", 0, SL), NAMES, A.mult, A.max)
        s0, m0, cq, n = 3 * PL * t, LV + LN, "c%d" % (h % 2), PL if last else 2 * PL
        mms([(pm(m0, m0 + PL), BACK, C15, True, True)] + ([] if last else [(pm(m0 + PL, m0 + 2 * PL), BACK, b("cs", 16, SL, 17), True, True)]))
        if not first and cutv:
            ts(b("sb", s0 + PL, s0 + 2 * PL), C15, BIG, A.mult)
        tt(b("d1", 0, SL, 17) if first else b("sb", s0 + 2 * PL, s0 + 3 * PL), U16, R16, A.max)
        if not first and cutv:
            move(b("lc", 2 * PL * t, 2 * PL * (t + 1)), b("sb", s0 + PL, s0 + 3 * PL), 128 * 64)
        ts(b(cq, 0, n), pm(m0, m0 + n), BIG, A.mult)
        if not last:
            move_on(QB[x] if first else b("qs", LN * t, LN * t + LN), ind(v("kq", 0, (QA if first else QB)[x][1][1]), b(cq, PL, 2 * PL)), OPT["E"][2])
        if first:
            cp(zq, QB[x])
            if cutv:
                tt(tP, camp, U16, A.subtract)
        elif cutv:
            move(b("lq", LN * t, LN * t + LN), b("qs", LN * t, LN * t + LN), 256 * LN)
        if OPT["E"][6] != "S":
            ts(W1, W1, 1.0, A.add, 0.0, A.max)
        if OPT["E"][6] != "V":
            act(W1, W1, F.Relu, 1.0)
        if OPT["E"][6] == "?":
            either()
        tt(WW, RS, WW, A.mult)
        nd2 = int(OPT["WR"][2 * h + x])
        for nh in range(nd2):
            move_on(b("wp", LN * k + 64 * nh, LN * k + 64 * nh + 64), pw(8 * nh, 8 * nh + 8), OPT["E"][8])
        if nd2 < 2:
            split(pw(8 * nd2, 16), vn("wa_%d" % x, (PL * k, PL * k + PL), (8 * nd2, 16)), vn("wb_%d" % x, (PL * k, PL * k + PL), (8 * nd2, 16)), OPT["E"][0])
        if first:
            return
        a = 0 if cutv else 2 * PL
        if cutv:
            tt(b("sb", s0, s0 + PL), tP, U16, A.mult)
        split(b("sb", s0 + a, s0 + 3 * PL), b("xa", a, 3 * PL), b("xb", a, 3 * PL), OPT["E"][1])
        if cutv:
            mms([(pm(m0 + 2 * PL, m0 + 3 * PL), BACK, b("sb", s0, s0 + PL), True, True), (pm(0, 3 * LN), IDB, v("cc", 0, 3 * LN), True, False)])
        calls = []
        for jj in range(16):
            calls.append((pm(16 * a + jj, 3 * LN, 16), v("sel", 128 * (jj % 8), 128 * (jj % 8) + 128), b("xb" if jj // 8 else "xa", a, 3 * PL), not cutv, jj == 15 or not cutv))
        mms(calls)
        if cutv:
            tt(b("eq", 0, LN), b("cex", 0, LN), pm(0, LN), A.is_equal)
            ts(b("eq", 15, LN, 16), pm(m0 + 2 * PL, m0 + 3 * PL), -1.0, A.mult, TOP / BIG, A.add)
            tt(b("val", 0, LN), b("nm0", 0, LN), pm(LN, 2 * LN), A.max)
            scan(b("cnt", 0, LN), v("rm", 0, LN), b("eq", 0, LN), A.mult, A.max)
            ts(b("so", 0, 2 * PL, 2), b("cnt", 15, LN, 16), BIG, A.mult, cD, A.min)
        act(b("vr", 0, LN), ind(VS, b("c1", 0, PL)), F.Sigmoid)
        tt(v("yr", L * t + 16 * p0, L * t + 16 * p0 + LN), b("vr", 0, LN), pm(2 * LN, 3 * LN), A.mult)

    def shortcuts(x):
        for pl in range(PL - 1, -1, -1):
            cp(ind(PG, v("so_%d" % x, 2 * pl, 2 * pl + 1)), v("val_%d" % x, 16 * pl, 16 * pl + 16))

    def fold(o, i):
        s = dsem()
        rec("G", lambda q: q.dma_start(ap(o), ap(i), accum_op=A.add).then_inc(T.sem[s], 16), [o], [o, i, v("back", 128, 256)], OPT["gi"], s, 16, OPT["fl"])
        if OPT["ab"]:
            ops[-1]["b"] = OPT["ab"]

    def spread(wr, wp, c0):
        s, z = dsem(), dsem()

        def first(q):
            for a in range(4):
                q.dma_start(T[wr][0:128:16, 256 * a:256 * a + 256], T[wp][32 * a:32 * a + 32, c0:c0 + 64]).then_inc(T.sem[s], 16)

        def others(q):
            for i in range(1, 16):
                q.dma_start(T[wr][i:128:16, :], T[wr][0:128:16, :]).then_inc(T.sem[z], 16)
        rec("Y", first, [v(wr, 0, 1024)], [v(wp, c0, c0 + 64)], 4 * OPT["yi"], s, 64, OPT["yl"] + 4 * OPT["yi"])
        rec("Y", others, [v(wr, 0, 1024)], [v(wr, 0, 1024)], 15 * OPT["yi"], z, 240, OPT["yl"] + 15 * OPT["yi"] + 500)

    def values(h, x):
        u0, k, t = 2 * h + x, h % NW, h // 2
        hop[0] = "%d%d" % (h, x)
        pd, how, nd2, vg = "pd%d" % (u0 % ND), OPT["SUM"][u0], int(OPT["WR"][u0]), {}
        acc = v("ps_a", LN * (1 - x), LN * (2 - x))
        lv = lambda a, e: v("lv_%d" % x, LN * k + a // 16, LN * k + e // 16)
        for nh in range(nd2, 2):
            vg[nh] = "vg%d" % (turns[0] % NG)
            turns[0] += 1
            act(v(vg[nh], 0, 1024), ind(VS, lv(1024 * nh, 1024 * nh + 1024)), F.Sigmoid)
        for nh in range(nd2):
            wr = "wr%d" % (turns[1] % NR)
            turns[1] += 1
            spread(wr, "wp_%d" % x, LN * k + 64 * nh)
            for a in range(0, 1024, OPT["VS"]):
                tt(v(pd, 1024 * nh + a, 1024 * nh + a + OPT["VS"]), ind(SG, lv(1024 * nh + a, 1024 * nh + a + OPT["VS"])), v(wr, a, a + OPT["VS"]), A.mult)
        if h % 2 == 0 and x == 0:
            mms([(PA, IDB, v("zz", 0, L), True, False)])
        closes = h % 2 and x and not (t and how in "dbg")
        if closes and t:
            mms([(PA, v("idf", 128 - 16 * t, 256 - 16 * t), v("la%d" % (t - 1), 0, L), False, False)], True)
        kept = {}
        for nh, j0 in ([(0, 0), (1, 0), (0, 1), (1, 1)] if how in "vu" else [(0, 0), (0, 1), (1, 0), (1, 1)]):
            o0 = 1024 * nh + 512 * j0
            if OLD:
                bk = "ps_w%d" % (bank[0] % NB)
                bank[0] += 1
                mms([(v(bk, u, 512, 8), v("sel", 128 * ((j0 + 2 * u) % 8), 128 * ((j0 + 2 * u) % 8) + 128),
                      vn("w%s_%d" % ("ab"[u // 4], x), (PL * k, PL * k + PL), (8 * nh, 8 * nh + 8)), True, True) for u in range(8)])
                wide, out = v(bk, 0, 512), vn(pd, (PL * nh, PL * nh + PL), (0, 8), (j0, 16, 2))
                if how in "vug" and nh == 0:
                    tt(wide, v(vg[nh], j0, 1024, 2), wide, A.mult)
                    if how != "v":
                        tt(out if how == "g" else wide, vn("pd%d" % ((u0 - 2) % ND), (0, PL), (0, 8), (j0, 16, 2)), wide, A.add)
                    kept[j0] = wide
                    continue
                tt(out, v(vg[nh], j0, 1024, 2), wide, A.mult)
                if how in "vu":
                    tt(out, out, kept[j0], A.add)
                if how in "vpu":
                    end = bool(closes and nh and j0)
                    mms([(v("ps_a", LN * (1 - x) + j0, LN * (2 - x), 2), IDF, vn(pd, (PL * nh, PL * nh + PL), n, (j0, 16, 2)), False, end and n == 7) for n in range(8)], not end)
                continue
            if nh >= nd2:
                bk = "ps_w%d" % (bank[0] % NB)
                bank[0] += 1
                mms([(v(bk, 64 * u, 64 * u + 64), v("sel", 128 * u, 128 * u + 128),
                      vn("w%s_%d" % ("ab"[j0], x), (PL * k, PL * k + PL), (8 * nh, 8 * nh + 8)), True, True) for u in range(8)])
                wide, out = v(bk, 0, 512), v(pd, o0, o0 + 512)
                if how in "vug" and nh == 0:
                    tt(wide, v(vg[nh], 512 * j0, 512 * j0 + 512), wide, A.mult)
                    if how != "v":
                        tt(out if how == "g" else wide, v("pd%d" % ((u0 - 2) % ND), 512 * j0, 512 * j0 + 512), wide, A.add)
                    kept[j0] = wide
                    continue
                tt(out, v(vg[nh], 512 * j0, 512 * j0 + 512), wide, A.mult)
                if how in "vu":
                    tt(out, out, kept[j0], A.add)
            if how in "vpu":
                end = bool(closes and nh and j0)
                a0 = LN * (1 - x) + 64 * j0
                mms([(v("ps_a", a0, a0 + 64), IDF, v(pd, o0 + n, o0 + 512, 8), False, end and n == 7) for n in range(8)], not end)
        half = lambda z, nh: vn(z, (PL * nh, PL * nh + PL), (0, 8), (0, 16)) if OLD else v(z, 1024 * nh, 1024 * nh + 1024)
        if how in "dag":
            fold(half(pd, 0), half(pd, 1))
        if how == "b":
            mine, pd = pd, "pd%d" % ((u0 - 2) % ND)
            for nh in range(2):
                fold(half(pd, 0), half(mine, nh))
        if how in "dbg":
            for n in range(0, 8, 2):
                mms([(acc, IDF, vn(pd, (0, PL), m, (0, 16)) if OLD else v(pd, m, 1024, 8), False, bool(closes and m == 7)) for m in (n, n + 1)], not (closes and n == 6))
            if h % 2 and x and t:
                mms([(PA, v("idf", 128 - 16 * t, 256 - 16 * t), v("la%d" % (t - 1), 0, L), False, True)])

    def report(t):
        y, ac = v("yy", L * t, L * t + L), v("ac", L * t, L * t + L)
        if t < NV - 1 or not OLD:
            move_on(ac, PA, OPT["E"][7] if t < NV - 1 else "V")
        if t < NV - 1:
            move(v("la%d" % t, 0, L), ac, 512 * L)
        tt(y, v("yr", L * t, L * t + L), PA, A.add) if OLD else tt(y, ind(ac, v("lp", 0, 16)), v("yr", L * t, L * t + L), A.add)
        store(T.ya[:, L * t:L * t + L], y)

    for h in range(2 * NV):
        for x in range(2):
            chain(h, x)
        if h % 2 and h < 2 * NV - 1:
            for x in range(2):
                shortcuts(x)
        lag[0] = OPT["LAG"][h]
        for x in range(2):
            values(h, x)
        if h % 2:
            report(h // 2)
        lag[0] = 0.0
    key = (n_out, n_in)
    if key not in ORDER:
        ORDER[key] = schedule(ops)
    for o, e in zip(ops, ORDER[key][1]):
        if len(o["alt"]) > 1:
            o.update(e=e, st=e, f=o["alt"][e][0], c=o["alt"][e][1], lat=o["alt"][e][1], grp=e + o["grp"][1:])
    emit(g, T, [ops[i] for i in ORDER[key][0]])
